import numpy as np
import ml_dtypes


def mxq(x, axis, fmt="e4m3"):
    dtype, down = {"e4m3": (ml_dtypes.float8_e4m3fn, 7), "e5m2": (ml_dtypes.float8_e5m2, 14)}[fmt]
    v = np.moveaxis(np.asarray(x, np.float32).astype(ml_dtypes.bfloat16).astype(np.float64), axis, -1)
    blocks = v.reshape(v.shape[:-1] + (-1, 32))
    amax = np.abs(blocks).max(-1, keepdims=True)
    byte = np.maximum(np.where(amax > 0, np.frexp(amax)[1] - 1 + 127, 0) - down, 1)
    scale = np.exp2(byte - 127.0)
    codes = (blocks / scale).astype(np.float32).astype(dtype).astype(np.float64)
    return np.moveaxis((codes * scale).reshape(v.shape), -1, axis)


WIDE = False


def mx_kscale(k):
    if not WIDE:
        return np.ones(k)
    levels = np.array([10, -10, 5, -5, 0])
    if k % 512:
        return np.exp2(np.random.permutation(np.resize(levels, k // 32))).repeat(32)
    a = np.empty((k // 512, 16))
    for p in range(k // 512):
        a[p, :8] = np.random.permutation(np.resize(levels, 8))
        for g in range(8):
            far = levels[np.abs(levels - a[p, g]) >= 10]
            a[p, g + 8] = far[np.random.randint(len(far))]
    return np.exp2(a.ravel()).repeat(32)


def f64(x):
    return np.asarray(x).astype(np.float64)


def striped(idx):
    return np.tile(idx.reshape(-1, 16).T, (8, 1)).astype(np.uint16)


def unstriped(offs):
    return offs[:16].T.reshape(-1).astype(np.int64)


E2M1 = np.array([0.0, 0.5, 1.0, 1.5, 2.0, 3.0, 4.0, 6.0, -0.0, -0.5, -1.0, -1.5, -2.0, -3.0, -4.0, -6.0])


def pack_weight(w, fmt):
    k, n = w.shape
    w = f64(np.asarray(w, np.float32).astype(ml_dtypes.bfloat16)).reshape(k // 32, 32, n)
    amax = np.abs(w).max(1)
    if fmt == "e4m3":
        byte = np.frexp(amax)[1] - 1 + 127 - 7
    else:
        mant, ex = np.frexp(amax / 6.0)
        byte = np.where(mant > 0.5, ex, ex - 1) + 127
    byte = np.clip(np.where(amax > 0, byte, 1), 1, 254)
    scaled = (w * np.exp2(127.0 - byte)[:, None, :]).reshape(k, n).astype(np.float32)
    by_word = np.ascontiguousarray(scaled.reshape(k // 512, 128, 4, n).transpose(0, 1, 3, 2))
    if fmt == "e4m3":
        words = by_word.astype(ml_dtypes.float8_e4m3fn).view(np.uint8)
    else:
        c = by_word.astype(ml_dtypes.float4_e2m1fn).view(np.uint8) & 0xF
        words = (c[..., 0::2] | (c[..., 1::2] << 4)).reshape(k // 512, 128, 2 * n)
    return np.ascontiguousarray(words), np.ascontiguousarray(byte.astype(np.uint8).reshape(k // 512, 16, n))


def unpack_weight(words, scales, fmt):
    g, _, n = scales.shape
    words = np.ascontiguousarray(words).reshape(g, 128, n, -1)
    if fmt == "e4m3":
        vals = words.view(ml_dtypes.float8_e4m3fn).astype(np.float64)
    else:
        nib = np.empty((g, 128, n, 4), np.uint8)
        nib[..., 0::2] = words & 0xF
        nib[..., 1::2] = words >> 4
        vals = E2M1[nib]
    vals = vals * np.repeat(np.exp2(scales.astype(np.float64) - 127.0), 8, axis=1)[..., None]
    return vals.transpose(0, 1, 3, 2).reshape(g * 512, n)


def gelu(v):
    return 0.5 * v * (1.0 + np.tanh(np.sqrt(2.0 / np.pi) * (v + 0.044715 * v**3)))


K, T, S, T2, S2, N = 1024, 4096, 1024, 2048, 1024, 512

def setup_inputs():
    n = np.random.standard_normal
    s = mx_kscale(K)[:, None]
    u = mx_kscale(S)[:, None]
    tab_words, tab_scales = pack_weight(n((K, T)) * s, "e4m3")
    tab2_words, tab2_scales = pack_weight(n((K, T2)) / np.sqrt(K) / s, "e4m3")
    attr_words, attr_scales = pack_weight(2.0 * n((S, N)) / np.sqrt(S) / u, "e2m1")
    rec = np.exp(-np.arange(S) / S + 0.2 * n(S)) * u[:, 0]
    return {
        "tab_words": tab_words, "tab_scales": tab_scales,
        "tab2_words": tab2_words, "tab2_scales": tab2_scales,
        "offs": striped(np.random.permutation(T)[:S]),
        "offs2": striped(np.random.permutation(T2)[:S2]),
        "rec": rec.astype(np.float32),
        "attr_words": attr_words, "attr_scales": attr_scales,
        "wg": (2.0 * n((S, N)) / np.sqrt(S) / u).astype(np.float32),
        "bg": (0.5 * n(N)).astype(np.float32),
    }

def reference(tab_words, tab_scales, tab2_words, tab2_scales, offs, offs2, rec, attr_words, attr_scales, wg, bg):
    v = unpack_weight(tab_words, tab_scales, "e4m3")[:, unstriped(offs)]
    v2 = unpack_weight(tab2_words, tab2_scales, "e4m3")[:, unstriped(offs2)]
    A = v.T @ v2
    z = np.maximum(A, 0.0) * f64(rec)[:, None]
    zq = mxq(z, 0, "e4m3")
    y = unpack_weight(attr_words, attr_scales, "e2m1").T @ zq
    g = (mxq(f64(wg), 0, "e4m3").T @ zq) + f64(bg)[:, None]
    return y * (1.0 / (1.0 + np.exp(-g)))

@@ -1,0 +1,239 @@
+from contextlib import ExitStack
+
+import concourse.mybir as mybir
+
+K, T, S, T2, S2, N = 1024, 4096, 1024, 2048, 1024, 512
+FLOPS = 2 * K * S * S2 + 2 * 2 * S * N * S2
+
+F32 = mybir.dt.float32
+BF16 = mybir.dt.bfloat16
+I32 = mybir.dt.int32
+U32 = mybir.dt.uint32
+U16 = mybir.dt.uint16
+U8 = mybir.dt.uint8
+FP8X4 = mybir.dt.float8_e4m3fn_x4
+FP4X4 = mybir.dt.float4_e2m1fn_x4
+ALU = mybir.AluOpType
+ACT = mybir.ActivationFunctionType
+
+P = 128
+PACK = 4
+KP = 512
+BANK = 512
+HALF = 512
+
+
+def tile_list_slate_candidate_profiles_kernel(
+    tc, tab_words, tab_scales, tab2_words, tab2_scales, offs, offs2, rec, attr_words, attr_scales, wg, bg, out
+):
+    nc = tc.nc
+    with ExitStack() as ctx:
+        keep = ctx.enter_context(tc.tile_pool(name="keep", bufs=1))
+        ring = ctx.enter_context(tc.tile_pool(name="ring", bufs=3))
+        psum = ctx.enter_context(tc.psum_pool(name="psum", bufs=1))
+
+        def held(shape, dtype, name):
+            return keep.tile(shape, dtype, name=name, align_bytes=64)
+
+        def bank(b, label):
+            return psum.tile([P, BANK], F32, name=label, tag="bank%d" % b)
+
+        idx = keep.tile([P, S // 16], U16, name="idx")
+        idx2 = keep.tile([P, S2 // 16], U16, name="idx2")
+        tw = [held([P, T], I32, "tw%d" % a) for a in range(2)]
+        t2w = [held([P, T2], I32, "t2w%d" % a) for a in range(2)]
+        ts = held([P, T // 4], I32, "ts")
+        t2s = held([P, T2 // 4], I32, "t2s")
+        asc = held([P, 2, N // 4], I32, "asc")
+        aw = held([P, 2, 2 * N // 4], I32, "aw")
+        wraw = [held([P, PACK, N], F32, "wraw%d" % a) for a in range(2)]
+        rec_t = held([P, 2, PACK], F32, "rec_t")
+        bg_t = held([P, N // P], F32, "bg_t")
+        warm = held([P, 1], F32, "warm")
+        warm2 = held([P, 1], F32, "warm2")
+
+        nc.vector.memset(t2s[:], 0)
+        nc.vector.memset(ts[:], 0)
+        nc.vector.memset(asc[:], 0)
+        nc.vector.memset(warm[:], 0.0)
+        nc.scalar.activation(warm2[:], warm[:], ACT.Sigmoid)
+
+        def words_of(tab, a):
+            return tab[a].rearrange("p n t -> p (n t)").bitcast(I32)
+
+        nc.sync.dma_start(idx2[:], offs2)
+        nc.sync.dma_start(idx[:], offs)
+        nc.sync.dma_start(t2w[0][:], words_of(tab2_words, 0))
+        for q in range(4):
+            nc.sync.dma_start(t2s[32 * q : 32 * q + 8, :], tab2_scales[:, 4 * q : 4 * q + 4, :].bitcast(I32))
+        nc.sync.dma_start(tw[0][:], words_of(tab_words, 0))
+        for q in range(4):
+            nc.sync.dma_start(ts[32 * q : 32 * q + 8, :], tab_scales[:, 4 * q : 4 * q + 4, :].bitcast(I32))
+        nc.sync.dma_start(tw[1][:], words_of(tab_words, 1))
+        nc.sync.dma_start(t2w[1][:], words_of(tab2_words, 1))
+        nc.sync.dma_start(rec_t[:], rec.rearrange("(a p t) -> p a t", a=2, t=PACK))
+        with nc.allow_non_contiguous_dma(reason="one bias value to a partition"):
+            nc.sync.dma_start(bg_t[:], bg.rearrange("(c p) -> p c", p=P))
+        for q in range(4):
+            nc.sync.dma_start(
+                asc[32 * q : 32 * q + 4, :, :],
+                attr_scales[:, 4 * q : 4 * q + 4, :].bitcast(I32).rearrange("a s n -> s a n"),
+            )
+        for a in range(2):
+            nc.sync.dma_start(wraw[a][:], wg[KP * a : KP * (a + 1), :].rearrange("(p t) n -> p t n", t=PACK))
+        nc.sync.dma_start(aw[:], attr_words.bitcast(I32).rearrange("a p n -> p a n"))
+
+        vw = [held([P, S], U32, "vw%d" % a) for a in range(2)]
+        vs_list = held([P, S], U8, "vs_list")
+        vs = held([P, S], U8, "vs")
+        v2w = [[held([P, HALF], U32, "v2w%d_%d" % (a, h)) for h in range(2)] for a in range(2)]
+        v2s = held([P, S2], U8, "v2s")
+
+        def gather_v(a):
+            for g in range(2):
+                nc.vector.tensor_copy(
+                    vw[a][:, KP * g : KP * (g + 1)].rearrange("p (t m) -> p m t", t=PACK),
+                    tw[a][:].bitcast(U32).indirect(idx[:, 32 * g : 32 * (g + 1)]),
+                )
+
+        def gather_v2(a, h):
+            nc.vector.tensor_copy(v2w[a][h][:], t2w[a][:].bitcast(U32).indirect(idx2[:, 32 * h : 32 * (h + 1)]))
+
+        gather_v2(0, 0)
+        nc.vector.tensor_copy(v2s[:], t2s[:].bitcast(U8).indirect(idx2[:]))
+        nc.vector.tensor_copy(vs_list[:], ts[:].bitcast(U8).indirect(idx[:]))
+        gather_v(0)
+        nc.vector.tensor_copy(
+            vs[:].rearrange("p (g t m) -> p g t m", g=2, t=PACK),
+            vs_list[:].rearrange("p (g m t) -> p g t m", g=2, t=PACK),
+        )
+        sgn = held([P, 2, PACK], F32, "sgn")
+        mag = held([P, 2, PACK], F32, "mag")
+        nc.scalar.activation(sgn[:], rec_t[:], ACT.Sign)
+        nc.scalar.activation(mag[:], rec_t[:], ACT.Abs)
+
+        def score(acc, g, t, a, h, c0, width):
+            m0 = KP * g + P * t
+            nc.tensor.matmul_mx(
+                out=acc,
+                lhsT=vw[a][:, m0 : m0 + P].bitcast(FP8X4),
+                lhsT_scale=vs[4 * a : P, m0 : m0 + P],
+                rhs=v2w[a][h][:, c0 : c0 + width].bitcast(FP8X4),
+                rhs_scale=v2s[4 * a : P, HALF * h + c0 : HALF * h + c0 + width],
+                start=(a == 0),
+                stop=(a == 1),
+            )
+
+        first = [bank(b, "first%d" % b) for b in range(8)]
+        for b in range(8):
+            score(first[b][:], b // 4, b % 4, 0, 0, 0, HALF)
+        gather_v(1)
+        gather_v2(1, 0)
+        for b in range(8):
+            score(first[b][:], b // 4, b % 4, 1, 0, 0, HALF)
+        gather_v2(0, 1)
+        gather_v2(1, 1)
+
+        planes = [held([P, PACK, HALF], BF16, "planes%d" % g) for g in range(2)]
+        zb = [[held([P, HALF, PACK], BF16, "zb%d_%d" % (h, g)) for g in range(2)] for h in range(2)]
+        zq = [[held([P, HALF], U32, "zq%d_%d" % (h, g)) for g in range(2)] for h in range(2)]
+        zs = [[held([P, HALF], U8, "zs%d_%d" % (h, g)) for g in range(2)] for h in range(2)]
+        wb = [held([P, N, PACK], BF16, "wb%d" % g) for g in range(2)]
+        wq = [held([P, N], U32, "wq%d" % g) for g in range(2)]
+        ws = [held([P, N], U8, "ws%d" % g) for g in range(2)]
+
+        def quantize(codes, scales, grouped):
+            nc.vector.quantize_mx(
+                out=codes[:].bitcast(FP8X4), scales=scales[:], in_=grouped[:].rearrange("p w t -> p (w t)")
+            )
+
+        def empty_first(b):
+            g, t = divmod(b, PACK)
+            nc.scalar.activation(planes[g][:, t, :], first[b][:], ACT.Relu, scale=mag[:, g, t : t + 1])
+
+        def sign_first(b):
+            g, t = divmod(b, PACK)
+            nc.vector.tensor_scalar(planes[g][:, t, :], planes[g][:, t, :], sgn[:, g, t : t + 1], None, ALU.mult)
+
+        def weave(dst, src):
+            return (
+                dst[:].rearrange("p (c i) t -> p c t i", i=4),
+                src[:].rearrange("p t (c i) -> p c t i", i=4),
+            )
+
+        second = []
+
+        def score_second(b):
+            g, c = divmod(b, 4)
+            acc = bank(b, "second%d" % b)
+            second.append(acc)
+            for t in range(PACK):
+                for a in range(2):
+                    score(acc[:, P * t : P * (t + 1)], g, t, a, 1, P * c, P)
+
+        def empty_second(b):
+            g, c = divmod(b, 4)
+            nc.vector.scalar_tensor_tensor(
+                zb[1][g][:, P * c : P * (c + 1), :],
+                second[b][:].rearrange("p (t n) -> p n t", t=PACK),
+                0.0,
+                rec_t[:, g : g + 1, :].to_broadcast([P, P, PACK]),
+                ALU.max,
+                ALU.mult,
+            )
+
+        def profile(h, c, slot):
+            gate_acc = bank(2 * slot, "gate%d_%d" % (h, c))
+            y_acc = bank(2 * slot + 1, "y%d_%d" % (h, c))
+            for g in range(2):
+                nc.tensor.matmul_mx(
+                    out=gate_acc[:],
+                    lhsT=wq[g][:, P * c : P * (c + 1)].bitcast(FP8X4),
+                    lhsT_scale=ws[g][:, P * c : P * (c + 1)],
+                    rhs=zq[h][g][:].bitcast(FP8X4),
+                    rhs_scale=zs[h][g][:],
+                    start=(g == 0),
+                    stop=(g == 1),
+                )
+            for g in range(2):
+                nc.tensor.matmul_mx(
+                    out=y_acc[:],
+                    lhsT=aw[:, g, :].bitcast(U8)[:, 2 * P * c : 2 * P * (c + 1)].bitcast(FP4X4),
+                    lhsT_scale=asc[:, g, :].bitcast(U8)[:, P * c : P * (c + 1)],
+                    rhs=zq[h][g][:].bitcast(FP8X4),
+                    rhs_scale=zs[h][g][:],
+                    start=(g == 0),
+                    stop=(g == 1),
+                )
+            gate = ring.tile([P, HALF], F32, name="gate")
+            nc.scalar.activation(gate[:], gate_acc[:], ACT.Sigmoid, bias=bg_t[:, c : c + 1])
+            res = ring.tile([P, HALF], F32, name="res")
+            nc.vector.tensor_tensor(res[:], y_acc[:], gate[:], ALU.mult)
+            nc.sync.dma_start(out[P * c : P * (c + 1), HALF * h : HALF * (h + 1)], res[:])
+
+        for b in range(8):
+            empty_first(b)
+            score_second(b)
+        for g in range(2):
+            for b in range(4 * g, 4 * g + 4):
+                sign_first(b)
+            dst, src = weave(zb[0][g], planes[g])
+            nc.vector.tensor_copy(dst, src)
+            dst, src = weave(wb[g], wraw[g])
+            nc.scalar.copy(dst, src)
+            empty_second(g)
+            quantize(zq[0][g], zs[0][g], zb[0][g])
+        empty_second(2)
+        quantize(wq[0], ws[0], wb[0])
+        empty_second(3)
+        quantize(wq[1], ws[1], wb[1])
+        empty_second(4)
+        quantize(zq[1][0], zs[1][0], zb[1][0])
+        for b in range(5, 8):
+            empty_second(b)
+        profile(0, 0, 0)
+        quantize(zq[1][1], zs[1][1], zb[1][1])
+        for c in range(1, 4):
+            profile(0, c, c)
+        for c in range(4):
+            profile(1, c, c)

@@ -21,6 +21,7 @@ PACK = 4
 KP = 512
 BANK = 512
 HALF = 512
+BY_VECTOR = (1, 3)
 
 
 def tile_list_slate_candidate_profiles_kernel(
@@ -29,11 +30,11 @@ def tile_list_slate_candidate_profiles_kernel(
     nc = tc.nc
     with ExitStack() as ctx:
         keep = ctx.enter_context(tc.tile_pool(name="keep", bufs=1))
-        ring = ctx.enter_context(tc.tile_pool(name="ring", bufs=3))
+        ring = ctx.enter_context(tc.tile_pool(name="ring", bufs=8))
         psum = ctx.enter_context(tc.psum_pool(name="psum", bufs=1))
 
-        def held(shape, dtype, name):
-            return keep.tile(shape, dtype, name=name, align_bytes=64)
+        def held(shape, dtype, name, tag=""):
+            return keep.tile(shape, dtype, name=name, tag=tag or name, align_bytes=64)
 
         def bank(b, label):
             return psum.tile([P, BANK], F32, name=label, tag="bank%d" % b)
@@ -46,14 +47,13 @@ def tile_list_slate_candidate_profiles_kernel(
         t2s = held([P, T2 // 4], I32, "t2s")
         asc = held([P, 2, N // 4], I32, "asc")
         aw = held([P, 2, 2 * N // 4], I32, "aw")
-        wraw = [held([P, PACK, N], F32, "wraw%d" % a) for a in range(2)]
         rec_t = held([P, 2, PACK], F32, "rec_t")
         bg_t = held([P, N // P], F32, "bg_t")
         warm = held([P, 1], F32, "warm")
         warm2 = held([P, 1], F32, "warm2")
 
-        nc.vector.memset(t2s[:], 0)
         nc.vector.memset(ts[:], 0)
+        nc.vector.memset(t2s[:], 0)
         nc.vector.memset(asc[:], 0)
         nc.vector.memset(warm[:], 0.0)
         nc.scalar.activation(warm2[:], warm[:], ACT.Sigmoid)
@@ -61,52 +61,55 @@ def tile_list_slate_candidate_profiles_kernel(
         def words_of(tab, a):
             return tab[a].rearrange("p n t -> p (n t)").bitcast(I32)
 
+        nc.sync.dma_start(t2w[0][:], words_of(tab2_words, 0))
         nc.sync.dma_start(idx2[:], offs2)
         nc.sync.dma_start(idx[:], offs)
-        nc.sync.dma_start(t2w[0][:], words_of(tab2_words, 0))
-        for q in range(4):
-            nc.sync.dma_start(t2s[32 * q : 32 * q + 8, :], tab2_scales[:, 4 * q : 4 * q + 4, :].bitcast(I32))
         nc.sync.dma_start(tw[0][:], words_of(tab_words, 0))
-        for q in range(4):
-            nc.sync.dma_start(ts[32 * q : 32 * q + 8, :], tab_scales[:, 4 * q : 4 * q + 4, :].bitcast(I32))
         nc.sync.dma_start(tw[1][:], words_of(tab_words, 1))
         nc.sync.dma_start(t2w[1][:], words_of(tab2_words, 1))
-        nc.sync.dma_start(rec_t[:], rec.rearrange("(a p t) -> p a t", a=2, t=PACK))
-        with nc.allow_non_contiguous_dma(reason="one bias value to a partition"):
-            nc.sync.dma_start(bg_t[:], bg.rearrange("(c p) -> p c", p=P))
+        nc.sync.dma_start(aw[:], attr_words.bitcast(I32).rearrange("a p n -> p a n"))
         for q in range(4):
-            nc.sync.dma_start(
+            nc.gpsimd.dma_start(ts[32 * q : 32 * q + 8, :], tab_scales[:, 4 * q : 4 * q + 4, :].bitcast(I32))
+        for q in range(4):
+            nc.gpsimd.dma_start(t2s[32 * q : 32 * q + 8, :], tab2_scales[:, 4 * q : 4 * q + 4, :].bitcast(I32))
+        nc.scalar.dma_start(rec_t[:], rec.rearrange("(a p t) -> p a t", a=2, t=PACK))
+        with nc.allow_non_contiguous_dma(reason="one bias value to a partition"):
+            nc.scalar.dma_start(bg_t[:], bg.rearrange("(c p) -> p c", p=P))
+        for q in range(4):
+            nc.scalar.dma_start(
                 asc[32 * q : 32 * q + 4, :, :],
                 attr_scales[:, 4 * q : 4 * q + 4, :].bitcast(I32).rearrange("a s n -> s a n"),
             )
-        for a in range(2):
-            nc.sync.dma_start(wraw[a][:], wg[KP * a : KP * (a + 1), :].rearrange("(p t) n -> p t n", t=PACK))
-        nc.sync.dma_start(aw[:], attr_words.bitcast(I32).rearrange("a p n -> p a n"))
 
-        vw = [held([P, S], U32, "vw%d" % a) for a in range(2)]
         vs_list = held([P, S], U8, "vs_list")
         vs = held([P, S], U8, "vs")
-        v2w = [[held([P, HALF], U32, "v2w%d_%d" % (a, h)) for h in range(2)] for a in range(2)]
         v2s = held([P, S2], U8, "v2s")
+        early2 = held([P, S2], U32, "early2")
+        v2w = [[early2[:, HALF * h : HALF * (h + 1)] for h in range(2)]]
+        vw = []
 
-        def gather_v(a):
-            for g in range(2):
-                nc.vector.tensor_copy(
-                    vw[a][:, KP * g : KP * (g + 1)].rearrange("p (t m) -> p m t", t=PACK),
-                    tw[a][:].bitcast(U32).indirect(idx[:, 32 * g : 32 * (g + 1)]),
-                )
+        def gather_v(a, g):
+            nc.vector.tensor_copy(
+                vw[a][g].rearrange("p (t m) -> p m t", t=PACK),
+                tw[a][:].bitcast(U32).indirect(idx[:, 32 * g : 32 * (g + 1)]),
+            )
 
         def gather_v2(a, h):
-            nc.vector.tensor_copy(v2w[a][h][:], t2w[a][:].bitcast(U32).indirect(idx2[:, 32 * h : 32 * (h + 1)]))
+            nc.vector.tensor_copy(v2w[a][h], t2w[a][:].bitcast(U32).indirect(idx2[:, 32 * h : 32 * (h + 1)]))
 
         gather_v2(0, 0)
-        nc.vector.tensor_copy(v2s[:], t2s[:].bitcast(U8).indirect(idx2[:]))
         nc.vector.tensor_copy(vs_list[:], ts[:].bitcast(U8).indirect(idx[:]))
-        gather_v(0)
         nc.vector.tensor_copy(
             vs[:].rearrange("p (g t m) -> p g t m", g=2, t=PACK),
             vs_list[:].rearrange("p (g m t) -> p g t m", g=2, t=PACK),
         )
+        nc.vector.tensor_copy(v2s[:], t2s[:].bitcast(U8).indirect(idx2[:]))
+        vw.append([held([P, KP], U32, "vw00", tag="t2s")[:], held([P, KP], U32, "vw01", tag="ts")[:]])
+        gather_v(0, 0)
+        gather_v(0, 1)
+        late = held([P, 4, KP], U32, "late", tag="tw0")
+        vw.append([late[:, 0, :], late[:, 1, :]])
+        v2w.append([late[:, 2, :], late[:, 3, :]])
         sgn = held([P, 2, PACK], F32, "sgn")
         mag = held([P, 2, PACK], F32, "mag")
         nc.scalar.activation(sgn[:], rec_t[:], ACT.Sign)
@@ -116,7 +119,7 @@ def tile_list_slate_candidate_profiles_kernel(
             m0 = KP * g + P * t
             nc.tensor.matmul_mx(
                 out=acc,
-                lhsT=vw[a][:, m0 : m0 + P].bitcast(FP8X4),
+                lhsT=vw[a][g][:, P * t : P * (t + 1)].bitcast(FP8X4),
                 lhsT_scale=vs[4 * a : P, m0 : m0 + P],
                 rhs=v2w[a][h][:, c0 : c0 + width].bitcast(FP8X4),
                 rhs_scale=v2s[4 * a : P, HALF * h + c0 : HALF * h + c0 + width],
@@ -127,7 +130,12 @@ def tile_list_slate_candidate_profiles_kernel(
         first = [bank(b, "first%d" % b) for b in range(8)]
         for b in range(8):
             score(first[b][:], b // 4, b % 4, 0, 0, 0, HALF)
-        gather_v(1)
+        gather_v(1, 0)
+        gather_v(1, 1)
+        wraw_all = held([P, 2, PACK, N], F32, "wraw", tag="tw1")
+        wraw = [wraw_all[:, a, :, :] for a in range(2)]
+        for a in range(2):
+            nc.sync.dma_start(wraw[a], wg[KP * a : KP * (a + 1), :].rearrange("(p t) n -> p t n", t=PACK))
         gather_v2(1, 0)
         for b in range(8):
             score(first[b][:], b // 4, b % 4, 1, 0, 0, HALF)
@@ -149,7 +157,12 @@ def tile_list_slate_candidate_profiles_kernel(
 
         def empty_first(b):
             g, t = divmod(b, PACK)
-            nc.scalar.activation(planes[g][:, t, :], first[b][:], ACT.Relu, scale=mag[:, g, t : t + 1])
+            if b in BY_VECTOR:
+                nc.vector.tensor_scalar(
+                    planes[g][:, t, :], first[b][:], 0.0, rec_t[:, g, t : t + 1], ALU.max, ALU.mult
+                )
+            else:
+                nc.scalar.activation(planes[g][:, t, :], first[b][:], ACT.Relu, scale=mag[:, g, t : t + 1])
 
         def sign_first(b):
             g, t = divmod(b, PACK)
@@ -157,8 +170,8 @@ def tile_list_slate_candidate_profiles_kernel(
 
         def weave(dst, src):
             return (
-                dst[:].rearrange("p (c i) t -> p c t i", i=4),
-                src[:].rearrange("p t (c i) -> p c t i", i=4),
+                dst.rearrange("p (c i) t -> p c t i", i=4),
+                src.rearrange("p t (c i) -> p c t i", i=4),
             )
 
         second = []
@@ -216,24 +229,22 @@ def tile_list_slate_candidate_profiles_kernel(
             score_second(b)
         for g in range(2):
             for b in range(4 * g, 4 * g + 4):
-                sign_first(b)
-            dst, src = weave(zb[0][g], planes[g])
+                if b not in BY_VECTOR:
+                    sign_first(b)
+            dst, src = weave(zb[0][g][:], planes[g][:])
             nc.vector.tensor_copy(dst, src)
-            dst, src = weave(wb[g], wraw[g])
-            nc.scalar.copy(dst, src)
-            empty_second(g)
             quantize(zq[0][g], zs[0][g], zb[0][g])
-        empty_second(2)
-        quantize(wq[0], ws[0], wb[0])
-        empty_second(3)
-        quantize(wq[1], ws[1], wb[1])
-        empty_second(4)
-        quantize(zq[1][0], zs[1][0], zb[1][0])
-        for b in range(5, 8):
-            empty_second(b)
-        profile(0, 0, 0)
-        quantize(zq[1][1], zs[1][1], zb[1][1])
-        for c in range(1, 4):
-            profile(0, c, c)
-        for c in range(4):
-            profile(1, c, c)
+        for g in range(2):
+            for half in range(2):
+                cols = slice(N // 2 * half, N // 2 * (half + 1))
+                dst, src = weave(wb[g][:, cols, :], wraw[g][:, :, cols])
+                nc.scalar.copy(dst, src)
+        for g in range(2):
+            quantize(wq[g], ws[g], wb[g])
+        for g in range(2):
+            for b in range(4 * g, 4 * g + 4):
+                empty_second(b)
+            quantize(zq[1][g], zs[1][g], zb[1][g])
+        for h in range(2):
+            for c in range(4):
+                profile(h, c, c)

@@ -45,18 +45,9 @@ def tile_list_slate_candidate_profiles_kernel(
         t2w = [held([P, T2], I32, "t2w%d" % a) for a in range(2)]
         ts = held([P, T // 4], I32, "ts")
         t2s = held([P, T2 // 4], I32, "t2s")
-        asc = held([P, 2, N // 4], I32, "asc")
-        aw = held([P, 2, 2 * N // 4], I32, "aw")
-        rec_t = held([P, 2, PACK], F32, "rec_t")
-        bg_t = held([P, N // P], F32, "bg_t")
-        warm = held([P, 1], F32, "warm")
-        warm2 = held([P, 1], F32, "warm2")
 
-        nc.vector.memset(ts[:], 0)
         nc.vector.memset(t2s[:], 0)
-        nc.vector.memset(asc[:], 0)
-        nc.vector.memset(warm[:], 0.0)
-        nc.scalar.activation(warm2[:], warm[:], ACT.Sigmoid)
+        nc.vector.memset(ts[:], 0)
 
         def words_of(tab, a):
             return tab[a].rearrange("p n t -> p (n t)").bitcast(I32)
@@ -64,22 +55,13 @@ def tile_list_slate_candidate_profiles_kernel(
         nc.sync.dma_start(t2w[0][:], words_of(tab2_words, 0))
         nc.sync.dma_start(idx2[:], offs2)
         nc.sync.dma_start(idx[:], offs)
+        for q in range(4):
+            nc.sync.dma_start(t2s[32 * q : 32 * q + 8, :], tab2_scales[:, 4 * q : 4 * q + 4, :].bitcast(I32))
+        for q in range(4):
+            nc.sync.dma_start(ts[32 * q : 32 * q + 8, :], tab_scales[:, 4 * q : 4 * q + 4, :].bitcast(I32))
         nc.sync.dma_start(tw[0][:], words_of(tab_words, 0))
         nc.sync.dma_start(tw[1][:], words_of(tab_words, 1))
         nc.sync.dma_start(t2w[1][:], words_of(tab2_words, 1))
-        nc.sync.dma_start(aw[:], attr_words.bitcast(I32).rearrange("a p n -> p a n"))
-        for q in range(4):
-            nc.gpsimd.dma_start(ts[32 * q : 32 * q + 8, :], tab_scales[:, 4 * q : 4 * q + 4, :].bitcast(I32))
-        for q in range(4):
-            nc.gpsimd.dma_start(t2s[32 * q : 32 * q + 8, :], tab2_scales[:, 4 * q : 4 * q + 4, :].bitcast(I32))
-        nc.scalar.dma_start(rec_t[:], rec.rearrange("(a p t) -> p a t", a=2, t=PACK))
-        with nc.allow_non_contiguous_dma(reason="one bias value to a partition"):
-            nc.scalar.dma_start(bg_t[:], bg.rearrange("(c p) -> p c", p=P))
-        for q in range(4):
-            nc.scalar.dma_start(
-                asc[32 * q : 32 * q + 4, :, :],
-                attr_scales[:, 4 * q : 4 * q + 4, :].bitcast(I32).rearrange("a s n -> s a n"),
-            )
 
         vs_list = held([P, S], U8, "vs_list")
         vs = held([P, S], U8, "vs")
@@ -98,18 +80,32 @@ def tile_list_slate_candidate_profiles_kernel(
             nc.vector.tensor_copy(v2w[a][h], t2w[a][:].bitcast(U32).indirect(idx2[:, 32 * h : 32 * (h + 1)]))
 
         gather_v2(0, 0)
+        nc.vector.tensor_copy(v2s[:], t2s[:].bitcast(U8).indirect(idx2[:]))
         nc.vector.tensor_copy(vs_list[:], ts[:].bitcast(U8).indirect(idx[:]))
         nc.vector.tensor_copy(
             vs[:].rearrange("p (g t m) -> p g t m", g=2, t=PACK),
             vs_list[:].rearrange("p (g m t) -> p g t m", g=2, t=PACK),
         )
-        nc.vector.tensor_copy(v2s[:], t2s[:].bitcast(U8).indirect(idx2[:]))
-        vw.append([held([P, KP], U32, "vw00", tag="t2s")[:], held([P, KP], U32, "vw01", tag="ts")[:]])
+        rec_t = held([P, 2, PACK], F32, "rec_t", tag="t2s")
+        nc.sync.dma_start(rec_t[:], rec.rearrange("(a p t) -> p a t", a=2, t=PACK))
+        bg_t = held([P, N // P], F32, "bg_t", tag="ts")
+        with nc.allow_non_contiguous_dma(reason="one bias value to a partition"):
+            nc.sync.dma_start(bg_t[:], bg.rearrange("(c p) -> p c", p=P))
+        asc = held([P, 2, N // 4], I32, "asc", tag="vs_list")
+        nc.vector.memset(asc[:], 0)
+        for q in range(4):
+            nc.sync.dma_start(
+                asc[32 * q : 32 * q + 4, :, :],
+                attr_scales[:, 4 * q : 4 * q + 4, :].bitcast(I32).rearrange("a s n -> s a n"),
+            )
+        vw_all = held([P, 4, KP], U32, "vw_all")
+        vw.extend([[vw_all[:, 2 * a + g, :] for g in range(2)] for a in range(2)])
         gather_v(0, 0)
         gather_v(0, 1)
-        late = held([P, 4, KP], U32, "late", tag="tw0")
-        vw.append([late[:, 0, :], late[:, 1, :]])
-        v2w.append([late[:, 2, :], late[:, 3, :]])
+        aw = held([P, 2, 2 * N // 4], I32, "aw", tag="tw0")
+        nc.sync.dma_start(aw[:], attr_words.bitcast(I32).rearrange("a p n -> p a n"))
+        late2 = held([P, S2], U32, "late2")
+        v2w.append([late2[:, HALF * h : HALF * (h + 1)] for h in range(2)])
         sgn = held([P, 2, PACK], F32, "sgn")
         mag = held([P, 2, PACK], F32, "mag")
         nc.scalar.activation(sgn[:], rec_t[:], ACT.Sign)

@@ -18,10 +18,23 @@ ACT = mybir.ActivationFunctionType
 
 P = 128
 PACK = 4
-KP = 512
-BANK = 512
-HALF = 512
-BY_VECTOR = (1, 3)
+PASS = P * PACK
+K_PASSES = K // PASS
+GROUPS = S // PASS
+QUADRANTS = 4
+QUAD = P // QUADRANTS
+ROWS = 4
+BANKS = 8
+HALF = S2 // 2
+LIST_COLS = PASS // 16
+N_TILES = N // P
+RUN = 4
+
+V_ROW = 0
+V2_ROW = K_PASSES * ROWS
+
+VECTOR_BANKS = (1, 3)
+SCALAR_PIECE = (GROUPS - 1, 1)
 
 
 def tile_list_slate_candidate_profiles_kernel(
@@ -30,217 +43,219 @@ def tile_list_slate_candidate_profiles_kernel(
     nc = tc.nc
     with ExitStack() as ctx:
         keep = ctx.enter_context(tc.tile_pool(name="keep", bufs=1))
-        ring = ctx.enter_context(tc.tile_pool(name="ring", bufs=8))
+        ring = ctx.enter_context(tc.tile_pool(name="ring", bufs=2 * N_TILES))
         psum = ctx.enter_context(tc.psum_pool(name="psum", bufs=1))
 
-        def held(shape, dtype, name, tag=""):
-            return keep.tile(shape, dtype, name=name, tag=tag or name, align_bytes=64)
+        def held(shape, dtype, name, after=""):
+            return keep.tile(shape, dtype, name=name, tag=after or name, align_bytes=64)
 
-        def bank(b, label):
-            return psum.tile([P, BANK], F32, name=label, tag="bank%d" % b)
+        def bank(b, name):
+            return psum.tile([P, HALF], F32, name=name, tag="bank%d" % b)
+
+        def halves(width):
+            return [slice(0, width // 2), slice(width // 2, width)]
 
         idx = keep.tile([P, S // 16], U16, name="idx")
         idx2 = keep.tile([P, S2 // 16], U16, name="idx2")
-        tw = [held([P, T], I32, "tw%d" % a) for a in range(2)]
-        t2w = [held([P, T2], I32, "t2w%d" % a) for a in range(2)]
-        ts = held([P, T // 4], I32, "ts")
-        t2s = held([P, T2 // 4], I32, "t2s")
+        tab_w = [held([P, T], I32, "tab_w%d" % a) for a in range(K_PASSES)]
+        tab2_w = [held([P, T2], I32, "tab2_w%d" % a) for a in range(K_PASSES)]
+        tab_s = held([P, T // 4], I32, "tab_s")
+        tab2_s = held([P, T2 // 4], I32, "tab2_s")
 
-        nc.vector.memset(t2s[:], 0)
-        nc.vector.memset(ts[:], 0)
+        nc.vector.memset(tab2_s[:], 0)
+        nc.vector.memset(tab_s[:], 0)
 
-        def words_of(tab, a):
-            return tab[a].rearrange("p n t -> p (n t)").bitcast(I32)
+        def load_words(tile, words, a):
+            nc.sync.dma_start(tile[:], words[a].rearrange("p n t -> p (n t)").bitcast(I32))
 
-        nc.sync.dma_start(t2w[0][:], words_of(tab2_words, 0))
+        def load_scales(tile, scales, row):
+            for q in range(QUADRANTS):
+                first_row = QUAD * q + row
+                nc.sync.dma_start(
+                    tile[first_row : first_row + K_PASSES * ROWS, :],
+                    scales[:, ROWS * q : ROWS * (q + 1), :].bitcast(I32),
+                )
+
         nc.sync.dma_start(idx2[:], offs2)
         nc.sync.dma_start(idx[:], offs)
-        for q in range(4):
-            nc.sync.dma_start(t2s[32 * q : 32 * q + 8, :], tab2_scales[:, 4 * q : 4 * q + 4, :].bitcast(I32))
-        for q in range(4):
-            nc.sync.dma_start(ts[32 * q : 32 * q + 8, :], tab_scales[:, 4 * q : 4 * q + 4, :].bitcast(I32))
-        nc.sync.dma_start(tw[0][:], words_of(tab_words, 0))
-        nc.sync.dma_start(tw[1][:], words_of(tab_words, 1))
-        nc.sync.dma_start(t2w[1][:], words_of(tab2_words, 1))
+        rec_t = held([P, GROUPS, PACK], F32, "rec_t")
+        nc.sync.dma_start(rec_t[:], rec.rearrange("(g p t) -> p g t", g=GROUPS, t=PACK))
+        load_scales(tab2_s, tab2_scales, V2_ROW)
+        load_words(tab2_w[0], tab2_words, 0)
+        load_scales(tab_s, tab_scales, V_ROW)
+        load_words(tab_w[0], tab_words, 0)
+        load_words(tab_w[1], tab_words, 1)
+        load_words(tab2_w[1], tab2_words, 1)
 
-        vs_list = held([P, S], U8, "vs_list")
-        vs = held([P, S], U8, "vs")
-        v2s = held([P, S2], U8, "v2s")
-        early2 = held([P, S2], U32, "early2")
-        v2w = [[early2[:, HALF * h : HALF * (h + 1)] for h in range(2)]]
-        vw = []
+        v_s_listed = held([P, S], U8, "v_s_listed")
+        v_s = held([P, S], U8, "v_s")
+        v2_s = held([P, S2], U8, "v2_s")
+        v2_w0 = held([P, S2], U32, "v2_w0")
+
+        nc.vector.tensor_copy(v2_s[:], tab2_s[:].bitcast(U8).indirect(idx2[:]))
+        nc.vector.tensor_copy(v2_w0[:], tab2_w[0][:].bitcast(U32).indirect(idx2[:]))
+        nc.vector.tensor_copy(v_s_listed[:], tab_s[:].bitcast(U8).indirect(idx[:]))
+        nc.vector.tensor_copy(
+            v_s[:].rearrange("p (g t m) -> p g t m", g=GROUPS, t=PACK),
+            v_s_listed[:].rearrange("p (g m t) -> p g t m", g=GROUPS, t=PACK),
+        )
+
+        bg_t = held([P, N_TILES], F32, "bg_t", after="tab2_s")
+        with nc.allow_non_contiguous_dma(reason="one bias value to a partition"):
+            nc.sync.dma_start(bg_t[:], bg.rearrange("(c p) -> p c", p=P))
+        attr_s = held([P, GROUPS, N // 4], I32, "attr_s", after="v_s_listed")
+        nc.gpsimd.memset(attr_s[:], 0)
+        for q in range(QUADRANTS):
+            nc.sync.dma_start(
+                attr_s[QUAD * q : QUAD * q + ROWS, :, :],
+                attr_scales[:, ROWS * q : ROWS * (q + 1), :].bitcast(I32).rearrange("g s n -> s g n"),
+            )
+
+        v_w = held([P, K_PASSES, GROUPS, PASS], U32, "v_w")
 
         def gather_v(a, g):
             nc.vector.tensor_copy(
-                vw[a][g].rearrange("p (t m) -> p m t", t=PACK),
-                tw[a][:].bitcast(U32).indirect(idx[:, 32 * g : 32 * (g + 1)]),
+                v_w[:, a, g, :].rearrange("p (t m) -> p m t", t=PACK),
+                tab_w[a][:].bitcast(U32).indirect(idx[:, LIST_COLS * g : LIST_COLS * (g + 1)]),
             )
 
-        def gather_v2(a, h):
-            nc.vector.tensor_copy(v2w[a][h], t2w[a][:].bitcast(U32).indirect(idx2[:, 32 * h : 32 * (h + 1)]))
+        for g in range(GROUPS):
+            gather_v(0, g)
 
-        gather_v2(0, 0)
-        nc.vector.tensor_copy(v2s[:], t2s[:].bitcast(U8).indirect(idx2[:]))
-        nc.vector.tensor_copy(vs_list[:], ts[:].bitcast(U8).indirect(idx[:]))
-        nc.vector.tensor_copy(
-            vs[:].rearrange("p (g t m) -> p g t m", g=2, t=PACK),
-            vs_list[:].rearrange("p (g m t) -> p g t m", g=2, t=PACK),
-        )
-        rec_t = held([P, 2, PACK], F32, "rec_t", tag="t2s")
-        nc.sync.dma_start(rec_t[:], rec.rearrange("(a p t) -> p a t", a=2, t=PACK))
-        bg_t = held([P, N // P], F32, "bg_t", tag="ts")
-        with nc.allow_non_contiguous_dma(reason="one bias value to a partition"):
-            nc.sync.dma_start(bg_t[:], bg.rearrange("(c p) -> p c", p=P))
-        asc = held([P, 2, N // 4], I32, "asc", tag="vs_list")
-        nc.vector.memset(asc[:], 0)
-        for q in range(4):
+        wg_rows = held([P, GROUPS, PACK, N], F32, "wg_rows", after="tab_w0")
+        for g in range(GROUPS):
             nc.sync.dma_start(
-                asc[32 * q : 32 * q + 4, :, :],
-                attr_scales[:, 4 * q : 4 * q + 4, :].bitcast(I32).rearrange("a s n -> s a n"),
+                wg_rows[:, g, :, :], wg[PASS * g : PASS * (g + 1), :].rearrange("(p t) n -> p t n", t=PACK)
             )
-        vw_all = held([P, 4, KP], U32, "vw_all")
-        vw.extend([[vw_all[:, 2 * a + g, :] for g in range(2)] for a in range(2)])
-        gather_v(0, 0)
-        gather_v(0, 1)
-        aw = held([P, 2, 2 * N // 4], I32, "aw", tag="tw0")
-        nc.sync.dma_start(aw[:], attr_words.bitcast(I32).rearrange("a p n -> p a n"))
-        late2 = held([P, S2], U32, "late2")
-        v2w.append([late2[:, HALF * h : HALF * (h + 1)] for h in range(2)])
-        sgn = held([P, 2, PACK], F32, "sgn")
-        mag = held([P, 2, PACK], F32, "mag")
-        nc.scalar.activation(sgn[:], rec_t[:], ACT.Sign)
-        nc.scalar.activation(mag[:], rec_t[:], ACT.Abs)
 
-        def score(acc, g, t, a, h, c0, width):
-            m0 = KP * g + P * t
+        v2_w1 = held([P, S2], U32, "v2_w1")
+        v2_w = [v2_w0, v2_w1]
+
+        def gather_v2_last_pass(h):
+            nc.vector.tensor_copy(
+                v2_w1[:, HALF * h : HALF * (h + 1)],
+                tab2_w[1][:].bitcast(U32).indirect(idx2[:, LIST_COLS * h : LIST_COLS * (h + 1)]),
+            )
+
+        rec_sign = held([P, GROUPS, PACK], F32, "rec_sign")
+        rec_size = held([P, GROUPS, PACK], F32, "rec_size")
+        nc.scalar.activation(rec_sign[:], rec_t[:], ACT.Sign)
+        nc.scalar.activation(rec_size[:], rec_t[:], ACT.Abs)
+
+        def score(acc, g, t, a, j0, width):
+            m0 = PASS * g + P * t
             nc.tensor.matmul_mx(
                 out=acc,
-                lhsT=vw[a][g][:, P * t : P * (t + 1)].bitcast(FP8X4),
-                lhsT_scale=vs[4 * a : P, m0 : m0 + P],
-                rhs=v2w[a][h][:, c0 : c0 + width].bitcast(FP8X4),
-                rhs_scale=v2s[4 * a : P, HALF * h + c0 : HALF * h + c0 + width],
+                lhsT=v_w[:, a, g, P * t : P * (t + 1)].bitcast(FP8X4),
+                lhsT_scale=v_s[V_ROW + ROWS * a : P, m0 : m0 + P],
+                rhs=v2_w[a][:, j0 : j0 + width].bitcast(FP8X4),
+                rhs_scale=v2_s[V2_ROW + ROWS * a : P, j0 : j0 + width],
                 start=(a == 0),
-                stop=(a == 1),
+                stop=(a == K_PASSES - 1),
             )
 
-        first = [bank(b, "first%d" % b) for b in range(8)]
-        for b in range(8):
-            score(first[b][:], b // 4, b % 4, 0, 0, 0, HALF)
+        first = [bank(b, "first%d" % b) for b in range(BANKS)]
+        for b in range(BANKS):
+            score(first[b][:], b // PACK, b % PACK, 0, 0, HALF)
         gather_v(1, 0)
+        gather_v2_last_pass(0)
         gather_v(1, 1)
-        wraw_all = held([P, 2, PACK, N], F32, "wraw", tag="tw1")
-        wraw = [wraw_all[:, a, :, :] for a in range(2)]
-        for a in range(2):
-            nc.sync.dma_start(wraw[a], wg[KP * a : KP * (a + 1), :].rearrange("(p t) n -> p t n", t=PACK))
-        gather_v2(1, 0)
-        for b in range(8):
-            score(first[b][:], b // 4, b % 4, 1, 0, 0, HALF)
-        gather_v2(0, 1)
-        gather_v2(1, 1)
+        attr_w = held([P, GROUPS, 2 * N // 4], I32, "attr_w", after="tab_w1")
+        nc.sync.dma_start(attr_w[:], attr_words.bitcast(I32).rearrange("g p n -> p g n"))
+        for b in range(BANKS):
+            score(first[b][:], b // PACK, b % PACK, 1, 0, HALF)
+        gather_v2_last_pass(1)
 
-        planes = [held([P, PACK, HALF], BF16, "planes%d" % g) for g in range(2)]
-        zb = [[held([P, HALF, PACK], BF16, "zb%d_%d" % (h, g)) for g in range(2)] for h in range(2)]
-        zq = [[held([P, HALF], U32, "zq%d_%d" % (h, g)) for g in range(2)] for h in range(2)]
-        zs = [[held([P, HALF], U8, "zs%d_%d" % (h, g)) for g in range(2)] for h in range(2)]
-        wb = [held([P, N, PACK], BF16, "wb%d" % g) for g in range(2)]
-        wq = [held([P, N], U32, "wq%d" % g) for g in range(2)]
-        ws = [held([P, N], U8, "ws%d" % g) for g in range(2)]
+        z_rows = [held([P, PACK, HALF], BF16, "z_rows%d" % g) for g in range(GROUPS)]
+        z_bf = [[held([P, HALF, PACK], BF16, "z_bf%d_%d" % (h, g)) for g in range(GROUPS)] for h in range(2)]
+        z_w = [[held([P, HALF], U32, "z_w%d_%d" % (h, g)) for g in range(GROUPS)] for h in range(2)]
+        z_s = [[held([P, HALF], U8, "z_s%d_%d" % (h, g)) for g in range(GROUPS)] for h in range(2)]
+        wg_bf = held([P, GROUPS, N, PACK], BF16, "wg_bf")
+        wg_w = [held([P, N], U32, "wg_w%d" % g) for g in range(GROUPS)]
+        wg_s = [held([P, N], U8, "wg_s%d" % g) for g in range(GROUPS)]
 
-        def quantize(codes, scales, grouped):
+        def quantize(words, scales, side_by_side):
             nc.vector.quantize_mx(
-                out=codes[:].bitcast(FP8X4), scales=scales[:], in_=grouped[:].rearrange("p w t -> p (w t)")
+                out=words[:].bitcast(FP8X4), scales=scales[:], in_=side_by_side.rearrange("p w t -> p (w t)")
+            )
+
+        def interleave(copy, side_by_side, rows):
+            copy(
+                side_by_side.rearrange("p (c r) t -> p c t r", r=RUN),
+                rows.rearrange("p t (c r) -> p c t r", r=RUN),
             )
 
         def empty_first(b):
             g, t = divmod(b, PACK)
-            if b in BY_VECTOR:
+            if b in VECTOR_BANKS:
                 nc.vector.tensor_scalar(
-                    planes[g][:, t, :], first[b][:], 0.0, rec_t[:, g, t : t + 1], ALU.max, ALU.mult
+                    z_rows[g][:, t, :], first[b][:], 0.0, rec_t[:, g, t : t + 1], ALU.max, ALU.mult
                 )
             else:
-                nc.scalar.activation(planes[g][:, t, :], first[b][:], ACT.Relu, scale=mag[:, g, t : t + 1])
-
-        def sign_first(b):
-            g, t = divmod(b, PACK)
-            nc.vector.tensor_scalar(planes[g][:, t, :], planes[g][:, t, :], sgn[:, g, t : t + 1], None, ALU.mult)
-
-        def weave(dst, src):
-            return (
-                dst.rearrange("p (c i) t -> p c t i", i=4),
-                src.rearrange("p t (c i) -> p c t i", i=4),
-            )
+                nc.scalar.activation(z_rows[g][:, t, :], first[b][:], ACT.Relu, scale=rec_size[:, g, t : t + 1])
 
         second = []
-
-        def score_second(b):
-            g, c = divmod(b, 4)
+        for b in range(BANKS):
+            empty_first(b)
+            g, c = divmod(b, PACK)
             acc = bank(b, "second%d" % b)
             second.append(acc)
             for t in range(PACK):
-                for a in range(2):
-                    score(acc[:, P * t : P * (t + 1)], g, t, a, 1, P * c, P)
+                for a in range(K_PASSES):
+                    score(acc[:, P * t : P * (t + 1)], g, t, a, HALF + P * c, P)
 
-        def empty_second(b):
-            g, c = divmod(b, 4)
-            nc.vector.scalar_tensor_tensor(
-                zb[1][g][:, P * c : P * (c + 1), :],
-                second[b][:].rearrange("p (t n) -> p n t", t=PACK),
-                0.0,
-                rec_t[:, g : g + 1, :].to_broadcast([P, P, PACK]),
-                ALU.max,
-                ALU.mult,
-            )
+        for g in range(GROUPS):
+            for t in range(PACK):
+                if PACK * g + t not in VECTOR_BANKS:
+                    row = z_rows[g][:, t, :]
+                    nc.vector.tensor_scalar(row, row, rec_sign[:, g, t : t + 1], None, ALU.mult)
+            for piece, cols in enumerate(halves(HALF)):
+                copy = nc.scalar.copy if (g, piece) == SCALAR_PIECE else nc.vector.tensor_copy
+                interleave(copy, z_bf[0][g][:, cols, :], z_rows[g][:, :, cols])
+            quantize(z_w[0][g], z_s[0][g], z_bf[0][g][:])
 
-        def profile(h, c, slot):
-            gate_acc = bank(2 * slot, "gate%d_%d" % (h, c))
-            y_acc = bank(2 * slot + 1, "y%d_%d" % (h, c))
-            for g in range(2):
-                nc.tensor.matmul_mx(
-                    out=gate_acc[:],
-                    lhsT=wq[g][:, P * c : P * (c + 1)].bitcast(FP8X4),
-                    lhsT_scale=ws[g][:, P * c : P * (c + 1)],
-                    rhs=zq[h][g][:].bitcast(FP8X4),
-                    rhs_scale=zs[h][g][:],
-                    start=(g == 0),
-                    stop=(g == 1),
+        for g in range(GROUPS):
+            for cols in halves(N):
+                interleave(nc.scalar.copy, wg_bf[:, g, cols, :], wg_rows[:, g, :, cols])
+            quantize(wg_w[g], wg_s[g], wg_bf[:, g, :, :])
+
+        for g in range(GROUPS):
+            for c in range(PACK):
+                nc.vector.scalar_tensor_tensor(
+                    z_bf[1][g][:, P * c : P * (c + 1), :],
+                    second[PACK * g + c][:].rearrange("p (t j) -> p j t", t=PACK),
+                    0.0,
+                    rec_t[:, g : g + 1, :].to_broadcast([P, P, PACK]),
+                    ALU.max,
+                    ALU.mult,
                 )
-            for g in range(2):
-                nc.tensor.matmul_mx(
-                    out=y_acc[:],
-                    lhsT=aw[:, g, :].bitcast(U8)[:, 2 * P * c : 2 * P * (c + 1)].bitcast(FP4X4),
-                    lhsT_scale=asc[:, g, :].bitcast(U8)[:, P * c : P * (c + 1)],
-                    rhs=zq[h][g][:].bitcast(FP8X4),
-                    rhs_scale=zs[h][g][:],
-                    start=(g == 0),
-                    stop=(g == 1),
-                )
-            gate = ring.tile([P, HALF], F32, name="gate")
-            nc.scalar.activation(gate[:], gate_acc[:], ACT.Sigmoid, bias=bg_t[:, c : c + 1])
-            res = ring.tile([P, HALF], F32, name="res")
-            nc.vector.tensor_tensor(res[:], y_acc[:], gate[:], ALU.mult)
-            nc.sync.dma_start(out[P * c : P * (c + 1), HALF * h : HALF * (h + 1)], res[:])
+            quantize(z_w[1][g], z_s[1][g], z_bf[1][g][:])
 
-        for b in range(8):
-            empty_first(b)
-            score_second(b)
-        for g in range(2):
-            for b in range(4 * g, 4 * g + 4):
-                if b not in BY_VECTOR:
-                    sign_first(b)
-            dst, src = weave(zb[0][g][:], planes[g][:])
-            nc.vector.tensor_copy(dst, src)
-            quantize(zq[0][g], zs[0][g], zb[0][g])
-        for g in range(2):
-            for half in range(2):
-                cols = slice(N // 2 * half, N // 2 * (half + 1))
-                dst, src = weave(wb[g][:, cols, :], wraw[g][:, :, cols])
-                nc.scalar.copy(dst, src)
-        for g in range(2):
-            quantize(wq[g], ws[g], wb[g])
-        for g in range(2):
-            for b in range(4 * g, 4 * g + 4):
-                empty_second(b)
-            quantize(zq[1][g], zs[1][g], zb[1][g])
+        attr_operand = [
+            (attr_w[:, g, :].bitcast(U8).bitcast(FP4X4), attr_s[:, g, :].bitcast(U8)) for g in range(GROUPS)
+        ]
+        wg_operand = [(wg_w[g][:].bitcast(FP8X4), wg_s[g][:]) for g in range(GROUPS)]
         for h in range(2):
-            for c in range(4):
-                profile(h, c, c)
+            for c in range(N_TILES):
+                n_cols = slice(P * c, P * (c + 1))
+                y_acc = bank(c, "y%d_%d" % (h, c))
+                gate_acc = bank(N_TILES + c, "gate%d_%d" % (h, c))
+                sums = [(y_acc, attr_operand), (gate_acc, wg_operand)]
+                for acc, operand in sums if h == 0 else reversed(sums):
+                    for g, (words, scales) in enumerate(operand):
+                        nc.tensor.matmul_mx(
+                            out=acc[:],
+                            lhsT=words[:, n_cols],
+                            lhsT_scale=scales[:, n_cols],
+                            rhs=z_w[h][g][:].bitcast(FP8X4),
+                            rhs_scale=z_s[h][g][:],
+                            start=(g == 0),
+                            stop=(g == GROUPS - 1),
+                        )
+                gate = ring.tile([P, HALF], F32, name="gate")
+                nc.scalar.activation(gate[:], gate_acc[:], ACT.Sigmoid, bias=bg_t[:, c : c + 1])
+                result = ring.tile([P, HALF], F32, name="result")
+                is_last = h == 1 and c == N_TILES - 1
+                for cols in halves(HALF) if is_last else [slice(0, HALF)]:
+                    nc.vector.tensor_tensor(result[:, cols], y_acc[:, cols], gate[:, cols], ALU.mult)
+                    nc.sync.dma_start(out[n_cols, HALF * h + cols.start : HALF * h + cols.stop], result[:, cols])

@@ -30,8 +30,8 @@ LIST_COLS = PASS // 16
 N_TILES = N // P
 RUN = 4
 
-V_ROW = 0
-V2_ROW = K_PASSES * ROWS
+PLANE_ROW = (12, 0)
+FIRST_ROW = 12
 
 VECTOR_BANKS = (1, 3)
 SCALAR_PIECE = (GROUPS - 1, 1)
@@ -62,54 +62,55 @@ def tile_list_slate_candidate_profiles_kernel(
         tab_s = held([P, T // 4], I32, "tab_s")
         tab2_s = held([P, T2 // 4], I32, "tab2_s")
 
-        nc.vector.memset(tab2_s[:], 0)
-        nc.vector.memset(tab_s[:], 0)
+        nc.gpsimd.memset(tab2_s[:], 0)
+        nc.gpsimd.memset(tab_s[:], 0)
 
         def load_words(tile, words, a):
             nc.sync.dma_start(tile[:], words[a].rearrange("p n t -> p (n t)").bitcast(I32))
 
-        def load_scales(tile, scales, row):
-            for q in range(QUADRANTS):
-                first_row = QUAD * q + row
-                nc.sync.dma_start(
-                    tile[first_row : first_row + K_PASSES * ROWS, :],
-                    scales[:, ROWS * q : ROWS * (q + 1), :].bitcast(I32),
-                )
+        def load_scales(tile, scales):
+            n_rows = K_PASSES * QUADRANTS * ROWS
+            nc.sync.dma_start(
+                tile[FIRST_ROW : FIRST_ROW + n_rows, :], scales.rearrange("a q n -> (a q) n").bitcast(I32)
+            )
 
         nc.sync.dma_start(idx2[:], offs2)
         nc.sync.dma_start(idx[:], offs)
         rec_t = held([P, GROUPS, PACK], F32, "rec_t")
         nc.sync.dma_start(rec_t[:], rec.rearrange("(g p t) -> p g t", g=GROUPS, t=PACK))
-        load_scales(tab2_s, tab2_scales, V2_ROW)
+        bg_t = held([P, N_TILES], F32, "bg_t")
+        with nc.allow_non_contiguous_dma(reason="one bias value to a partition"):
+            nc.scalar.dma_start(bg_t[:], bg.rearrange("(c p) -> p c", p=P))
+        load_scales(tab2_s, tab2_scales)
+        load_scales(tab_s, tab_scales)
         load_words(tab2_w[0], tab2_words, 0)
-        load_scales(tab_s, tab_scales, V_ROW)
         load_words(tab_w[0], tab_words, 0)
         load_words(tab_w[1], tab_words, 1)
         load_words(tab2_w[1], tab2_words, 1)
 
         v_s_listed = held([P, S], U8, "v_s_listed")
-        v_s = held([P, S], U8, "v_s")
-        v2_s = held([P, S2], U8, "v2_s")
+        v2_s_listed = held([P, S2], U8, "v2_s_listed")
+        planes = held([P, S + S2], U8, "planes")
+        v_s = planes[:, 0:S]
+        v2_s = planes[:, S : S + S2]
         v2_w0 = held([P, S2], U32, "v2_w0")
 
-        nc.vector.tensor_copy(v2_s[:], tab2_s[:].bitcast(U8).indirect(idx2[:]))
-        nc.vector.tensor_copy(v2_w0[:], tab2_w[0][:].bitcast(U32).indirect(idx2[:]))
+        nc.vector.tensor_copy(v2_s_listed[:], tab2_s[:].bitcast(U8).indirect(idx2[:]))
         nc.vector.tensor_copy(v_s_listed[:], tab_s[:].bitcast(U8).indirect(idx[:]))
+        nc.vector.tensor_copy(v2_s.bitcast(I32), v2_s_listed[:].bitcast(I32))
         nc.vector.tensor_copy(
-            v_s[:].rearrange("p (g t m) -> p g t m", g=GROUPS, t=PACK),
+            v_s.rearrange("p (g t m) -> p g t m", g=GROUPS, t=PACK),
             v_s_listed[:].rearrange("p (g m t) -> p g t m", g=GROUPS, t=PACK),
         )
-
-        bg_t = held([P, N_TILES], F32, "bg_t", after="tab2_s")
-        with nc.allow_non_contiguous_dma(reason="one bias value to a partition"):
-            nc.sync.dma_start(bg_t[:], bg.rearrange("(c p) -> p c", p=P))
-        attr_s = held([P, GROUPS, N // 4], I32, "attr_s", after="v_s_listed")
-        nc.gpsimd.memset(attr_s[:], 0)
-        for q in range(QUADRANTS):
-            nc.sync.dma_start(
-                attr_s[QUAD * q : QUAD * q + ROWS, :, :],
-                attr_scales[:, ROWS * q : ROWS * (q + 1), :].bitcast(I32).rearrange("g s n -> s g n"),
-            )
+        for a in range(K_PASSES):
+            for q in range(QUADRANTS):
+                source = FIRST_ROW + ROWS * (QUADRANTS * a + q)
+                target = QUAD * q + PLANE_ROW[a]
+                if source != target:
+                    nc.scalar.dma_start(
+                        planes[target : target + ROWS, :].bitcast(I32), planes[source : source + ROWS, :].bitcast(I32)
+                    )
+        nc.vector.tensor_copy(v2_w0[:], tab2_w[0][:].bitcast(U32).indirect(idx2[:]))
 
         v_w = held([P, K_PASSES, GROUPS, PASS], U32, "v_w")
 
@@ -147,9 +148,9 @@ def tile_list_slate_candidate_profiles_kernel(
             nc.tensor.matmul_mx(
                 out=acc,
                 lhsT=v_w[:, a, g, P * t : P * (t + 1)].bitcast(FP8X4),
-                lhsT_scale=v_s[V_ROW + ROWS * a : P, m0 : m0 + P],
+                lhsT_scale=planes[PLANE_ROW[a] : P, m0 : m0 + P],
                 rhs=v2_w[a][:, j0 : j0 + width].bitcast(FP8X4),
-                rhs_scale=v2_s[V2_ROW + ROWS * a : P, j0 : j0 + width],
+                rhs_scale=planes[PLANE_ROW[a] : P, S + j0 : S + j0 + width],
                 start=(a == 0),
                 stop=(a == K_PASSES - 1),
             )
@@ -165,6 +166,13 @@ def tile_list_slate_candidate_profiles_kernel(
         for b in range(BANKS):
             score(first[b][:], b // PACK, b % PACK, 1, 0, HALF)
         gather_v2_last_pass(1)
+        attr_s = held([P, GROUPS, N // 4], I32, "attr_s", after="tab2_w1")
+        nc.gpsimd.memset(attr_s[:], 0)
+        for q in range(QUADRANTS):
+            nc.sync.dma_start(
+                attr_s[QUAD * q : QUAD * q + ROWS, :, :],
+                attr_scales[:, ROWS * q : ROWS * (q + 1), :].bitcast(I32).rearrange("g s n -> s g n"),
+            )
 
         z_rows = [held([P, PACK, HALF], BF16, "z_rows%d" % g) for g in range(GROUPS)]
         z_bf = [[held([P, HALF, PACK], BF16, "z_bf%d_%d" % (h, g)) for g in range(GROUPS)] for h in range(2)]

@@ -33,8 +33,9 @@ RUN = 4
 PLANE_ROW = (12, 0)
 FIRST_ROW = 12
 
-VECTOR_BANKS = (1, 3)
-SCALAR_PIECE = (GROUPS - 1, 1)
+SCALAR_GROUPS = ()
+WG_ON_GPSIMD = ()
+WG_PIECES = 2
 
 
 def tile_list_slate_candidate_profiles_kernel(
@@ -58,12 +59,12 @@ def tile_list_slate_candidate_profiles_kernel(
         idx = keep.tile([P, S // 16], U16, name="idx")
         idx2 = keep.tile([P, S2 // 16], U16, name="idx2")
         tab_w = [held([P, T], I32, "tab_w%d" % a) for a in range(K_PASSES)]
-        tab2_w = [held([P, T2], I32, "tab2_w%d" % a) for a in range(K_PASSES)]
+        tab2_w = [held([P, T2], I32, "tab2_w0")]
         tab_s = held([P, T // 4], I32, "tab_s")
         tab2_s = held([P, T2 // 4], I32, "tab2_s")
 
         nc.gpsimd.memset(tab2_s[:], 0)
-        nc.gpsimd.memset(tab_s[:], 0)
+        nc.vector.memset(tab_s[:], 0)
 
         def load_words(tile, words, a):
             nc.sync.dma_start(tile[:], words[a].rearrange("p n t -> p (n t)").bitcast(I32))
@@ -80,13 +81,12 @@ def tile_list_slate_candidate_profiles_kernel(
         nc.sync.dma_start(rec_t[:], rec.rearrange("(g p t) -> p g t", g=GROUPS, t=PACK))
         bg_t = held([P, N_TILES], F32, "bg_t")
         with nc.allow_non_contiguous_dma(reason="one bias value to a partition"):
-            nc.scalar.dma_start(bg_t[:], bg.rearrange("(c p) -> p c", p=P))
+            nc.sync.dma_start(bg_t[:], bg.rearrange("(c p) -> p c", p=P))
         load_scales(tab2_s, tab2_scales)
         load_scales(tab_s, tab_scales)
         load_words(tab2_w[0], tab2_words, 0)
         load_words(tab_w[0], tab_words, 0)
         load_words(tab_w[1], tab_words, 1)
-        load_words(tab2_w[1], tab2_words, 1)
 
         v_s_listed = held([P, S], U8, "v_s_listed")
         v2_s_listed = held([P, S2], U8, "v2_s_listed")
@@ -111,12 +111,14 @@ def tile_list_slate_candidate_profiles_kernel(
                         planes[target : target + ROWS, :].bitcast(I32), planes[source : source + ROWS, :].bitcast(I32)
                     )
         nc.vector.tensor_copy(v2_w0[:], tab2_w[0][:].bitcast(U32).indirect(idx2[:]))
+        tab2_w.append(held([P, T2], I32, "tab2_w1", after="tab2_w0"))
+        load_words(tab2_w[1], tab2_words, 1)
 
-        v_w = held([P, K_PASSES, GROUPS, PASS], U32, "v_w")
+        v_w = [[held([P, PASS], U32, "v_w%d_%d" % (a, g)) for g in range(GROUPS)] for a in range(K_PASSES)]
 
         def gather_v(a, g):
             nc.vector.tensor_copy(
-                v_w[:, a, g, :].rearrange("p (t m) -> p m t", t=PACK),
+                v_w[a][g][:].rearrange("p (t m) -> p m t", t=PACK),
                 tab_w[a][:].bitcast(U32).indirect(idx[:, LIST_COLS * g : LIST_COLS * (g + 1)]),
             )
 
@@ -138,35 +140,49 @@ def tile_list_slate_candidate_profiles_kernel(
                 tab2_w[1][:].bitcast(U32).indirect(idx2[:, LIST_COLS * h : LIST_COLS * (h + 1)]),
             )
 
-        rec_sign = held([P, GROUPS, PACK], F32, "rec_sign")
+        warm = held([P, 1], F32, "warm")
+        nc.scalar.activation(warm[:], rec_t[:, 0, 0:1], ACT.Sigmoid)
+        rec_sign = held([P, GROUPS, 2, 2], BF16, "rec_sign")
         rec_size = held([P, GROUPS, PACK], F32, "rec_size")
-        nc.scalar.activation(rec_sign[:], rec_t[:], ACT.Sign)
-        nc.scalar.activation(rec_size[:], rec_t[:], ACT.Abs)
+        if SCALAR_GROUPS:
+            nc.scalar.activation(rec_sign[:].rearrange("p g u e -> p g (u e)"), rec_t[:], ACT.Sign)
+            nc.scalar.activation(rec_size[:], rec_t[:], ACT.Abs)
 
-        def score(acc, g, t, a, j0, width):
+        def score(acc, g, t, a, j0, width, start, stop):
             m0 = PASS * g + P * t
             nc.tensor.matmul_mx(
                 out=acc,
-                lhsT=v_w[:, a, g, P * t : P * (t + 1)].bitcast(FP8X4),
+                lhsT=v_w[a][g][:, P * t : P * (t + 1)].bitcast(FP8X4),
                 lhsT_scale=planes[PLANE_ROW[a] : P, m0 : m0 + P],
                 rhs=v2_w[a][:, j0 : j0 + width].bitcast(FP8X4),
                 rhs_scale=planes[PLANE_ROW[a] : P, S + j0 : S + j0 + width],
-                start=(a == 0),
-                stop=(a == K_PASSES - 1),
+                start=start,
+                stop=stop,
             )
+
+        def fill(acc, h, b, a):
+            g, c = divmod(b, PACK)
+            if (h, g) in SCALAR_GROUPS:
+                score(acc[:], g, c, a, HALF * h, HALF, a == 0, a == K_PASSES - 1)
+            else:
+                for t in range(PACK):
+                    score(
+                        acc[:, P * t : P * (t + 1)], g, t, a, HALF * h + P * c, P,
+                        a == 0 and t == 0, a == K_PASSES - 1 and t == PACK - 1,
+                    )
 
         first = [bank(b, "first%d" % b) for b in range(BANKS)]
         for b in range(BANKS):
-            score(first[b][:], b // PACK, b % PACK, 0, 0, HALF)
+            fill(first[b], 0, b, 0)
         gather_v(1, 0)
-        gather_v2_last_pass(0)
         gather_v(1, 1)
         attr_w = held([P, GROUPS, 2 * N // 4], I32, "attr_w", after="tab_w1")
         nc.sync.dma_start(attr_w[:], attr_words.bitcast(I32).rearrange("g p n -> p g n"))
+        gather_v2_last_pass(0)
         for b in range(BANKS):
-            score(first[b][:], b // PACK, b % PACK, 1, 0, HALF)
+            fill(first[b], 0, b, 1)
         gather_v2_last_pass(1)
-        attr_s = held([P, GROUPS, N // 4], I32, "attr_s", after="tab2_w1")
+        attr_s = held([P, GROUPS, N // 4], I32, "attr_s", after="tab2_w0")
         nc.gpsimd.memset(attr_s[:], 0)
         for q in range(QUADRANTS):
             nc.sync.dma_start(
@@ -174,11 +190,11 @@ def tile_list_slate_candidate_profiles_kernel(
                 attr_scales[:, ROWS * q : ROWS * (q + 1), :].bitcast(I32).rearrange("g s n -> s g n"),
             )
 
-        z_rows = [held([P, PACK, HALF], BF16, "z_rows%d" % g) for g in range(GROUPS)]
+        z_pairs = [[held([P, 2, HALF, 2], BF16, "z_pairs%d_%d" % (h, g)) for g in range(GROUPS)] for h in range(2)]
         z_bf = [[held([P, HALF, PACK], BF16, "z_bf%d_%d" % (h, g)) for g in range(GROUPS)] for h in range(2)]
         z_w = [[held([P, HALF], U32, "z_w%d_%d" % (h, g)) for g in range(GROUPS)] for h in range(2)]
         z_s = [[held([P, HALF], U8, "z_s%d_%d" % (h, g)) for g in range(GROUPS)] for h in range(2)]
-        wg_bf = held([P, GROUPS, N, PACK], BF16, "wg_bf")
+        wg_bf = [held([P, N, PACK], BF16, "wg_bf%d" % g) for g in range(GROUPS)]
         wg_w = [held([P, N], U32, "wg_w%d" % g) for g in range(GROUPS)]
         wg_s = [held([P, N], U8, "wg_s%d" % g) for g in range(GROUPS)]
 
@@ -187,57 +203,59 @@ def tile_list_slate_candidate_profiles_kernel(
                 out=words[:].bitcast(FP8X4), scales=scales[:], in_=side_by_side.rearrange("p w t -> p (w t)")
             )
 
-        def interleave(copy, side_by_side, rows):
-            copy(
-                side_by_side.rearrange("p (c r) t -> p c t r", r=RUN),
-                rows.rearrange("p t (c r) -> p c t r", r=RUN),
-            )
+        def cast_wg(g):
+            for piece in range(WG_PIECES):
+                cols = slice(N // WG_PIECES * piece, N // WG_PIECES * (piece + 1))
+                side_by_side = wg_bf[g][:, cols, :].rearrange("p (c r) t -> p c t r", r=RUN)
+                rows = wg_rows[:, g, :, cols].rearrange("p t (c r) -> p c t r", r=RUN)
+                if g in WG_ON_GPSIMD:
+                    nc.gpsimd.tensor_scalar(side_by_side, rows, 1.0, 0.0, ALU.mult, ALU.add)
+                else:
+                    nc.scalar.copy(side_by_side, rows)
 
-        def empty_first(b):
-            g, t = divmod(b, PACK)
-            if b in VECTOR_BANKS:
-                nc.vector.tensor_scalar(
-                    z_rows[g][:, t, :], first[b][:], 0.0, rec_t[:, g, t : t + 1], ALU.max, ALU.mult
+        def empty(acc, h, b):
+            g, c = divmod(b, PACK)
+            if (h, g) in SCALAR_GROUPS:
+                nc.scalar.activation(
+                    z_pairs[h][g][:, c // 2, :, c % 2], acc[:], ACT.Relu, scale=rec_size[:, g, c : c + 1]
                 )
             else:
-                nc.scalar.activation(z_rows[g][:, t, :], first[b][:], ACT.Relu, scale=rec_size[:, g, t : t + 1])
-
-        second = []
-        for b in range(BANKS):
-            empty_first(b)
-            g, c = divmod(b, PACK)
-            acc = bank(b, "second%d" % b)
-            second.append(acc)
-            for t in range(PACK):
-                for a in range(K_PASSES):
-                    score(acc[:, P * t : P * (t + 1)], g, t, a, HALF + P * c, P)
-
-        for g in range(GROUPS):
-            for t in range(PACK):
-                if PACK * g + t not in VECTOR_BANKS:
-                    row = z_rows[g][:, t, :]
-                    nc.vector.tensor_scalar(row, row, rec_sign[:, g, t : t + 1], None, ALU.mult)
-            for piece, cols in enumerate(halves(HALF)):
-                copy = nc.scalar.copy if (g, piece) == SCALAR_PIECE else nc.vector.tensor_copy
-                interleave(copy, z_bf[0][g][:, cols, :], z_rows[g][:, :, cols])
-            quantize(z_w[0][g], z_s[0][g], z_bf[0][g][:])
-
-        for g in range(GROUPS):
-            for cols in halves(N):
-                interleave(nc.scalar.copy, wg_bf[:, g, cols, :], wg_rows[:, g, :, cols])
-            quantize(wg_w[g], wg_s[g], wg_bf[:, g, :, :])
-
-        for g in range(GROUPS):
-            for c in range(PACK):
                 nc.vector.scalar_tensor_tensor(
-                    z_bf[1][g][:, P * c : P * (c + 1), :],
-                    second[PACK * g + c][:].rearrange("p (t j) -> p j t", t=PACK),
+                    z_bf[h][g][:, P * c : P * (c + 1), :],
+                    acc[:].rearrange("p (t j) -> p j t", t=PACK),
                     0.0,
                     rec_t[:, g : g + 1, :].to_broadcast([P, P, PACK]),
                     ALU.max,
                     ALU.mult,
                 )
-            quantize(z_w[1][g], z_s[1][g], z_bf[1][g][:])
+
+        def finish(h):
+            for g in range(GROUPS):
+                if (h, g) in SCALAR_GROUPS:
+                    nc.vector.tensor_tensor(
+                        z_bf[h][g][:].rearrange("p j (u e) -> p j u e", e=2),
+                        z_pairs[h][g][:].rearrange("p u j e -> p j u e"),
+                        rec_sign[:, g : g + 1, :, :].to_broadcast([P, HALF, 2, 2]),
+                        ALU.mult,
+                    )
+            for g in sorted(range(GROUPS), key=lambda g: (h, g) in SCALAR_GROUPS):
+                quantize(z_w[h][g], z_s[h][g], z_bf[h][g][:])
+
+        second = []
+        for b in range(BANKS):
+            empty(first[b], 0, b)
+            acc = bank(b, "second%d" % b)
+            second.append(acc)
+            for a in range(K_PASSES):
+                fill(acc, 1, b, a)
+        finish(0)
+        cast_wg(0)
+        cast_wg(1)
+        quantize(wg_w[0], wg_s[0], wg_bf[0][:])
+        for b in range(BANKS):
+            empty(second[b], 1, b)
+        quantize(wg_w[1], wg_s[1], wg_bf[1][:])
+        finish(1)
 
         attr_operand = [
             (attr_w[:, g, :].bitcast(U8).bitcast(FP4X4), attr_s[:, g, :].bitcast(U8)) for g in range(GROUPS)

@@ -33,9 +33,11 @@ RUN = 4
 PLANE_ROW = (12, 0)
 FIRST_ROW = 12
 
-SCALAR_GROUPS = ()
+SCALAR_GROUPS = ((1, 0),)
 WG_ON_GPSIMD = ()
 WG_PIECES = 2
+PLAIN_PASSES = ()
+LATE_Z = (1, 0)
 
 
 def tile_list_slate_candidate_profiles_kernel(
@@ -59,7 +61,7 @@ def tile_list_slate_candidate_profiles_kernel(
         idx = keep.tile([P, S // 16], U16, name="idx")
         idx2 = keep.tile([P, S2 // 16], U16, name="idx2")
         tab_w = [held([P, T], I32, "tab_w%d" % a) for a in range(K_PASSES)]
-        tab2_w = [held([P, T2], I32, "tab2_w0")]
+        tab2_w = [held([P, T2], I32, "tab2_w%d" % a) for a in range(K_PASSES)]
         tab_s = held([P, T // 4], I32, "tab_s")
         tab2_s = held([P, T2 // 4], I32, "tab2_s")
 
@@ -79,13 +81,11 @@ def tile_list_slate_candidate_profiles_kernel(
         nc.sync.dma_start(idx[:], offs)
         rec_t = held([P, GROUPS, PACK], F32, "rec_t")
         nc.sync.dma_start(rec_t[:], rec.rearrange("(g p t) -> p g t", g=GROUPS, t=PACK))
-        bg_t = held([P, N_TILES], F32, "bg_t")
-        with nc.allow_non_contiguous_dma(reason="one bias value to a partition"):
-            nc.sync.dma_start(bg_t[:], bg.rearrange("(c p) -> p c", p=P))
         load_scales(tab2_s, tab2_scales)
         load_scales(tab_s, tab_scales)
         load_words(tab2_w[0], tab2_words, 0)
         load_words(tab_w[0], tab_words, 0)
+        load_words(tab2_w[1], tab2_words, 1)
         load_words(tab_w[1], tab_words, 1)
 
         v_s_listed = held([P, S], U8, "v_s_listed")
@@ -111,16 +111,23 @@ def tile_list_slate_candidate_profiles_kernel(
                         planes[target : target + ROWS, :].bitcast(I32), planes[source : source + ROWS, :].bitcast(I32)
                     )
         nc.vector.tensor_copy(v2_w0[:], tab2_w[0][:].bitcast(U32).indirect(idx2[:]))
-        tab2_w.append(held([P, T2], I32, "tab2_w1", after="tab2_w0"))
-        load_words(tab2_w[1], tab2_words, 1)
+        bg_t = held([P, N_TILES], F32, "bg_t", after="tab2_w0")
+        with nc.allow_non_contiguous_dma(reason="one bias value to a partition"):
+            nc.sync.dma_start(bg_t[:], bg.rearrange("(c p) -> p c", p=P))
 
         v_w = [[held([P, PASS], U32, "v_w%d_%d" % (a, g)) for g in range(GROUPS)] for a in range(K_PASSES)]
 
         def gather_v(a, g):
-            nc.vector.tensor_copy(
-                v_w[a][g][:].rearrange("p (t m) -> p m t", t=PACK),
-                tab_w[a][:].bitcast(U32).indirect(idx[:, LIST_COLS * g : LIST_COLS * (g + 1)]),
-            )
+            window = tab_w[a][:].bitcast(U32).indirect(idx[:, LIST_COLS * g : LIST_COLS * (g + 1)])
+            if a in PLAIN_PASSES:
+                listed = held([P, PASS], U32, "listed%d_%d" % (a, g))
+                nc.vector.tensor_copy(listed[:], window)
+                nc.vector.tensor_copy(
+                    v_w[a][g][:].rearrange("p (t c r) -> p c t r", t=PACK, r=RUN),
+                    listed[:].rearrange("p (c r t) -> p c t r", t=PACK, r=RUN),
+                )
+            else:
+                nc.vector.tensor_copy(v_w[a][g][:].rearrange("p (t m) -> p m t", t=PACK), window)
 
         for g in range(GROUPS):
             gather_v(0, g)
@@ -133,12 +140,6 @@ def tile_list_slate_candidate_profiles_kernel(
 
         v2_w1 = held([P, S2], U32, "v2_w1")
         v2_w = [v2_w0, v2_w1]
-
-        def gather_v2_last_pass(h):
-            nc.vector.tensor_copy(
-                v2_w1[:, HALF * h : HALF * (h + 1)],
-                tab2_w[1][:].bitcast(U32).indirect(idx2[:, LIST_COLS * h : LIST_COLS * (h + 1)]),
-            )
 
         warm = held([P, 1], F32, "warm")
         nc.scalar.activation(warm[:], rec_t[:, 0, 0:1], ACT.Sigmoid)
@@ -174,15 +175,14 @@ def tile_list_slate_candidate_profiles_kernel(
         first = [bank(b, "first%d" % b) for b in range(BANKS)]
         for b in range(BANKS):
             fill(first[b], 0, b, 0)
-        gather_v(1, 0)
-        gather_v(1, 1)
-        attr_w = held([P, GROUPS, 2 * N // 4], I32, "attr_w", after="tab_w1")
+        nc.vector.tensor_copy(v2_w1[:], tab2_w[1][:].bitcast(U32).indirect(idx2[:]))
+        attr_w = held([P, GROUPS, 2 * N // 4], I32, "attr_w", after="tab2_w1")
         nc.sync.dma_start(attr_w[:], attr_words.bitcast(I32).rearrange("g p n -> p g n"))
-        gather_v2_last_pass(0)
-        for b in range(BANKS):
-            fill(first[b], 0, b, 1)
-        gather_v2_last_pass(1)
-        attr_s = held([P, GROUPS, N // 4], I32, "attr_s", after="tab2_w0")
+        for g in range(GROUPS):
+            gather_v(1, g)
+            for b in range(PACK * g, PACK * (g + 1)):
+                fill(first[b], 0, b, 1)
+        attr_s = held([P, GROUPS, N // 4], I32, "attr_s", after="tab_w1")
         nc.gpsimd.memset(attr_s[:], 0)
         for q in range(QUADRANTS):
             nc.sync.dma_start(
@@ -191,7 +191,10 @@ def tile_list_slate_candidate_profiles_kernel(
             )
 
         z_pairs = [[held([P, 2, HALF, 2], BF16, "z_pairs%d_%d" % (h, g)) for g in range(GROUPS)] for h in range(2)]
-        z_bf = [[held([P, HALF, PACK], BF16, "z_bf%d_%d" % (h, g)) for g in range(GROUPS)] for h in range(2)]
+        z_bf = [
+            [held([P, HALF, PACK], BF16, "z_bf%d_%d" % (h, g)) if (h, g) != LATE_Z else None for g in range(GROUPS)]
+            for h in range(2)
+        ]
         z_w = [[held([P, HALF], U32, "z_w%d_%d" % (h, g)) for g in range(GROUPS)] for h in range(2)]
         z_s = [[held([P, HALF], U8, "z_s%d_%d" % (h, g)) for g in range(GROUPS)] for h in range(2)]
         wg_bf = [held([P, N, PACK], BF16, "wg_bf%d" % g) for g in range(GROUPS)]
@@ -209,7 +212,9 @@ def tile_list_slate_candidate_profiles_kernel(
                 side_by_side = wg_bf[g][:, cols, :].rearrange("p (c r) t -> p c t r", r=RUN)
                 rows = wg_rows[:, g, :, cols].rearrange("p t (c r) -> p c t r", r=RUN)
                 if g in WG_ON_GPSIMD:
-                    nc.gpsimd.tensor_scalar(side_by_side, rows, 1.0, 0.0, ALU.mult, ALU.add)
+                    nc.gpsimd.tensor_scalar(
+                        wg_bf[g][:, cols, :], wg_rows[:, g, :, cols].rearrange("p t w -> p w t"), 1.0, 0.0, ALU.mult, ALU.add
+                    )
                 else:
                     nc.scalar.copy(side_by_side, rows)
 
@@ -252,36 +257,46 @@ def tile_list_slate_candidate_profiles_kernel(
         cast_wg(0)
         cast_wg(1)
         quantize(wg_w[0], wg_s[0], wg_bf[0][:])
+        quantize(wg_w[1], wg_s[1], wg_bf[1][:])
         for b in range(BANKS):
             empty(second[b], 1, b)
-        quantize(wg_w[1], wg_s[1], wg_bf[1][:])
+        if LATE_Z:
+            z_bf[1][0] = held([P, HALF, PACK], BF16, "z_bf1_0", after="wg_bf1")
         finish(1)
 
         attr_operand = [
             (attr_w[:, g, :].bitcast(U8).bitcast(FP4X4), attr_s[:, g, :].bitcast(U8)) for g in range(GROUPS)
         ]
         wg_operand = [(wg_w[g][:].bitcast(FP8X4), wg_s[g][:]) for g in range(GROUPS)]
+
+        def profile(acc, operand, h, c):
+            for g, (words, scales) in enumerate(operand):
+                nc.tensor.matmul_mx(
+                    out=acc[:],
+                    lhsT=words[:, P * c : P * (c + 1)],
+                    lhsT_scale=scales[:, P * c : P * (c + 1)],
+                    rhs=z_w[h][g][:].bitcast(FP8X4),
+                    rhs_scale=z_s[h][g][:],
+                    start=(g == 0),
+                    stop=(g == GROUPS - 1),
+                )
+
         for h in range(2):
+            y_acc = [bank(c, "y%d_%d" % (h, c)) for c in range(N_TILES)]
+            if h == 0:
+                for c in range(N_TILES):
+                    profile(y_acc[c], attr_operand, h, c)
             for c in range(N_TILES):
-                n_cols = slice(P * c, P * (c + 1))
-                y_acc = bank(c, "y%d_%d" % (h, c))
                 gate_acc = bank(N_TILES + c, "gate%d_%d" % (h, c))
-                sums = [(y_acc, attr_operand), (gate_acc, wg_operand)]
-                for acc, operand in sums if h == 0 else reversed(sums):
-                    for g, (words, scales) in enumerate(operand):
-                        nc.tensor.matmul_mx(
-                            out=acc[:],
-                            lhsT=words[:, n_cols],
-                            lhsT_scale=scales[:, n_cols],
-                            rhs=z_w[h][g][:].bitcast(FP8X4),
-                            rhs_scale=z_s[h][g][:],
-                            start=(g == 0),
-                            stop=(g == GROUPS - 1),
-                        )
+                profile(gate_acc, wg_operand, h, c)
+                if h == 1:
+                    profile(y_acc[c], attr_operand, h, c)
                 gate = ring.tile([P, HALF], F32, name="gate")
                 nc.scalar.activation(gate[:], gate_acc[:], ACT.Sigmoid, bias=bg_t[:, c : c + 1])
                 result = ring.tile([P, HALF], F32, name="result")
                 is_last = h == 1 and c == N_TILES - 1
                 for cols in halves(HALF) if is_last else [slice(0, HALF)]:
-                    nc.vector.tensor_tensor(result[:, cols], y_acc[:, cols], gate[:, cols], ALU.mult)
-                    nc.sync.dma_start(out[n_cols, HALF * h + cols.start : HALF * h + cols.stop], result[:, cols])
+                    nc.vector.tensor_tensor(result[:, cols], y_acc[c][:, cols], gate[:, cols], ALU.mult)
+                    nc.sync.dma_start(
+                        out[P * c : P * (c + 1), HALF * h + cols.start : HALF * h + cols.stop], result[:, cols]
+                    )

@@ -31,7 +31,7 @@ N_TILES = N // P
 RUN = 4
 
 PLANE_ROW = (12, 0)
-FIRST_ROW = 12
+FIRST_ROW = 96
 
 SCALAR_GROUPS = ((1, 0),)
 WG_ON_GPSIMD = ()
@@ -65,8 +65,8 @@ def tile_list_slate_candidate_profiles_kernel(
         tab_s = held([P, T // 4], I32, "tab_s")
         tab2_s = held([P, T2 // 4], I32, "tab2_s")
 
-        nc.gpsimd.memset(tab2_s[:], 0)
-        nc.vector.memset(tab_s[:], 0)
+        nc.vector.memset(tab2_s[0:FIRST_ROW, :], 0)
+        nc.vector.memset(tab_s[0:FIRST_ROW, :], 0)
 
         def load_words(tile, words, a):
             nc.sync.dma_start(tile[:], words[a].rearrange("p n t -> p (n t)").bitcast(I32))
@@ -77,12 +77,12 @@ def tile_list_slate_candidate_profiles_kernel(
                 tile[FIRST_ROW : FIRST_ROW + n_rows, :], scales.rearrange("a q n -> (a q) n").bitcast(I32)
             )
 
+        load_scales(tab2_s, tab2_scales)
         nc.sync.dma_start(idx2[:], offs2)
+        load_scales(tab_s, tab_scales)
         nc.sync.dma_start(idx[:], offs)
         rec_t = held([P, GROUPS, PACK], F32, "rec_t")
         nc.sync.dma_start(rec_t[:], rec.rearrange("(g p t) -> p g t", g=GROUPS, t=PACK))
-        load_scales(tab2_s, tab2_scales)
-        load_scales(tab_s, tab_scales)
         load_words(tab2_w[0], tab2_words, 0)
         load_words(tab_w[0], tab_words, 0)
         load_words(tab2_w[1], tab2_words, 1)
@@ -90,9 +90,10 @@ def tile_list_slate_candidate_profiles_kernel(
 
         v_s_listed = held([P, S], U8, "v_s_listed")
         v2_s_listed = held([P, S2], U8, "v2_s_listed")
-        planes = held([P, S + S2], U8, "planes")
-        v_s = planes[:, 0:S]
-        v2_s = planes[:, S : S + S2]
+        planes = [held([P, S + S2], U8, "planes%d" % a) for a in range(K_PASSES)]
+        nc.gpsimd.memset(planes[1][:].bitcast(I32), 0)
+        v_s = planes[0][:, 0:S]
+        v2_s = planes[0][:, S : S + S2]
         v2_w0 = held([P, S2], U32, "v2_w0")
 
         nc.vector.tensor_copy(v2_s_listed[:], tab2_s[:].bitcast(U8).indirect(idx2[:]))
@@ -102,14 +103,17 @@ def tile_list_slate_candidate_profiles_kernel(
             v_s.rearrange("p (g t m) -> p g t m", g=GROUPS, t=PACK),
             v_s_listed[:].rearrange("p (g m t) -> p g t m", g=GROUPS, t=PACK),
         )
-        for a in range(K_PASSES):
-            for q in range(QUADRANTS):
-                source = FIRST_ROW + ROWS * (QUADRANTS * a + q)
-                target = QUAD * q + PLANE_ROW[a]
-                if source != target:
-                    nc.scalar.dma_start(
-                        planes[target : target + ROWS, :].bitcast(I32), planes[source : source + ROWS, :].bitcast(I32)
-                    )
+        for q in range(QUADRANTS - 1):
+            source = FIRST_ROW + ROWS * q
+            target = QUAD * q + PLANE_ROW[0]
+            nc.scalar.dma_start(
+                planes[0][target : target + ROWS, :].bitcast(I32), planes[0][source : source + ROWS, :].bitcast(I32)
+            )
+        for s in range(ROWS):
+            source = FIRST_ROW + ROWS * QUADRANTS + s
+            nc.sync.dma_start(
+                planes[1][PLANE_ROW[1] + s : P : QUAD, :].bitcast(I32), planes[0][source:P:ROWS, :].bitcast(I32)
+            )
         nc.vector.tensor_copy(v2_w0[:], tab2_w[0][:].bitcast(U32).indirect(idx2[:]))
         bg_t = held([P, N_TILES], F32, "bg_t", after="tab2_w0")
         with nc.allow_non_contiguous_dma(reason="one bias value to a partition"):
@@ -154,9 +158,9 @@ def tile_list_slate_candidate_profiles_kernel(
             nc.tensor.matmul_mx(
                 out=acc,
                 lhsT=v_w[a][g][:, P * t : P * (t + 1)].bitcast(FP8X4),
-                lhsT_scale=planes[PLANE_ROW[a] : P, m0 : m0 + P],
+                lhsT_scale=planes[a][PLANE_ROW[a] : P, m0 : m0 + P],
                 rhs=v2_w[a][:, j0 : j0 + width].bitcast(FP8X4),
-                rhs_scale=planes[PLANE_ROW[a] : P, S + j0 : S + j0 + width],
+                rhs_scale=planes[a][PLANE_ROW[a] : P, S + j0 : S + j0 + width],
                 start=start,
                 stop=stop,
             )

@@ -60,7 +60,7 @@ def tile_list_slate_candidate_profiles_kernel(
 
         idx = keep.tile([P, S // 16], U16, name="idx")
         idx2 = keep.tile([P, S2 // 16], U16, name="idx2")
-        tab_w = [held([P, T], I32, "tab_w%d" % a) for a in range(K_PASSES)]
+        tab_w = [held([P, T], I32, "tab_w0")]
         tab2_w = [held([P, T2], I32, "tab2_w%d" % a) for a in range(K_PASSES)]
         tab_s = held([P, T // 4], I32, "tab_s")
         tab2_s = held([P, T2 // 4], I32, "tab2_s")
@@ -84,9 +84,8 @@ def tile_list_slate_candidate_profiles_kernel(
         rec_t = held([P, GROUPS, PACK], F32, "rec_t")
         nc.sync.dma_start(rec_t[:], rec.rearrange("(g p t) -> p g t", g=GROUPS, t=PACK))
         load_words(tab2_w[0], tab2_words, 0)
-        load_words(tab_w[0], tab_words, 0)
         load_words(tab2_w[1], tab2_words, 1)
-        load_words(tab_w[1], tab_words, 1)
+        load_words(tab_w[0], tab_words, 0)
 
         v_s_listed = held([P, S], U8, "v_s_listed")
         v2_s_listed = held([P, S2], U8, "v2_s_listed")
@@ -106,9 +105,11 @@ def tile_list_slate_candidate_profiles_kernel(
         for q in range(QUADRANTS - 1):
             source = FIRST_ROW + ROWS * q
             target = QUAD * q + PLANE_ROW[0]
-            nc.scalar.dma_start(
+            nc.sync.dma_start(
                 planes[0][target : target + ROWS, :].bitcast(I32), planes[0][source : source + ROWS, :].bitcast(I32)
             )
+        tab_w.append(held([P, T], I32, "tab_w1", after="v_s_listed"))
+        load_words(tab_w[1], tab_words, 1)
         for s in range(ROWS):
             source = FIRST_ROW + ROWS * QUADRANTS + s
             nc.sync.dma_start(
@@ -133,17 +134,20 @@ def tile_list_slate_candidate_profiles_kernel(
             else:
                 nc.vector.tensor_copy(v_w[a][g][:].rearrange("p (t m) -> p m t", t=PACK), window)
 
-        for g in range(GROUPS):
-            gather_v(0, g)
-
-        wg_rows = held([P, GROUPS, PACK, N], F32, "wg_rows", after="tab_w0")
+        v2_w1 = held([P, S2], U32, "v2_w1")
+        v2_w = [v2_w0, v2_w1]
+        nc.vector.tensor_copy(v2_w1[:], tab2_w[1][:].bitcast(U32).indirect(idx2[:]))
+        wg_rows = held([P, GROUPS, PACK, N], F32, "wg_rows", after="tab2_w1")
         for g in range(GROUPS):
             nc.sync.dma_start(
                 wg_rows[:, g, :, :], wg[PASS * g : PASS * (g + 1), :].rearrange("(p t) n -> p t n", t=PACK)
             )
 
-        v2_w1 = held([P, S2], U32, "v2_w1")
-        v2_w = [v2_w0, v2_w1]
+        for g in range(GROUPS):
+            gather_v(0, g)
+        attr_w = held([P, GROUPS, 2 * N // 4], I32, "attr_w", after="tab_w0")
+        nc.sync.dma_start(attr_w[:], attr_words.bitcast(I32).rearrange("g p n -> p g n"))
+
 
         warm = held([P, 1], F32, "warm")
         nc.scalar.activation(warm[:], rec_t[:, 0, 0:1], ACT.Sigmoid)
@@ -179,14 +183,11 @@ def tile_list_slate_candidate_profiles_kernel(
         first = [bank(b, "first%d" % b) for b in range(BANKS)]
         for b in range(BANKS):
             fill(first[b], 0, b, 0)
-        nc.vector.tensor_copy(v2_w1[:], tab2_w[1][:].bitcast(U32).indirect(idx2[:]))
-        attr_w = held([P, GROUPS, 2 * N // 4], I32, "attr_w", after="tab2_w1")
-        nc.sync.dma_start(attr_w[:], attr_words.bitcast(I32).rearrange("g p n -> p g n"))
         for g in range(GROUPS):
             gather_v(1, g)
             for b in range(PACK * g, PACK * (g + 1)):
                 fill(first[b], 0, b, 1)
-        attr_s = held([P, GROUPS, N // 4], I32, "attr_s", after="tab_w1")
+        attr_s = held([P, GROUPS, N // 4], I32, "attr_s", after="v_s_listed")
         nc.gpsimd.memset(attr_s[:], 0)
         for q in range(QUADRANTS):
             nc.sync.dma_start(

@@ -37,6 +37,7 @@ SCALAR_GROUPS = ((1, 0),)
 WG_ON_GPSIMD = ()
 WG_PIECES = 2
 PLAIN_PASSES = ()
+GPSIMD_TILES = 0
 LATE_Z = (1, 0)
 
 
@@ -149,8 +150,6 @@ def tile_list_slate_candidate_profiles_kernel(
         nc.sync.dma_start(attr_w[:], attr_words.bitcast(I32).rearrange("g p n -> p g n"))
 
 
-        warm = held([P, 1], F32, "warm")
-        nc.scalar.activation(warm[:], rec_t[:, 0, 0:1], ACT.Sigmoid)
         rec_sign = held([P, GROUPS, 2, 2], BF16, "rec_sign")
         rec_size = held([P, GROUPS, PACK], F32, "rec_size")
         if SCALAR_GROUPS:
@@ -274,34 +273,53 @@ def tile_list_slate_candidate_profiles_kernel(
         ]
         wg_operand = [(wg_w[g][:].bitcast(FP8X4), wg_s[g][:]) for g in range(GROUPS)]
 
-        def profile(acc, operand, h, c):
-            for g, (words, scales) in enumerate(operand):
-                nc.tensor.matmul_mx(
-                    out=acc[:],
-                    lhsT=words[:, P * c : P * (c + 1)],
-                    lhsT_scale=scales[:, P * c : P * (c + 1)],
-                    rhs=z_w[h][g][:].bitcast(FP8X4),
-                    rhs_scale=z_s[h][g][:],
-                    start=(g == 0),
-                    stop=(g == GROUPS - 1),
+        def profile(acc, operand, h, c, g, first_group):
+            words, scales = operand[g]
+            nc.tensor.matmul_mx(
+                out=acc[:],
+                lhsT=words[:, P * c : P * (c + 1)],
+                lhsT_scale=scales[:, P * c : P * (c + 1)],
+                rhs=z_w[h][g][:].bitcast(FP8X4),
+                rhs_scale=z_s[h][g][:],
+                start=(g == first_group),
+                stop=(g != first_group),
+            )
+
+        def finish_tile(h, c, y, gate_acc, multiply):
+            gate = ring.tile([P, HALF], F32, name="gate")
+            nc.scalar.activation(gate[:], gate_acc[:], ACT.Sigmoid, bias=bg_t[:, c : c + 1])
+            result = ring.tile([P, HALF], F32, name="result")
+            is_last = h == 1 and c == N_TILES - 1
+            for cols in halves(HALF) if is_last else [slice(0, HALF)]:
+                multiply(result[:, cols], y[:, cols], gate[:, cols], ALU.mult)
+                nc.sync.dma_start(
+                    out[P * c : P * (c + 1), HALF * h + cols.start : HALF * h + cols.stop], result[:, cols]
                 )
 
-        for h in range(2):
-            y_acc = [bank(c, "y%d_%d" % (h, c)) for c in range(N_TILES)]
-            if h == 0:
-                for c in range(N_TILES):
-                    profile(y_acc[c], attr_operand, h, c)
-            for c in range(N_TILES):
-                gate_acc = bank(N_TILES + c, "gate%d_%d" % (h, c))
-                profile(gate_acc, wg_operand, h, c)
-                if h == 1:
-                    profile(y_acc[c], attr_operand, h, c)
-                gate = ring.tile([P, HALF], F32, name="gate")
-                nc.scalar.activation(gate[:], gate_acc[:], ACT.Sigmoid, bias=bg_t[:, c : c + 1])
-                result = ring.tile([P, HALF], F32, name="result")
-                is_last = h == 1 and c == N_TILES - 1
-                for cols in halves(HALF) if is_last else [slice(0, HALF)]:
-                    nc.vector.tensor_tensor(result[:, cols], y_acc[c][:, cols], gate[:, cols], ALU.mult)
-                    nc.sync.dma_start(
-                        out[P * c : P * (c + 1), HALF * h + cols.start : HALF * h + cols.stop], result[:, cols]
-                    )
+        y_acc = [bank(c, "y0_%d" % c) for c in range(N_TILES)]
+        gate_acc = [bank(N_TILES + c, "gate0_%d" % c) for c in range(N_TILES)]
+        for c in range(N_TILES):
+            for g in range(GROUPS):
+                profile(y_acc[c], attr_operand, 0, c, g, 0)
+        for c in range(N_TILES):
+            for g in range(GROUPS):
+                profile(gate_acc[c], wg_operand, 0, c, g, 0)
+        y_out = [held([P, HALF], F32, "y_out%d" % c) for c in range(GPSIMD_TILES)]
+        for c in range(GPSIMD_TILES):
+            nc.scalar.copy(y_out[c][:], y_acc[c][:])
+        for c in range(N_TILES):
+            if c < GPSIMD_TILES:
+                finish_tile(0, c, y_out[c], gate_acc[c], nc.gpsimd.tensor_tensor)
+            else:
+                finish_tile(0, c, y_acc[c], gate_acc[c], nc.vector.tensor_tensor)
+
+        y_acc = [bank(c, "y1_%d" % c) for c in range(N_TILES)]
+        gate_acc = [bank(N_TILES + c, "gate1_%d" % c) for c in range(N_TILES)]
+        for c in range(N_TILES + 1):
+            if c < N_TILES:
+                for g in (1, 0):
+                    profile(gate_acc[c], wg_operand, 1, c, g, 1)
+            if c > 0:
+                for g in (1, 0):
+                    profile(y_acc[c - 1], attr_operand, 1, c - 1, g, 1)
+                finish_tile(1, c - 1, y_acc[c - 1], gate_acc[c - 1], nc.vector.tensor_tensor)

@@ -30,15 +30,10 @@ LIST_COLS = PASS // 16
 N_TILES = N // P
 RUN = 4
 
+FIRST_ROW = P - QUAD
 PLANE_ROW = (12, 0)
-FIRST_ROW = 96
 
-SCALAR_GROUPS = ((1, 0),)
-WG_ON_GPSIMD = ()
-WG_PIECES = 2
-PLAIN_PASSES = ()
-GPSIMD_TILES = 0
-LATE_Z = (1, 0)
+SCALAR_HALF, SCALAR_GROUP = 1, 0
 
 
 def tile_list_slate_candidate_profiles_kernel(
@@ -61,7 +56,7 @@ def tile_list_slate_candidate_profiles_kernel(
 
         idx = keep.tile([P, S // 16], U16, name="idx")
         idx2 = keep.tile([P, S2 // 16], U16, name="idx2")
-        tab_w = [held([P, T], I32, "tab_w0")]
+        tab_w0 = held([P, T], I32, "tab_w0")
         tab2_w = [held([P, T2], I32, "tab2_w%d" % a) for a in range(K_PASSES)]
         tab_s = held([P, T // 4], I32, "tab_s")
         tab2_s = held([P, T2 // 4], I32, "tab2_s")
@@ -73,10 +68,7 @@ def tile_list_slate_candidate_profiles_kernel(
             nc.sync.dma_start(tile[:], words[a].rearrange("p n t -> p (n t)").bitcast(I32))
 
         def load_scales(tile, scales):
-            n_rows = K_PASSES * QUADRANTS * ROWS
-            nc.sync.dma_start(
-                tile[FIRST_ROW : FIRST_ROW + n_rows, :], scales.rearrange("a q n -> (a q) n").bitcast(I32)
-            )
+            nc.sync.dma_start(tile[FIRST_ROW:P, :], scales.rearrange("a q n -> (a q) n").bitcast(I32))
 
         load_scales(tab2_s, tab2_scales)
         nc.sync.dma_start(idx2[:], offs2)
@@ -86,21 +78,18 @@ def tile_list_slate_candidate_profiles_kernel(
         nc.sync.dma_start(rec_t[:], rec.rearrange("(g p t) -> p g t", g=GROUPS, t=PACK))
         load_words(tab2_w[0], tab2_words, 0)
         load_words(tab2_w[1], tab2_words, 1)
-        load_words(tab_w[0], tab_words, 0)
+        load_words(tab_w0, tab_words, 0)
 
         v_s_listed = held([P, S], U8, "v_s_listed")
         v2_s_listed = held([P, S2], U8, "v2_s_listed")
         planes = [held([P, S + S2], U8, "planes%d" % a) for a in range(K_PASSES)]
         nc.gpsimd.memset(planes[1][:].bitcast(I32), 0)
-        v_s = planes[0][:, 0:S]
-        v2_s = planes[0][:, S : S + S2]
-        v2_w0 = held([P, S2], U32, "v2_w0")
 
         nc.vector.tensor_copy(v2_s_listed[:], tab2_s[:].bitcast(U8).indirect(idx2[:]))
         nc.vector.tensor_copy(v_s_listed[:], tab_s[:].bitcast(U8).indirect(idx[:]))
-        nc.vector.tensor_copy(v2_s.bitcast(I32), v2_s_listed[:].bitcast(I32))
+        nc.vector.tensor_copy(planes[0][:, S : S + S2].bitcast(I32), v2_s_listed[:].bitcast(I32))
         nc.vector.tensor_copy(
-            v_s.rearrange("p (g t m) -> p g t m", g=GROUPS, t=PACK),
+            planes[0][:, 0:S].rearrange("p (g t m) -> p g t m", g=GROUPS, t=PACK),
             v_s_listed[:].rearrange("p (g m t) -> p g t m", g=GROUPS, t=PACK),
         )
         for q in range(QUADRANTS - 1):
@@ -109,35 +98,32 @@ def tile_list_slate_candidate_profiles_kernel(
             nc.sync.dma_start(
                 planes[0][target : target + ROWS, :].bitcast(I32), planes[0][source : source + ROWS, :].bitcast(I32)
             )
-        tab_w.append(held([P, T], I32, "tab_w1", after="v_s_listed"))
+        tab_w = [tab_w0, held([P, T], I32, "tab_w1", after="v_s_listed")]
         load_words(tab_w[1], tab_words, 1)
         for s in range(ROWS):
             source = FIRST_ROW + ROWS * QUADRANTS + s
             nc.sync.dma_start(
                 planes[1][PLANE_ROW[1] + s : P : QUAD, :].bitcast(I32), planes[0][source:P:ROWS, :].bitcast(I32)
             )
-        nc.vector.tensor_copy(v2_w0[:], tab2_w[0][:].bitcast(U32).indirect(idx2[:]))
+
+        v_w = [[held([P, PASS], U32, "v_w%d_%d" % (a, g)) for g in range(GROUPS)] for a in range(K_PASSES)]
+        v2_w = [held([P, S2], U32, "v2_w%d" % a) for a in range(K_PASSES)]
+
+        def gather_v(a, g):
+            nc.vector.tensor_copy(
+                v_w[a][g][:].rearrange("p (t m) -> p m t", t=PACK),
+                tab_w[a][:].bitcast(U32).indirect(idx[:, LIST_COLS * g : LIST_COLS * (g + 1)]),
+            )
+
+        def gather_v2(a):
+            nc.vector.tensor_copy(v2_w[a][:], tab2_w[a][:].bitcast(U32).indirect(idx2[:]))
+
+        gather_v2(0)
         bg_t = held([P, N_TILES], F32, "bg_t", after="tab2_w0")
         with nc.allow_non_contiguous_dma(reason="one bias value to a partition"):
             nc.sync.dma_start(bg_t[:], bg.rearrange("(c p) -> p c", p=P))
 
-        v_w = [[held([P, PASS], U32, "v_w%d_%d" % (a, g)) for g in range(GROUPS)] for a in range(K_PASSES)]
-
-        def gather_v(a, g):
-            window = tab_w[a][:].bitcast(U32).indirect(idx[:, LIST_COLS * g : LIST_COLS * (g + 1)])
-            if a in PLAIN_PASSES:
-                listed = held([P, PASS], U32, "listed%d_%d" % (a, g))
-                nc.vector.tensor_copy(listed[:], window)
-                nc.vector.tensor_copy(
-                    v_w[a][g][:].rearrange("p (t c r) -> p c t r", t=PACK, r=RUN),
-                    listed[:].rearrange("p (c r t) -> p c t r", t=PACK, r=RUN),
-                )
-            else:
-                nc.vector.tensor_copy(v_w[a][g][:].rearrange("p (t m) -> p m t", t=PACK), window)
-
-        v2_w1 = held([P, S2], U32, "v2_w1")
-        v2_w = [v2_w0, v2_w1]
-        nc.vector.tensor_copy(v2_w1[:], tab2_w[1][:].bitcast(U32).indirect(idx2[:]))
+        gather_v2(1)
         wg_rows = held([P, GROUPS, PACK, N], F32, "wg_rows", after="tab2_w1")
         for g in range(GROUPS):
             nc.sync.dma_start(
@@ -149,12 +135,13 @@ def tile_list_slate_candidate_profiles_kernel(
         attr_w = held([P, GROUPS, 2 * N // 4], I32, "attr_w", after="tab_w0")
         nc.sync.dma_start(attr_w[:], attr_words.bitcast(I32).rearrange("g p n -> p g n"))
 
-
         rec_sign = held([P, GROUPS, 2, 2], BF16, "rec_sign")
         rec_size = held([P, GROUPS, PACK], F32, "rec_size")
-        if SCALAR_GROUPS:
-            nc.scalar.activation(rec_sign[:].rearrange("p g u e -> p g (u e)"), rec_t[:], ACT.Sign)
-            nc.scalar.activation(rec_size[:], rec_t[:], ACT.Abs)
+        nc.scalar.activation(rec_sign[:].rearrange("p g u e -> p g (u e)"), rec_t[:], ACT.Sign)
+        nc.scalar.activation(rec_size[:], rec_t[:], ACT.Abs)
+
+        def for_scalar(h, g):
+            return (h, g) == (SCALAR_HALF, SCALAR_GROUP)
 
         def score(acc, g, t, a, j0, width, start, stop):
             m0 = PASS * g + P * t
@@ -170,14 +157,13 @@ def tile_list_slate_candidate_profiles_kernel(
 
         def fill(acc, h, b, a):
             g, c = divmod(b, PACK)
-            if (h, g) in SCALAR_GROUPS:
-                score(acc[:], g, c, a, HALF * h, HALF, a == 0, a == K_PASSES - 1)
+            first_pass, last_pass = a == 0, a == K_PASSES - 1
+            if for_scalar(h, g):
+                score(acc[:], g, c, a, HALF * h, HALF, first_pass, last_pass)
             else:
                 for t in range(PACK):
-                    score(
-                        acc[:, P * t : P * (t + 1)], g, t, a, HALF * h + P * c, P,
-                        a == 0 and t == 0, a == K_PASSES - 1 and t == PACK - 1,
-                    )
+                    start, stop = first_pass and t == 0, last_pass and t == PACK - 1
+                    score(acc[:, P * t : P * (t + 1)], g, t, a, HALF * h + P * c, P, start, stop)
 
         first = [bank(b, "first%d" % b) for b in range(BANKS)]
         for b in range(BANKS):
@@ -194,11 +180,13 @@ def tile_list_slate_candidate_profiles_kernel(
                 attr_scales[:, ROWS * q : ROWS * (q + 1), :].bitcast(I32).rearrange("g s n -> s g n"),
             )
 
-        z_pairs = [[held([P, 2, HALF, 2], BF16, "z_pairs%d_%d" % (h, g)) for g in range(GROUPS)] for h in range(2)]
-        z_bf = [
-            [held([P, HALF, PACK], BF16, "z_bf%d_%d" % (h, g)) if (h, g) != LATE_Z else None for g in range(GROUPS)]
+        z_pairs = held([P, 2, HALF, 2], BF16, "z_pairs")
+        z_bf = {
+            (h, g): held([P, HALF, PACK], BF16, "z_bf%d_%d" % (h, g))
             for h in range(2)
-        ]
+            for g in range(GROUPS)
+            if not for_scalar(h, g)
+        }
         z_w = [[held([P, HALF], U32, "z_w%d_%d" % (h, g)) for g in range(GROUPS)] for h in range(2)]
         z_s = [[held([P, HALF], U8, "z_s%d_%d" % (h, g)) for g in range(GROUPS)] for h in range(2)]
         wg_bf = [held([P, N, PACK], BF16, "wg_bf%d" % g) for g in range(GROUPS)]
@@ -207,30 +195,16 @@ def tile_list_slate_candidate_profiles_kernel(
 
         def quantize(words, scales, side_by_side):
             nc.vector.quantize_mx(
-                out=words[:].bitcast(FP8X4), scales=scales[:], in_=side_by_side.rearrange("p w t -> p (w t)")
+                out=words[:].bitcast(FP8X4), scales=scales[:], in_=side_by_side[:].rearrange("p w t -> p (w t)")
             )
-
-        def cast_wg(g):
-            for piece in range(WG_PIECES):
-                cols = slice(N // WG_PIECES * piece, N // WG_PIECES * (piece + 1))
-                side_by_side = wg_bf[g][:, cols, :].rearrange("p (c r) t -> p c t r", r=RUN)
-                rows = wg_rows[:, g, :, cols].rearrange("p t (c r) -> p c t r", r=RUN)
-                if g in WG_ON_GPSIMD:
-                    nc.gpsimd.tensor_scalar(
-                        wg_bf[g][:, cols, :], wg_rows[:, g, :, cols].rearrange("p t w -> p w t"), 1.0, 0.0, ALU.mult, ALU.add
-                    )
-                else:
-                    nc.scalar.copy(side_by_side, rows)
 
         def empty(acc, h, b):
             g, c = divmod(b, PACK)
-            if (h, g) in SCALAR_GROUPS:
-                nc.scalar.activation(
-                    z_pairs[h][g][:, c // 2, :, c % 2], acc[:], ACT.Relu, scale=rec_size[:, g, c : c + 1]
-                )
+            if for_scalar(h, g):
+                nc.scalar.activation(z_pairs[:, c // 2, :, c % 2], acc[:], ACT.Relu, scale=rec_size[:, g, c : c + 1])
             else:
                 nc.vector.scalar_tensor_tensor(
-                    z_bf[h][g][:, P * c : P * (c + 1), :],
+                    z_bf[h, g][:, P * c : P * (c + 1), :],
                     acc[:].rearrange("p (t j) -> p j t", t=PACK),
                     0.0,
                     rec_t[:, g : g + 1, :].to_broadcast([P, P, PACK]),
@@ -238,88 +212,81 @@ def tile_list_slate_candidate_profiles_kernel(
                     ALU.mult,
                 )
 
-        def finish(h):
-            for g in range(GROUPS):
-                if (h, g) in SCALAR_GROUPS:
-                    nc.vector.tensor_tensor(
-                        z_bf[h][g][:].rearrange("p j (u e) -> p j u e", e=2),
-                        z_pairs[h][g][:].rearrange("p u j e -> p j u e"),
-                        rec_sign[:, g : g + 1, :, :].to_broadcast([P, HALF, 2, 2]),
-                        ALU.mult,
-                    )
-            for g in sorted(range(GROUPS), key=lambda g: (h, g) in SCALAR_GROUPS):
-                quantize(z_w[h][g], z_s[h][g], z_bf[h][g][:])
-
         second = []
         for b in range(BANKS):
             empty(first[b], 0, b)
-            acc = bank(b, "second%d" % b)
-            second.append(acc)
+            second.append(bank(b, "second%d" % b))
             for a in range(K_PASSES):
-                fill(acc, 1, b, a)
-        finish(0)
-        cast_wg(0)
-        cast_wg(1)
-        quantize(wg_w[0], wg_s[0], wg_bf[0][:])
-        quantize(wg_w[1], wg_s[1], wg_bf[1][:])
+                fill(second[b], 1, b, a)
+        for g in range(GROUPS):
+            quantize(z_w[0][g], z_s[0][g], z_bf[0, g])
+
+        for g in range(GROUPS):
+            for cols in halves(N):
+                nc.scalar.copy(
+                    wg_bf[g][:, cols, :].rearrange("p (c r) t -> p c t r", r=RUN),
+                    wg_rows[:, g, :, cols].rearrange("p t (c r) -> p c t r", r=RUN),
+                )
+        for g in range(GROUPS):
+            quantize(wg_w[g], wg_s[g], wg_bf[g])
+
         for b in range(BANKS):
             empty(second[b], 1, b)
-        if LATE_Z:
-            z_bf[1][0] = held([P, HALF, PACK], BF16, "z_bf1_0", after="wg_bf1")
-        finish(1)
+        woven = held([P, HALF, PACK], BF16, "woven", after="wg_bf1")
+        z_bf[SCALAR_HALF, SCALAR_GROUP] = woven
+        nc.vector.tensor_tensor(
+            woven[:].rearrange("p j (u e) -> p j u e", e=2),
+            z_pairs[:].rearrange("p u j e -> p j u e"),
+            rec_sign[:, SCALAR_GROUP : SCALAR_GROUP + 1, :, :].to_broadcast([P, HALF, 2, 2]),
+            ALU.mult,
+        )
+        group_order = [sorted(range(GROUPS), key=lambda g: for_scalar(h, g)) for h in range(2)]
+        for g in group_order[1]:
+            quantize(z_w[1][g], z_s[1][g], z_bf[1, g])
 
         attr_operand = [
             (attr_w[:, g, :].bitcast(U8).bitcast(FP4X4), attr_s[:, g, :].bitcast(U8)) for g in range(GROUPS)
         ]
         wg_operand = [(wg_w[g][:].bitcast(FP8X4), wg_s[g][:]) for g in range(GROUPS)]
 
-        def profile(acc, operand, h, c, g, first_group):
-            words, scales = operand[g]
-            nc.tensor.matmul_mx(
-                out=acc[:],
-                lhsT=words[:, P * c : P * (c + 1)],
-                lhsT_scale=scales[:, P * c : P * (c + 1)],
-                rhs=z_w[h][g][:].bitcast(FP8X4),
-                rhs_scale=z_s[h][g][:],
-                start=(g == first_group),
-                stop=(g != first_group),
-            )
+        def profile(acc, operand, h, c):
+            for g in group_order[h]:
+                words, scales = operand[g]
+                nc.tensor.matmul_mx(
+                    out=acc[:],
+                    lhsT=words[:, P * c : P * (c + 1)],
+                    lhsT_scale=scales[:, P * c : P * (c + 1)],
+                    rhs=z_w[h][g][:].bitcast(FP8X4),
+                    rhs_scale=z_s[h][g][:],
+                    start=(g == group_order[h][0]),
+                    stop=(g == group_order[h][-1]),
+                )
 
-        def finish_tile(h, c, y, gate_acc, multiply):
+        def gate_and_store(h, c, y_sum, gate_sum):
             gate = ring.tile([P, HALF], F32, name="gate")
-            nc.scalar.activation(gate[:], gate_acc[:], ACT.Sigmoid, bias=bg_t[:, c : c + 1])
+            nc.scalar.activation(gate[:], gate_sum[:], ACT.Sigmoid, bias=bg_t[:, c : c + 1])
             result = ring.tile([P, HALF], F32, name="result")
             is_last = h == 1 and c == N_TILES - 1
             for cols in halves(HALF) if is_last else [slice(0, HALF)]:
-                multiply(result[:, cols], y[:, cols], gate[:, cols], ALU.mult)
+                nc.vector.tensor_tensor(result[:, cols], y_sum[:, cols], gate[:, cols], ALU.mult)
                 nc.sync.dma_start(
                     out[P * c : P * (c + 1), HALF * h + cols.start : HALF * h + cols.stop], result[:, cols]
                 )
 
-        y_acc = [bank(c, "y0_%d" % c) for c in range(N_TILES)]
-        gate_acc = [bank(N_TILES + c, "gate0_%d" % c) for c in range(N_TILES)]
+        y_first = [bank(c, "y0_%d" % c) for c in range(N_TILES)]
+        gate_first = [bank(N_TILES + c, "gate0_%d" % c) for c in range(N_TILES)]
         for c in range(N_TILES):
-            for g in range(GROUPS):
-                profile(y_acc[c], attr_operand, 0, c, g, 0)
+            profile(y_first[c], attr_operand, 0, c)
         for c in range(N_TILES):
-            for g in range(GROUPS):
-                profile(gate_acc[c], wg_operand, 0, c, g, 0)
-        y_out = [held([P, HALF], F32, "y_out%d" % c) for c in range(GPSIMD_TILES)]
-        for c in range(GPSIMD_TILES):
-            nc.scalar.copy(y_out[c][:], y_acc[c][:])
+            profile(gate_first[c], wg_operand, 0, c)
         for c in range(N_TILES):
-            if c < GPSIMD_TILES:
-                finish_tile(0, c, y_out[c], gate_acc[c], nc.gpsimd.tensor_tensor)
-            else:
-                finish_tile(0, c, y_acc[c], gate_acc[c], nc.vector.tensor_tensor)
+            gate_and_store(0, c, y_first[c], gate_first[c])
 
-        y_acc = [bank(c, "y1_%d" % c) for c in range(N_TILES)]
-        gate_acc = [bank(N_TILES + c, "gate1_%d" % c) for c in range(N_TILES)]
-        for c in range(N_TILES + 1):
-            if c < N_TILES:
-                for g in (1, 0):
-                    profile(gate_acc[c], wg_operand, 1, c, g, 1)
-            if c > 0:
-                for g in (1, 0):
-                    profile(y_acc[c - 1], attr_operand, 1, c - 1, g, 1)
-                finish_tile(1, c - 1, y_acc[c - 1], gate_acc[c - 1], nc.vector.tensor_tensor)
+        y_second = [bank(c, "y1_%d" % c) for c in range(N_TILES)]
+        gate_second = [bank(N_TILES + c, "gate1_%d" % c) for c in range(N_TILES)]
+        profile(gate_second[0], wg_operand, 1, 0)
+        for c in range(N_TILES):
+            if c + 1 < N_TILES:
+                profile(gate_second[c + 1], wg_operand, 1, c + 1)
+            profile(y_second[c], attr_operand, 1, c)
+            gate_and_store(1, c, y_second[c], gate_second[c])

@@ -119,10 +119,6 @@ def tile_list_slate_candidate_profiles_kernel(
             nc.vector.tensor_copy(v2_w[a][:], tab2_w[a][:].bitcast(U32).indirect(idx2[:]))
 
         gather_v2(0)
-        bg_t = held([P, N_TILES], F32, "bg_t", after="tab2_w0")
-        with nc.allow_non_contiguous_dma(reason="one bias value to a partition"):
-            nc.sync.dma_start(bg_t[:], bg.rearrange("(c p) -> p c", p=P))
-
         gather_v2(1)
         wg_rows = held([P, GROUPS, PACK, N], F32, "wg_rows", after="tab2_w1")
         for g in range(GROUPS):
@@ -229,6 +225,9 @@ def tile_list_slate_candidate_profiles_kernel(
                 )
         for g in range(GROUPS):
             quantize(wg_w[g], wg_s[g], wg_bf[g])
+        bg_t = held([P, N_TILES], F32, "bg_t", after="tab2_w1")
+        with nc.allow_non_contiguous_dma(reason="one bias value to a partition"):
+            nc.sync.dma_start(bg_t[:], bg.rearrange("(c p) -> p c", p=P))
 
         for b in range(BANKS):
             empty(second[b], 1, b)
@@ -273,8 +272,8 @@ def tile_list_slate_candidate_profiles_kernel(
                     out[P * c : P * (c + 1), HALF * h + cols.start : HALF * h + cols.stop], result[:, cols]
                 )
 
-        y_first = [bank(c, "y0_%d" % c) for c in range(N_TILES)]
-        gate_first = [bank(N_TILES + c, "gate0_%d" % c) for c in range(N_TILES)]
+        y_first = [bank(N_TILES + c, "y0_%d" % c) for c in range(N_TILES)]
+        gate_first = [bank(c, "gate0_%d" % c) for c in range(N_TILES)]
         for c in range(N_TILES):
             profile(y_first[c], attr_operand, 0, c)
         for c in range(N_TILES):
@@ -282,8 +281,8 @@ def tile_list_slate_candidate_profiles_kernel(
         for c in range(N_TILES):
             gate_and_store(0, c, y_first[c], gate_first[c])
 
-        y_second = [bank(c, "y1_%d" % c) for c in range(N_TILES)]
-        gate_second = [bank(N_TILES + c, "gate1_%d" % c) for c in range(N_TILES)]
+        y_second = [bank(N_TILES + c, "y1_%d" % c) for c in range(N_TILES)]
+        gate_second = [bank(c, "gate1_%d" % c) for c in range(N_TILES)]
         profile(gate_second[0], wg_operand, 1, 0)
         for c in range(N_TILES):
             if c + 1 < N_TILES:

@@ -133,6 +133,8 @@ def tile_list_slate_candidate_profiles_kernel(
 
         rec_sign = held([P, GROUPS, 2, 2], BF16, "rec_sign")
         rec_size = held([P, GROUPS, PACK], F32, "rec_size")
+        warm = held([P, 1], F32, "warm")
+        nc.scalar.activation(warm[:], rec_t[:, 0, 0:1], ACT.Sigmoid)
         nc.scalar.activation(rec_sign[:].rearrange("p g u e -> p g (u e)"), rec_t[:], ACT.Sign)
         nc.scalar.activation(rec_size[:], rec_t[:], ACT.Abs)
 
@@ -181,9 +183,10 @@ def tile_list_slate_candidate_profiles_kernel(
             (h, g): held([P, HALF, PACK], BF16, "z_bf%d_%d" % (h, g))
             for h in range(2)
             for g in range(GROUPS)
-            if not for_scalar(h, g)
+            if h == 0
         }
-        z_w = [[held([P, HALF], U32, "z_w%d_%d" % (h, g)) for g in range(GROUPS)] for h in range(2)]
+        z_w = [[held([P, HALF], U32, "z_w0_%d" % g) for g in range(GROUPS)], [held([P, HALF], U32, "z_w1_0")]]
+        z_late = [held([P, HALF // 2, PACK], BF16, "z_late0")]
         z_s = [[held([P, HALF], U8, "z_s%d_%d" % (h, g)) for g in range(GROUPS)] for h in range(2)]
         wg_bf = [held([P, N, PACK], BF16, "wg_bf%d" % g) for g in range(GROUPS)]
         wg_w = [held([P, N], U32, "wg_w%d" % g) for g in range(GROUPS)]
@@ -200,7 +203,7 @@ def tile_list_slate_candidate_profiles_kernel(
                 nc.scalar.activation(z_pairs[:, c // 2, :, c % 2], acc[:], ACT.Relu, scale=rec_size[:, g, c : c + 1])
             else:
                 nc.vector.scalar_tensor_tensor(
-                    z_bf[h, g][:, P * c : P * (c + 1), :],
+                    z_bf[h, g][:, P * c : P * (c + 1), :] if h == 0 else z_late[c // 2][:, P * (c % 2) : P * (c % 2 + 1), :],
                     acc[:].rearrange("p (t j) -> p j t", t=PACK),
                     0.0,
                     rec_t[:, g : g + 1, :].to_broadcast([P, P, PACK]),
@@ -217,6 +220,9 @@ def tile_list_slate_candidate_profiles_kernel(
         for g in range(GROUPS):
             quantize(z_w[0][g], z_s[0][g], z_bf[0, g])
 
+        for b in (4, 5):
+            empty(second[b], 1, b)
+
         for g in range(GROUPS):
             for cols in halves(N):
                 nc.scalar.copy(
@@ -229,9 +235,13 @@ def tile_list_slate_candidate_profiles_kernel(
         with nc.allow_non_contiguous_dma(reason="one bias value to a partition"):
             nc.sync.dma_start(bg_t[:], bg.rearrange("(c p) -> p c", p=P))
 
-        for b in range(BANKS):
+        z_late.append(held([P, HALF // 2, PACK], BF16, "z_late1", after="wg_bf1"))
+        z_w[1].append(held([P, HALF], U32, "z_w1_1", after="wg_bf0"))
+        for b in (0, 1, 2, 3, 6, 7):
             empty(second[b], 1, b)
-        woven = held([P, HALF, PACK], BF16, "woven", after="wg_bf1")
+        for part, cols in enumerate(halves(HALF)):
+            quantize(z_w[1][1][:, cols], z_s[1][1][:, cols], z_late[part])
+        woven = held([P, HALF, PACK], BF16, "woven", after="z_late0")
         z_bf[SCALAR_HALF, SCALAR_GROUP] = woven
         nc.vector.tensor_tensor(
             woven[:].rearrange("p j (u e) -> p j u e", e=2),
@@ -240,16 +250,15 @@ def tile_list_slate_candidate_profiles_kernel(
             ALU.mult,
         )
         group_order = [sorted(range(GROUPS), key=lambda g: for_scalar(h, g)) for h in range(2)]
-        for g in group_order[1]:
-            quantize(z_w[1][g], z_s[1][g], z_bf[1, g])
+        quantize(z_w[1][0], z_s[1][0], woven)
 
         attr_operand = [
             (attr_w[:, g, :].bitcast(U8).bitcast(FP4X4), attr_s[:, g, :].bitcast(U8)) for g in range(GROUPS)
         ]
         wg_operand = [(wg_w[g][:].bitcast(FP8X4), wg_s[g][:]) for g in range(GROUPS)]
 
-        def profile(acc, operand, h, c):
-            for g in group_order[h]:
+        def profile(acc, operand, h, c, groups=None):
+            for g in groups or group_order[h]:
                 words, scales = operand[g]
                 nc.tensor.matmul_mx(
                     out=acc[:],
@@ -264,7 +273,10 @@ def tile_list_slate_candidate_profiles_kernel(
         def gate_and_store(h, c, y_sum, gate_sum):
             gate = ring.tile([P, HALF], F32, name="gate")
             nc.scalar.activation(gate[:], gate_sum[:], ACT.Sigmoid, bias=bg_t[:, c : c + 1])
-            result = ring.tile([P, HALF], F32, name="result")
+            if (h, c) == (0, 0):
+                result = held([P, HALF], F32, "result_first", after="z_late0")
+            else:
+                result = ring.tile([P, HALF], F32, name="result")
             is_last = h == 1 and c == N_TILES - 1
             for cols in halves(HALF) if is_last else [slice(0, HALF)]:
                 nc.vector.tensor_tensor(result[:, cols], y_sum[:, cols], gate[:, cols], ALU.mult)
@@ -272,8 +284,9 @@ def tile_list_slate_candidate_profiles_kernel(
                     out[P * c : P * (c + 1), HALF * h + cols.start : HALF * h + cols.stop], result[:, cols]
                 )
 
-        y_first = [bank(N_TILES + c, "y0_%d" % c) for c in range(N_TILES)]
-        gate_first = [bank(c, "gate0_%d" % c) for c in range(N_TILES)]
+        y_banks, gate_banks = (0, 4, 1, 5), (2, 6, 3, 7)
+        y_first = [bank(y_banks[c], "y0_%d" % c) for c in range(N_TILES)]
+        gate_first = [bank(gate_banks[c], "gate0_%d" % c) for c in range(N_TILES)]
         for c in range(N_TILES):
             profile(y_first[c], attr_operand, 0, c)
         for c in range(N_TILES):
@@ -281,11 +294,11 @@ def tile_list_slate_candidate_profiles_kernel(
         for c in range(N_TILES):
             gate_and_store(0, c, y_first[c], gate_first[c])
 
-        y_second = [bank(N_TILES + c, "y1_%d" % c) for c in range(N_TILES)]
-        gate_second = [bank(c, "gate1_%d" % c) for c in range(N_TILES)]
-        profile(gate_second[0], wg_operand, 1, 0)
+        y_second = [bank(y_banks[c], "y1_%d" % c) for c in range(N_TILES)]
+        gate_second = [bank(gate_banks[c], "gate1_%d" % c) for c in range(N_TILES)]
+        for g in group_order[1]:
+            for c in range(N_TILES):
+                profile(gate_second[c], wg_operand, 1, c, [g])
         for c in range(N_TILES):
-            if c + 1 < N_TILES:
-                profile(gate_second[c + 1], wg_operand, 1, c + 1)
             profile(y_second[c], attr_operand, 1, c)
             gate_and_store(1, c, y_second[c], gate_second[c])

@@ -57,7 +57,7 @@ def tile_list_slate_candidate_profiles_kernel(
         idx = keep.tile([P, S // 16], U16, name="idx")
         idx2 = keep.tile([P, S2 // 16], U16, name="idx2")
         tab_w0 = held([P, T], I32, "tab_w0")
-        tab2_w = [held([P, T2], I32, "tab2_w%d" % a) for a in range(K_PASSES)]
+        tab2_w = [held([P, T2], I32, "tab2_w0")]
         tab_s = held([P, T // 4], I32, "tab_s")
         tab2_s = held([P, T2 // 4], I32, "tab2_s")
 
@@ -74,32 +74,45 @@ def tile_list_slate_candidate_profiles_kernel(
         nc.sync.dma_start(idx2[:], offs2)
         load_scales(tab_s, tab_scales)
         nc.sync.dma_start(idx[:], offs)
+        load_words(tab2_w[0], tab2_words, 0)
+        load_words(tab_w0, tab_words, 0)
         rec_t = held([P, GROUPS, PACK], F32, "rec_t")
         nc.sync.dma_start(rec_t[:], rec.rearrange("(g p t) -> p g t", g=GROUPS, t=PACK))
-        load_words(tab2_w[0], tab2_words, 0)
-        load_words(tab2_w[1], tab2_words, 1)
-        load_words(tab_w0, tab_words, 0)
 
         v_s_listed = held([P, S], U8, "v_s_listed")
-        v2_s_listed = held([P, S2], U8, "v2_s_listed")
         planes = [held([P, S + S2], U8, "planes%d" % a) for a in range(K_PASSES)]
         nc.gpsimd.memset(planes[1][:].bitcast(I32), 0)
 
-        nc.vector.tensor_copy(v2_s_listed[:], tab2_s[:].bitcast(U8).indirect(idx2[:]))
+        def list_cols(first, count):
+            return slice(first // 16, (first + count) // 16)
+
+        def gather_v2_scales(h, after=""):
+            listed = held([P, HALF], U8, "v2_s_listed%d" % h, after=after)
+            nc.vector.tensor_copy(listed[:], tab2_s[:].bitcast(U8).indirect(idx2[:, list_cols(HALF * h, HALF)]))
+            nc.vector.tensor_copy(planes[0][:, S + HALF * h : S + HALF * (h + 1)].bitcast(I32), listed[:].bitcast(I32))
+
+        def move_first_pass(cols):
+            for q in range(QUADRANTS - 1):
+                source = FIRST_ROW + ROWS * q
+                target = QUAD * q + PLANE_ROW[0]
+                nc.sync.dma_start(
+                    planes[0][target : target + ROWS, cols].bitcast(I32),
+                    planes[0][source : source + ROWS, cols].bitcast(I32),
+                )
+
+        gather_v2_scales(0)
         nc.vector.tensor_copy(v_s_listed[:], tab_s[:].bitcast(U8).indirect(idx[:]))
-        nc.vector.tensor_copy(planes[0][:, S : S + S2].bitcast(I32), v2_s_listed[:].bitcast(I32))
         nc.vector.tensor_copy(
             planes[0][:, 0:S].rearrange("p (g t m) -> p g t m", g=GROUPS, t=PACK),
             v_s_listed[:].rearrange("p (g m t) -> p g t m", g=GROUPS, t=PACK),
         )
-        for q in range(QUADRANTS - 1):
-            source = FIRST_ROW + ROWS * q
-            target = QUAD * q + PLANE_ROW[0]
-            nc.sync.dma_start(
-                planes[0][target : target + ROWS, :].bitcast(I32), planes[0][source : source + ROWS, :].bitcast(I32)
-            )
+        move_first_pass(slice(0, S + HALF))
         tab_w = [tab_w0, held([P, T], I32, "tab_w1", after="v_s_listed")]
         load_words(tab_w[1], tab_words, 1)
+        gather_v2_scales(1, after="tab_s")
+        move_first_pass(slice(S + HALF, S + S2))
+        tab2_w.append(held([P, T2], I32, "tab2_w1", after="tab_s"))
+        load_words(tab2_w[1], tab2_words, 1)
         for s in range(ROWS):
             source = FIRST_ROW + ROWS * QUADRANTS + s
             nc.sync.dma_start(
@@ -108,6 +121,7 @@ def tile_list_slate_candidate_profiles_kernel(
 
         v_w = [[held([P, PASS], U32, "v_w%d_%d" % (a, g)) for g in range(GROUPS)] for a in range(K_PASSES)]
         v2_w = [held([P, S2], U32, "v2_w%d" % a) for a in range(K_PASSES)]
+        QUARTER = HALF // 2
 
         def gather_v(a, g):
             nc.vector.tensor_copy(
@@ -115,12 +129,13 @@ def tile_list_slate_candidate_profiles_kernel(
                 tab_w[a][:].bitcast(U32).indirect(idx[:, LIST_COLS * g : LIST_COLS * (g + 1)]),
             )
 
-        def gather_v2(a):
-            nc.vector.tensor_copy(v2_w[a][:], tab2_w[a][:].bitcast(U32).indirect(idx2[:]))
+        def gather_v2(a, j0, width):
+            nc.vector.tensor_copy(
+                v2_w[a][:, j0 : j0 + width], tab2_w[a][:].bitcast(U32).indirect(idx2[:, list_cols(j0, width)])
+            )
 
-        gather_v2(0)
-        gather_v2(1)
-        wg_rows = held([P, GROUPS, PACK, N], F32, "wg_rows", after="tab2_w1")
+        gather_v2(0, 0, S2)
+        wg_rows = held([P, GROUPS, PACK, N], F32, "wg_rows", after="tab2_w0")
         for g in range(GROUPS):
             nc.sync.dma_start(
                 wg_rows[:, g, :, :], wg[PASS * g : PASS * (g + 1), :].rearrange("(p t) n -> p t n", t=PACK)
@@ -158,18 +173,26 @@ def tile_list_slate_candidate_profiles_kernel(
             first_pass, last_pass = a == 0, a == K_PASSES - 1
             if for_scalar(h, g):
                 score(acc[:], g, c, a, HALF * h, HALF, first_pass, last_pass)
+            elif h == 0 and b < 2:
+                for e in range(2):
+                    score(acc[:, QUARTER * e : QUARTER * (e + 1)], g, 2 * b + e, a, 0, QUARTER, first_pass and e == 0, last_pass and e == 1)
             else:
                 for t in range(PACK):
                     start, stop = first_pass and t == 0, last_pass and t == PACK - 1
                     score(acc[:, P * t : P * (t + 1)], g, t, a, HALF * h + P * c, P, start, stop)
 
-        first = [bank(b, "first%d" % b) for b in range(BANKS)]
+        FIRST_ORDER = (0, 1, 4, 5, 2, 3, 6, 7)
+        SECOND_ORDER = (4, 5, 0, 1, 6, 7, 2, 3)
+        first = {b: bank(n, "first%d" % b) for n, b in enumerate(FIRST_ORDER)}
         for b in range(BANKS):
             fill(first[b], 0, b, 0)
         for g in range(GROUPS):
             gather_v(1, g)
-            for b in range(PACK * g, PACK * (g + 1)):
+        for part in range(2):
+            gather_v2(1, QUARTER * part, QUARTER)
+            for b in FIRST_ORDER[PACK * part : PACK * (part + 1)]:
                 fill(first[b], 0, b, 1)
+        gather_v2(1, HALF, HALF)
         attr_s = held([P, GROUPS, N // 4], I32, "attr_s", after="v_s_listed")
         nc.gpsimd.memset(attr_s[:], 0)
         for q in range(QUADRANTS):
@@ -179,6 +202,7 @@ def tile_list_slate_candidate_profiles_kernel(
             )
 
         z_pairs = held([P, 2, HALF, 2], BF16, "z_pairs")
+        z_pairs0 = held([P, 2, QUARTER, 2], BF16, "z_pairs0")
         z_bf = {
             (h, g): held([P, HALF, PACK], BF16, "z_bf%d_%d" % (h, g))
             for h in range(2)
@@ -201,6 +225,10 @@ def tile_list_slate_candidate_profiles_kernel(
             g, c = divmod(b, PACK)
             if for_scalar(h, g):
                 nc.scalar.activation(z_pairs[:, c // 2, :, c % 2], acc[:], ACT.Relu, scale=rec_size[:, g, c : c + 1])
+            elif h == 0 and b < 2:
+                for e in range(2):
+                    t = 2 * b + e
+                    nc.scalar.activation(z_pairs0[:, b, :, e], acc[:, QUARTER * e : QUARTER * (e + 1)], ACT.Relu, scale=rec_size[:, g, t : t + 1])
             else:
                 nc.vector.scalar_tensor_tensor(
                     z_bf[h, g][:, P * c : P * (c + 1), :] if h == 0 else z_late[c // 2][:, P * (c % 2) : P * (c % 2 + 1), :],
@@ -211,13 +239,20 @@ def tile_list_slate_candidate_profiles_kernel(
                     ALU.mult,
                 )
 
-        second = []
-        for b in range(BANKS):
-            empty(first[b], 0, b)
-            second.append(bank(b, "second%d" % b))
+        second = {}
+        for n in range(BANKS):
+            empty(first[FIRST_ORDER[n]], 0, FIRST_ORDER[n])
+            b = SECOND_ORDER[n]
+            second[b] = bank(n, "second%d" % b)
             for a in range(K_PASSES):
                 fill(second[b], 1, b, a)
-        for g in range(GROUPS):
+        nc.vector.tensor_tensor(
+            z_bf[0, 0][:, 0:QUARTER, :].rearrange("p j (u e) -> p j u e", e=2),
+            z_pairs0[:].rearrange("p u j e -> p j u e"),
+            rec_sign[:, 0:1, :, :].to_broadcast([P, QUARTER, 2, 2]),
+            ALU.mult,
+        )
+        for g in (1, 0):
             quantize(z_w[0][g], z_s[0][g], z_bf[0, g])
 
         for b in (4, 5):
@@ -231,7 +266,7 @@ def tile_list_slate_candidate_profiles_kernel(
                 )
         for g in range(GROUPS):
             quantize(wg_w[g], wg_s[g], wg_bf[g])
-        bg_t = held([P, N_TILES], F32, "bg_t", after="tab2_w1")
+        bg_t = held([P, N_TILES], F32, "bg_t", after="tab2_w0")
         with nc.allow_non_contiguous_dma(reason="one bias value to a partition"):
             nc.sync.dma_start(bg_t[:], bg.rearrange("(c p) -> p c", p=P))
 
@@ -249,7 +284,7 @@ def tile_list_slate_candidate_profiles_kernel(
             rec_sign[:, SCALAR_GROUP : SCALAR_GROUP + 1, :, :].to_broadcast([P, HALF, 2, 2]),
             ALU.mult,
         )
-        group_order = [sorted(range(GROUPS), key=lambda g: for_scalar(h, g)) for h in range(2)]
+        group_order = [(1, 0), (1, 0)]
         quantize(z_w[1][0], z_s[1][0], woven)
 
         attr_operand = [
@@ -284,7 +319,7 @@ def tile_list_slate_candidate_profiles_kernel(
                     out[P * c : P * (c + 1), HALF * h + cols.start : HALF * h + cols.stop], result[:, cols]
                 )
 
-        y_banks, gate_banks = (0, 4, 1, 5), (2, 6, 3, 7)
+        y_banks, gate_banks = [SECOND_ORDER.index(b) for b in (4, 5, 0, 1)], [SECOND_ORDER.index(b) for b in (2, 6, 3, 7)]
         y_first = [bank(y_banks[c], "y0_%d" % c) for c in range(N_TILES)]
         gate_first = [bank(gate_banks[c], "gate0_%d" % c) for c in range(N_TILES)]
         for c in range(N_TILES):

@@ -56,7 +56,7 @@ def tile_list_slate_candidate_profiles_kernel(
 
         idx = keep.tile([P, S // 16], U16, name="idx")
         idx2 = keep.tile([P, S2 // 16], U16, name="idx2")
-        tab_w0 = held([P, T], I32, "tab_w0")
+        tab_w = [held([P, T], I32, "tab_w%d" % a) for a in range(K_PASSES)]
         tab2_w = [held([P, T2], I32, "tab2_w0")]
         tab_s = held([P, T // 4], I32, "tab_s")
         tab2_s = held([P, T2 // 4], I32, "tab2_s")
@@ -75,9 +75,10 @@ def tile_list_slate_candidate_profiles_kernel(
         load_scales(tab_s, tab_scales)
         nc.sync.dma_start(idx[:], offs)
         load_words(tab2_w[0], tab2_words, 0)
-        load_words(tab_w0, tab_words, 0)
+        load_words(tab_w[0], tab_words, 0)
         rec_t = held([P, GROUPS, PACK], F32, "rec_t")
         nc.sync.dma_start(rec_t[:], rec.rearrange("(g p t) -> p g t", g=GROUPS, t=PACK))
+        load_words(tab_w[1], tab_words, 1)
 
         v_s_listed = held([P, S], U8, "v_s_listed")
         planes = [held([P, S + S2], U8, "planes%d" % a) for a in range(K_PASSES)]
@@ -86,32 +87,21 @@ def tile_list_slate_candidate_profiles_kernel(
         def list_cols(first, count):
             return slice(first // 16, (first + count) // 16)
 
-        def gather_v2_scales(h, after=""):
-            listed = held([P, HALF], U8, "v2_s_listed%d" % h, after=after)
-            nc.vector.tensor_copy(listed[:], tab2_s[:].bitcast(U8).indirect(idx2[:, list_cols(HALF * h, HALF)]))
-            nc.vector.tensor_copy(planes[0][:, S + HALF * h : S + HALF * (h + 1)].bitcast(I32), listed[:].bitcast(I32))
-
-        def move_first_pass(cols):
-            for q in range(QUADRANTS - 1):
-                source = FIRST_ROW + ROWS * q
-                target = QUAD * q + PLANE_ROW[0]
-                nc.sync.dma_start(
-                    planes[0][target : target + ROWS, cols].bitcast(I32),
-                    planes[0][source : source + ROWS, cols].bitcast(I32),
-                )
-
-        gather_v2_scales(0)
+        v2_s_listed = held([P, S2], U8, "v2_s_listed")
+        nc.vector.tensor_copy(v2_s_listed[:], tab2_s[:].bitcast(U8).indirect(idx2[:]))
         nc.vector.tensor_copy(v_s_listed[:], tab_s[:].bitcast(U8).indirect(idx[:]))
+        nc.vector.tensor_copy(planes[0][:, S : S + S2].bitcast(I32), v2_s_listed[:].bitcast(I32))
         nc.vector.tensor_copy(
             planes[0][:, 0:S].rearrange("p (g t m) -> p g t m", g=GROUPS, t=PACK),
             v_s_listed[:].rearrange("p (g m t) -> p g t m", g=GROUPS, t=PACK),
         )
-        move_first_pass(slice(0, S + HALF))
-        tab_w = [tab_w0, held([P, T], I32, "tab_w1", after="v_s_listed")]
-        load_words(tab_w[1], tab_words, 1)
-        gather_v2_scales(1, after="tab_s")
-        move_first_pass(slice(S + HALF, S + S2))
-        tab2_w.append(held([P, T2], I32, "tab2_w1", after="tab_s"))
+        for q in range(QUADRANTS - 1):
+            source = FIRST_ROW + ROWS * q
+            target = QUAD * q + PLANE_ROW[0]
+            nc.sync.dma_start(
+                planes[0][target : target + ROWS, :].bitcast(I32), planes[0][source : source + ROWS, :].bitcast(I32)
+            )
+        tab2_w.append(held([P, T2], I32, "tab2_w1", after="v_s_listed"))
         load_words(tab2_w[1], tab2_words, 1)
         for s in range(ROWS):
             source = FIRST_ROW + ROWS * QUADRANTS + s
@@ -184,7 +174,17 @@ def tile_list_slate_candidate_profiles_kernel(
         FIRST_ORDER = (0, 1, 4, 5, 2, 3, 6, 7)
         SECOND_ORDER = (4, 5, 0, 1, 6, 7, 2, 3)
         first = {b: bank(n, "first%d" % b) for n, b in enumerate(FIRST_ORDER)}
-        for b in range(BANKS):
+        for n in range(4):
+            nc.tensor.matmul_mx(
+                out=first[FIRST_ORDER[-1]][:],
+                lhsT=v_w[0][0][:, 0:P].bitcast(FP8X4),
+                lhsT_scale=v2_s_listed[:, 0:P],
+                rhs=v2_w[0][:, 0:HALF].bitcast(FP8X4),
+                rhs_scale=v2_s_listed[:, 0:HALF],
+                start=True,
+                stop=True,
+            )
+        for b in FIRST_ORDER:
             fill(first[b], 0, b, 0)
         for g in range(GROUPS):
             gather_v(1, g)
@@ -193,7 +193,7 @@ def tile_list_slate_candidate_profiles_kernel(
             for b in FIRST_ORDER[PACK * part : PACK * (part + 1)]:
                 fill(first[b], 0, b, 1)
         gather_v2(1, HALF, HALF)
-        attr_s = held([P, GROUPS, N // 4], I32, "attr_s", after="v_s_listed")
+        attr_s = held([P, GROUPS, N // 4], I32, "attr_s", after="tab_w1")
         nc.gpsimd.memset(attr_s[:], 0)
         for q in range(QUADRANTS):
             nc.sync.dma_start(

@@ -172,7 +172,7 @@ def tile_list_slate_candidate_profiles_kernel(
                     score(acc[:, P * t : P * (t + 1)], g, t, a, HALF * h + P * c, P, start, stop)
 
         FIRST_ORDER = (0, 1, 4, 5, 2, 3, 6, 7)
-        SECOND_ORDER = (4, 5, 0, 1, 6, 7, 2, 3)
+        SECOND_ORDER = (4, 0, 5, 1, 2, 3, 6, 7)
         first = {b: bank(n, "first%d" % b) for n, b in enumerate(FIRST_ORDER)}
         for n in range(4):
             nc.tensor.matmul_mx(
@@ -201,7 +201,6 @@ def tile_list_slate_candidate_profiles_kernel(
                 attr_scales[:, ROWS * q : ROWS * (q + 1), :].bitcast(I32).rearrange("g s n -> s g n"),
             )
 
-        z_pairs = held([P, 2, HALF, 2], BF16, "z_pairs")
         z_pairs0 = held([P, 2, QUARTER, 2], BF16, "z_pairs0")
         z_bf = {
             (h, g): held([P, HALF, PACK], BF16, "z_bf%d_%d" % (h, g))
@@ -260,13 +259,19 @@ def tile_list_slate_candidate_profiles_kernel(
 
         for g in range(GROUPS):
             for cols in halves(N):
+                if g == 0 and cols.start == 0:
+                    nc.gpsimd.tensor_scalar(
+                        wg_bf[g][:, cols, :], wg_rows[:, g, :, cols].rearrange("p t n -> p n t"), 1.0, 0.0, ALU.mult, ALU.add
+                    )
+                    continue
                 nc.scalar.copy(
                     wg_bf[g][:, cols, :].rearrange("p (c r) t -> p c t r", r=RUN),
                     wg_rows[:, g, :, cols].rearrange("p t (c r) -> p c t r", r=RUN),
                 )
         for g in range(GROUPS):
             quantize(wg_w[g], wg_s[g], wg_bf[g])
-        bg_t = held([P, N_TILES], F32, "bg_t", after="tab2_w0")
+        z_pairs = held([P, 2, HALF, 2], BF16, "z_pairs", after="tab2_w0")
+        bg_t = held([P, N_TILES], F32, "bg_t", after="v_w0_0")
         with nc.allow_non_contiguous_dma(reason="one bias value to a partition"):
             nc.sync.dma_start(bg_t[:], bg.rearrange("(c p) -> p c", p=P))
 
@@ -319,7 +324,7 @@ def tile_list_slate_candidate_profiles_kernel(
                     out[P * c : P * (c + 1), HALF * h + cols.start : HALF * h + cols.stop], result[:, cols]
                 )
 
-        y_banks, gate_banks = [SECOND_ORDER.index(b) for b in (4, 5, 0, 1)], [SECOND_ORDER.index(b) for b in (2, 6, 3, 7)]
+        y_banks, gate_banks = [SECOND_ORDER.index(b) for b in (4, 0, 5, 1)], [SECOND_ORDER.index(b) for b in (2, 3, 6, 7)]
         y_first = [bank(y_banks[c], "y0_%d" % c) for c in range(N_TILES)]
         gate_first = [bank(gate_banks[c], "gate0_%d" % c) for c in range(N_TILES)]
         for c in range(N_TILES):

@@ -44,6 +44,10 @@ def tile_list_slate_candidate_profiles_kernel(
         keep = ctx.enter_context(tc.tile_pool(name="keep", bufs=1))
         ring = ctx.enter_context(tc.tile_pool(name="ring", bufs=2 * N_TILES))
         psum = ctx.enter_context(tc.psum_pool(name="psum", bufs=1))
+        shared = ctx.enter_context(tc.tile_pool(name="shared", bufs=1))
+
+        def placed(shape, dtype, name, offset):
+            return shared.tile(shape, dtype, name=name, offset=offset, align_bytes=64)
 
         def held(shape, dtype, name, after=""):
             return keep.tile(shape, dtype, name=name, tag=after or name, align_bytes=64)
@@ -211,7 +215,7 @@ def tile_list_slate_candidate_profiles_kernel(
         z_w = [[held([P, HALF], U32, "z_w0_%d" % g) for g in range(GROUPS)], [held([P, HALF], U32, "z_w1_0")]]
         z_late = [held([P, HALF // 2, PACK], BF16, "z_late0")]
         z_s = [[held([P, HALF], U8, "z_s%d_%d" % (h, g)) for g in range(GROUPS)] for h in range(2)]
-        wg_bf = [held([P, N, PACK], BF16, "wg_bf%d" % g) for g in range(GROUPS)]
+        wg_bf = [held([P, N, PACK], BF16, "wg_bf0"), placed([P, N, PACK], BF16, "wg_bf1", 0)]
         wg_w = [held([P, N], U32, "wg_w%d" % g) for g in range(GROUPS)]
         wg_s = [held([P, N], U8, "wg_s%d" % g) for g in range(GROUPS)]
 
@@ -251,10 +255,8 @@ def tile_list_slate_candidate_profiles_kernel(
             rec_sign[:, 0:1, :, :].to_broadcast([P, QUARTER, 2, 2]),
             ALU.mult,
         )
-        for g in (1, 0):
+        for g, b in ((1, 4), (0, 5)):
             quantize(z_w[0][g], z_s[0][g], z_bf[0, g])
-
-        for b in (4, 5):
             empty(second[b], 1, b)
 
         for g in range(GROUPS):
@@ -275,48 +277,57 @@ def tile_list_slate_candidate_profiles_kernel(
         with nc.allow_non_contiguous_dma(reason="one bias value to a partition"):
             nc.sync.dma_start(bg_t[:], bg.rearrange("(c p) -> p c", p=P))
 
-        z_late.append(held([P, HALF // 2, PACK], BF16, "z_late1", after="wg_bf1"))
+        z_late.append(placed([P, HALF // 2, PACK], BF16, "z_late1", 2 * HALF))
         z_w[1].append(held([P, HALF], U32, "z_w1_1", after="wg_bf0"))
         for b in (0, 1, 2, 3, 6, 7):
             empty(second[b], 1, b)
         for part, cols in enumerate(halves(HALF)):
             quantize(z_w[1][1][:, cols], z_s[1][1][:, cols], z_late[part])
-        woven = held([P, HALF, PACK], BF16, "woven", after="z_late0")
-        z_bf[SCALAR_HALF, SCALAR_GROUP] = woven
-        nc.vector.tensor_tensor(
-            woven[:].rearrange("p j (u e) -> p j u e", e=2),
-            z_pairs[:].rearrange("p u j e -> p j u e"),
-            rec_sign[:, SCALAR_GROUP : SCALAR_GROUP + 1, :, :].to_broadcast([P, HALF, 2, 2]),
-            ALU.mult,
-        )
+        woven = [held([P, QUARTER, PACK], BF16, "woven0", after="z_late0"), placed([P, QUARTER, PACK], BF16, "woven1", 2 * HALF)]
+        for part, cols in enumerate(halves(HALF)):
+            nc.vector.tensor_tensor(
+                woven[part][:].rearrange("p j (u e) -> p j u e", e=2),
+                z_pairs[:, :, cols, :].rearrange("p u j e -> p j u e"),
+                rec_sign[:, SCALAR_GROUP : SCALAR_GROUP + 1, :, :].to_broadcast([P, QUARTER, 2, 2]),
+                ALU.mult,
+            )
         group_order = [(1, 0), (1, 0)]
-        quantize(z_w[1][0], z_s[1][0], woven)
+        for part, cols in enumerate(halves(HALF)):
+            quantize(z_w[1][0][:, cols], z_s[1][0][:, cols], woven[part])
 
         attr_operand = [
             (attr_w[:, g, :].bitcast(U8).bitcast(FP4X4), attr_s[:, g, :].bitcast(U8)) for g in range(GROUPS)
         ]
         wg_operand = [(wg_w[g][:].bitcast(FP8X4), wg_s[g][:]) for g in range(GROUPS)]
 
-        def profile(acc, operand, h, c, groups=None):
+        def profile(acc, operand, h, c, groups=None, cols=slice(0, HALF)):
             for g in groups or group_order[h]:
                 words, scales = operand[g]
                 nc.tensor.matmul_mx(
-                    out=acc[:],
+                    out=acc[:, cols],
                     lhsT=words[:, P * c : P * (c + 1)],
                     lhsT_scale=scales[:, P * c : P * (c + 1)],
-                    rhs=z_w[h][g][:].bitcast(FP8X4),
-                    rhs_scale=z_s[h][g][:],
+                    rhs=z_w[h][g][:, cols].bitcast(FP8X4),
+                    rhs_scale=z_s[h][g][:, cols],
                     start=(g == group_order[h][0]),
-                    stop=(g == group_order[h][-1]),
+                    stop=(g == group_order[h][-1] and cols.stop == HALF),
                 )
 
         def gate_and_store(h, c, y_sum, gate_sum):
             gate = ring.tile([P, HALF], F32, name="gate")
             nc.scalar.activation(gate[:], gate_sum[:], ACT.Sigmoid, bias=bg_t[:, c : c + 1])
             if (h, c) == (0, 0):
-                result = held([P, HALF], F32, "result_first", after="z_late0")
+                result = placed([P, HALF], F32, "result_first", 0)
+            elif (h, c) == (0, N_TILES - 1):
+                result = placed([P, HALF], F32, "result_pool", 4 * HALF)
             else:
                 result = ring.tile([P, HALF], F32, name="result")
+            if (h, c) == (0, N_TILES - 1):
+                y_copy = held([P, HALF], F32, "y_copy")
+                nc.scalar.copy(y_copy[:], y_sum[:])
+                nc.gpsimd.tensor_tensor(result[:], y_copy[:], gate[:], ALU.mult)
+                nc.sync.dma_start(out[P * c : P * (c + 1), 0:HALF], result[:])
+                return
             is_last = h == 1 and c == N_TILES - 1
             for cols in halves(HALF) if is_last else [slice(0, HALF)]:
                 nc.vector.tensor_tensor(result[:, cols], y_sum[:, cols], gate[:, cols], ALU.mult)
@@ -327,7 +338,10 @@ def tile_list_slate_candidate_profiles_kernel(
         y_banks, gate_banks = [SECOND_ORDER.index(b) for b in (4, 0, 5, 1)], [SECOND_ORDER.index(b) for b in (2, 3, 6, 7)]
         y_first = [bank(y_banks[c], "y0_%d" % c) for c in range(N_TILES)]
         gate_first = [bank(gate_banks[c], "gate0_%d" % c) for c in range(N_TILES)]
-        for c in range(N_TILES):
+        for g in group_order[0]:
+            for c in range(2):
+                profile(y_first[c], attr_operand, 0, c, [g])
+        for c in range(2, N_TILES):
             profile(y_first[c], attr_operand, 0, c)
         for c in range(N_TILES):
             profile(gate_first[c], wg_operand, 0, c)
@@ -336,9 +350,11 @@ def tile_list_slate_candidate_profiles_kernel(
 
         y_second = [bank(y_banks[c], "y1_%d" % c) for c in range(N_TILES)]
         gate_second = [bank(gate_banks[c], "gate1_%d" % c) for c in range(N_TILES)]
-        for g in group_order[1]:
+        for c in range(N_TILES):
+            profile(gate_second[c], wg_operand, 1, c, [1])
+        for cols in halves(HALF):
             for c in range(N_TILES):
-                profile(gate_second[c], wg_operand, 1, c, [g])
+                profile(gate_second[c], wg_operand, 1, c, [0], cols)
         for c in range(N_TILES):
             profile(y_second[c], attr_operand, 1, c)
             gate_and_store(1, c, y_second[c], gate_second[c])

@@ -26,14 +26,19 @@ QUAD = P // QUADRANTS
 ROWS = 4
 BANKS = 8
 HALF = S2 // 2
-LIST_COLS = PASS // 16
+QUARTER = HALF // 2
+PER_COLUMN = 16
 N_TILES = N // P
 RUN = 4
 
 FIRST_ROW = P - QUAD
 PLANE_ROW = (12, 0)
 
-SCALAR_HALF, SCALAR_GROUP = 1, 0
+SCALAR_GROUP = 0
+SCALAR_PIECES = (2, 4)
+FIRST_PIECES = (0, 1, 4, 5, 2, 3, 6, 7)
+SECOND_PIECES = (4, 0, 5, 1, 2, 3, 6, 7)
+GROUP_ORDER = (1, 0)
 
 
 def tile_list_slate_candidate_profiles_kernel(
@@ -88,8 +93,8 @@ def tile_list_slate_candidate_profiles_kernel(
         planes = [held([P, S + S2], U8, "planes%d" % a) for a in range(K_PASSES)]
         nc.gpsimd.memset(planes[1][:].bitcast(I32), 0)
 
-        def list_cols(first, count):
-            return slice(first // 16, (first + count) // 16)
+        def list_cols(entry, count):
+            return slice(entry // PER_COLUMN, (entry + count) // PER_COLUMN)
 
         v2_s_listed = held([P, S2], U8, "v2_s_listed")
         nc.vector.tensor_copy(v2_s_listed[:], tab2_s[:].bitcast(U8).indirect(idx2[:]))
@@ -115,12 +120,11 @@ def tile_list_slate_candidate_profiles_kernel(
 
         v_w = [[held([P, PASS], U32, "v_w%d_%d" % (a, g)) for g in range(GROUPS)] for a in range(K_PASSES)]
         v2_w = [held([P, S2], U32, "v2_w%d" % a) for a in range(K_PASSES)]
-        QUARTER = HALF // 2
 
         def gather_v(a, g):
             nc.vector.tensor_copy(
                 v_w[a][g][:].rearrange("p (t m) -> p m t", t=PACK),
-                tab_w[a][:].bitcast(U32).indirect(idx[:, LIST_COLS * g : LIST_COLS * (g + 1)]),
+                tab_w[a][:].bitcast(U32).indirect(idx[:, list_cols(PASS * g, PASS)]),
             )
 
         def gather_v2(a, j0, width):
@@ -147,8 +151,8 @@ def tile_list_slate_candidate_profiles_kernel(
         nc.scalar.activation(rec_sign[:].rearrange("p g u e -> p g (u e)"), rec_t[:], ACT.Sign)
         nc.scalar.activation(rec_size[:], rec_t[:], ACT.Abs)
 
-        def for_scalar(h, g):
-            return (h, g) == (SCALAR_HALF, SCALAR_GROUP)
+        def for_scalar(h, b):
+            return b < SCALAR_PIECES[h]
 
         def score(acc, g, t, a, j0, width, start, stop):
             m0 = PASS * g + P * t
@@ -162,40 +166,30 @@ def tile_list_slate_candidate_profiles_kernel(
                 stop=stop,
             )
 
-        def fill(acc, h, b, a):
+        def fill(acc, h, b, a, opens=0):
             g, c = divmod(b, PACK)
-            first_pass, last_pass = a == 0, a == K_PASSES - 1
-            if for_scalar(h, g):
-                score(acc[:], g, c, a, HALF * h, HALF, first_pass, last_pass)
-            elif h == 0 and b < 2:
-                for e in range(2):
-                    score(acc[:, QUARTER * e : QUARTER * (e + 1)], g, 2 * b + e, a, 0, QUARTER, first_pass and e == 0, last_pass and e == 1)
-            else:
+            first_pass, last_pass = a == opens, a != opens
+            if not for_scalar(h, b):
                 for t in range(PACK):
                     start, stop = first_pass and t == 0, last_pass and t == PACK - 1
                     score(acc[:, P * t : P * (t + 1)], g, t, a, HALF * h + P * c, P, start, stop)
+            elif h == 0:
+                for e, cols in enumerate(halves(HALF)):
+                    score(acc[:, cols], g, 2 * c + e, a, 0, QUARTER, first_pass and e == 0, last_pass and e == 1)
+            else:
+                score(acc[:], g, c, a, HALF * h, HALF, first_pass, last_pass)
 
-        FIRST_ORDER = (0, 1, 4, 5, 2, 3, 6, 7)
-        SECOND_ORDER = (4, 0, 5, 1, 2, 3, 6, 7)
-        first = {b: bank(n, "first%d" % b) for n, b in enumerate(FIRST_ORDER)}
-        for n in range(4):
-            nc.tensor.matmul_mx(
-                out=first[FIRST_ORDER[-1]][:],
-                lhsT=v_w[0][0][:, 0:P].bitcast(FP8X4),
-                lhsT_scale=v2_s_listed[:, 0:P],
-                rhs=v2_w[0][:, 0:HALF].bitcast(FP8X4),
-                rhs_scale=v2_s_listed[:, 0:HALF],
-                start=True,
-                stop=True,
-            )
-        for b in FIRST_ORDER:
+        first = {b: bank(n, "first%d" % b) for n, b in enumerate(FIRST_PIECES)}
+        last_piece = FIRST_PIECES[-1]
+        for b in FIRST_PIECES[:-1]:
             fill(first[b], 0, b, 0)
         for g in range(GROUPS):
             gather_v(1, g)
-        for part in range(2):
+        for part, pieces in enumerate(halves(BANKS)):
             gather_v2(1, QUARTER * part, QUARTER)
-            for b in FIRST_ORDER[PACK * part : PACK * (part + 1)]:
-                fill(first[b], 0, b, 1)
+            for b in FIRST_PIECES[pieces]:
+                fill(first[b], 0, b, 1, opens=int(b == last_piece))
+        fill(first[last_piece], 0, last_piece, 0, opens=1)
         gather_v2(1, HALF, HALF)
         attr_s = held([P, GROUPS, N // 4], I32, "attr_s", after="tab_w1")
         nc.gpsimd.memset(attr_s[:], 0)
@@ -205,15 +199,10 @@ def tile_list_slate_candidate_profiles_kernel(
                 attr_scales[:, ROWS * q : ROWS * (q + 1), :].bitcast(I32).rearrange("g s n -> s g n"),
             )
 
-        z_pairs0 = held([P, 2, QUARTER, 2], BF16, "z_pairs0")
-        z_bf = {
-            (h, g): held([P, HALF, PACK], BF16, "z_bf%d_%d" % (h, g))
-            for h in range(2)
-            for g in range(GROUPS)
-            if h == 0
-        }
+        z_pairs = [held([P, 2, QUARTER, 2], BF16, "z_pairs0")]
+        z_first = [held([P, HALF, PACK], BF16, "z_first%d" % g) for g in range(GROUPS)]
         z_w = [[held([P, HALF], U32, "z_w0_%d" % g) for g in range(GROUPS)], [held([P, HALF], U32, "z_w1_0")]]
-        z_late = [held([P, HALF // 2, PACK], BF16, "z_late0")]
+        z_second = [held([P, QUARTER, PACK], BF16, "z_second0")]
         z_s = [[held([P, HALF], U8, "z_s%d_%d" % (h, g)) for g in range(GROUPS)] for h in range(2)]
         wg_bf = [held([P, N, PACK], BF16, "wg_bf0"), placed([P, N, PACK], BF16, "wg_bf1", 0)]
         wg_w = [held([P, N], U32, "wg_w%d" % g) for g in range(GROUPS)]
@@ -226,72 +215,79 @@ def tile_list_slate_candidate_profiles_kernel(
 
         def empty(acc, h, b):
             g, c = divmod(b, PACK)
-            if for_scalar(h, g):
-                nc.scalar.activation(z_pairs[:, c // 2, :, c % 2], acc[:], ACT.Relu, scale=rec_size[:, g, c : c + 1])
-            elif h == 0 and b < 2:
-                for e in range(2):
-                    t = 2 * b + e
-                    nc.scalar.activation(z_pairs0[:, b, :, e], acc[:, QUARTER * e : QUARTER * (e + 1)], ACT.Relu, scale=rec_size[:, g, t : t + 1])
-            else:
+            if not for_scalar(h, b):
+                target, block = (z_first[g], c) if h == 0 else (z_second[c // 2], c % 2)
                 nc.vector.scalar_tensor_tensor(
-                    z_bf[h, g][:, P * c : P * (c + 1), :] if h == 0 else z_late[c // 2][:, P * (c % 2) : P * (c % 2 + 1), :],
+                    target[:, P * block : P * (block + 1), :],
                     acc[:].rearrange("p (t j) -> p j t", t=PACK),
                     0.0,
                     rec_t[:, g : g + 1, :].to_broadcast([P, P, PACK]),
                     ALU.max,
                     ALU.mult,
                 )
+            elif h == 0:
+                for e, cols in enumerate(halves(HALF)):
+                    size = rec_size[:, g, 2 * c + e : 2 * c + e + 1]
+                    nc.scalar.activation(z_pairs[h][:, c, :, e], acc[:, cols], ACT.Relu, scale=size)
+            else:
+                nc.scalar.activation(z_pairs[h][:, c // 2, :, c % 2], acc[:], ACT.Relu, scale=rec_size[:, g, c : c + 1])
+
+        def weave(fours, pairs):
+            nc.vector.tensor_tensor(
+                fours.rearrange("p j (u e) -> p j u e", e=2),
+                pairs.rearrange("p u j e -> p j u e"),
+                rec_sign[:, SCALAR_GROUP : SCALAR_GROUP + 1, :, :].to_broadcast([P, QUARTER, 2, 2]),
+                ALU.mult,
+            )
 
         second = {}
-        for n in range(BANKS):
-            empty(first[FIRST_ORDER[n]], 0, FIRST_ORDER[n])
-            b = SECOND_ORDER[n]
-            second[b] = bank(n, "second%d" % b)
+        for n, (b_first, b_second) in enumerate(zip(FIRST_PIECES, SECOND_PIECES)):
+            empty(first[b_first], 0, b_first)
+            second[b_second] = bank(n, "second%d" % b_second)
             for a in range(K_PASSES):
-                fill(second[b], 1, b, a)
-        nc.vector.tensor_tensor(
-            z_bf[0, 0][:, 0:QUARTER, :].rearrange("p j (u e) -> p j u e", e=2),
-            z_pairs0[:].rearrange("p u j e -> p j u e"),
-            rec_sign[:, 0:1, :, :].to_broadcast([P, QUARTER, 2, 2]),
-            ALU.mult,
-        )
-        for g, b in ((1, 4), (0, 5)):
-            quantize(z_w[0][g], z_s[0][g], z_bf[0, g])
+                fill(second[b_second], 1, b_second, a)
+        weave(z_first[SCALAR_GROUP][:, 0:QUARTER, :], z_pairs[0][:])
+        vector_pieces = range(SCALAR_PIECES[1], BANKS)
+        for g, b in zip(GROUP_ORDER, vector_pieces[:2]):
+            quantize(z_w[0][g], z_s[0][g], z_first[g])
             empty(second[b], 1, b)
 
         for g in range(GROUPS):
-            for cols in halves(N):
-                if g == 0 and cols.start == 0:
+            for part, cols in enumerate(halves(N)):
+                if (g, part) == (0, 0):
                     nc.gpsimd.tensor_scalar(
-                        wg_bf[g][:, cols, :], wg_rows[:, g, :, cols].rearrange("p t n -> p n t"), 1.0, 0.0, ALU.mult, ALU.add
+                        wg_bf[g][:, cols, :],
+                        wg_rows[:, g, :, cols].rearrange("p t n -> p n t"),
+                        1.0,
+                        0.0,
+                        ALU.mult,
+                        ALU.add,
                     )
-                    continue
-                nc.scalar.copy(
-                    wg_bf[g][:, cols, :].rearrange("p (c r) t -> p c t r", r=RUN),
-                    wg_rows[:, g, :, cols].rearrange("p t (c r) -> p c t r", r=RUN),
-                )
+                else:
+                    nc.scalar.copy(
+                        wg_bf[g][:, cols, :].rearrange("p (c r) t -> p c t r", r=RUN),
+                        wg_rows[:, g, :, cols].rearrange("p t (c r) -> p c t r", r=RUN),
+                    )
         for g in range(GROUPS):
             quantize(wg_w[g], wg_s[g], wg_bf[g])
-        z_pairs = held([P, 2, HALF, 2], BF16, "z_pairs", after="tab2_w0")
+        z_pairs.append(held([P, 2, HALF, 2], BF16, "z_pairs1", after="tab2_w0"))
         bg_t = held([P, N_TILES], F32, "bg_t", after="v_w0_0")
         with nc.allow_non_contiguous_dma(reason="one bias value to a partition"):
             nc.sync.dma_start(bg_t[:], bg.rearrange("(c p) -> p c", p=P))
 
-        z_late.append(placed([P, HALF // 2, PACK], BF16, "z_late1", 2 * HALF))
+        middle = 2 * HALF
+        z_second.append(placed([P, QUARTER, PACK], BF16, "z_second1", middle))
         z_w[1].append(held([P, HALF], U32, "z_w1_1", after="wg_bf0"))
-        for b in (0, 1, 2, 3, 6, 7):
+        for b in [*range(SCALAR_PIECES[1]), *vector_pieces[2:]]:
             empty(second[b], 1, b)
         for part, cols in enumerate(halves(HALF)):
-            quantize(z_w[1][1][:, cols], z_s[1][1][:, cols], z_late[part])
-        woven = [held([P, QUARTER, PACK], BF16, "woven0", after="z_late0"), placed([P, QUARTER, PACK], BF16, "woven1", 2 * HALF)]
+            quantize(z_w[1][1][:, cols], z_s[1][1][:, cols], z_second[part])
+        woven = [
+            held([P, QUARTER, PACK], BF16, "woven0", after="z_second0"),
+            placed([P, QUARTER, PACK], BF16, "woven1", middle),
+        ]
         for part, cols in enumerate(halves(HALF)):
-            nc.vector.tensor_tensor(
-                woven[part][:].rearrange("p j (u e) -> p j u e", e=2),
-                z_pairs[:, :, cols, :].rearrange("p u j e -> p j u e"),
-                rec_sign[:, SCALAR_GROUP : SCALAR_GROUP + 1, :, :].to_broadcast([P, QUARTER, 2, 2]),
-                ALU.mult,
-            )
-        group_order = [(1, 0), (1, 0)]
+            weave(woven[part][:], z_pairs[1][:, :, cols, :])
         for part, cols in enumerate(halves(HALF)):
             quantize(z_w[1][0][:, cols], z_s[1][0][:, cols], woven[part])
 
@@ -300,8 +296,8 @@ def tile_list_slate_candidate_profiles_kernel(
         ]
         wg_operand = [(wg_w[g][:].bitcast(FP8X4), wg_s[g][:]) for g in range(GROUPS)]
 
-        def profile(acc, operand, h, c, groups=None, cols=slice(0, HALF)):
-            for g in groups or group_order[h]:
+        def profile(acc, operand, h, c, groups=GROUP_ORDER, cols=slice(0, HALF)):
+            for g in groups:
                 words, scales = operand[g]
                 nc.tensor.matmul_mx(
                     out=acc[:, cols],
@@ -309,25 +305,19 @@ def tile_list_slate_candidate_profiles_kernel(
                     lhsT_scale=scales[:, P * c : P * (c + 1)],
                     rhs=z_w[h][g][:, cols].bitcast(FP8X4),
                     rhs_scale=z_s[h][g][:, cols],
-                    start=(g == group_order[h][0]),
-                    stop=(g == group_order[h][-1] and cols.stop == HALF),
+                    start=(g == GROUP_ORDER[0]),
+                    stop=(g == GROUP_ORDER[-1] and cols.stop == HALF),
                 )
 
         def gate_and_store(h, c, y_sum, gate_sum):
             gate = ring.tile([P, HALF], F32, name="gate")
             nc.scalar.activation(gate[:], gate_sum[:], ACT.Sigmoid, bias=bg_t[:, c : c + 1])
             if (h, c) == (0, 0):
-                result = placed([P, HALF], F32, "result_first", 0)
+                result = placed([P, HALF], F32, "result_low", 0)
             elif (h, c) == (0, N_TILES - 1):
-                result = placed([P, HALF], F32, "result_pool", 4 * HALF)
+                result = placed([P, HALF], F32, "result_high", 2 * middle)
             else:
                 result = ring.tile([P, HALF], F32, name="result")
-            if (h, c) == (0, N_TILES - 1):
-                y_copy = held([P, HALF], F32, "y_copy")
-                nc.scalar.copy(y_copy[:], y_sum[:])
-                nc.gpsimd.tensor_tensor(result[:], y_copy[:], gate[:], ALU.mult)
-                nc.sync.dma_start(out[P * c : P * (c + 1), 0:HALF], result[:])
-                return
             is_last = h == 1 and c == N_TILES - 1
             for cols in halves(HALF) if is_last else [slice(0, HALF)]:
                 nc.vector.tensor_tensor(result[:, cols], y_sum[:, cols], gate[:, cols], ALU.mult)
@@ -335,13 +325,13 @@ def tile_list_slate_candidate_profiles_kernel(
                     out[P * c : P * (c + 1), HALF * h + cols.start : HALF * h + cols.stop], result[:, cols]
                 )
 
-        y_banks, gate_banks = [SECOND_ORDER.index(b) for b in (4, 0, 5, 1)], [SECOND_ORDER.index(b) for b in (2, 3, 6, 7)]
+        y_banks, gate_banks = range(N_TILES), range(N_TILES, BANKS)
         y_first = [bank(y_banks[c], "y0_%d" % c) for c in range(N_TILES)]
         gate_first = [bank(gate_banks[c], "gate0_%d" % c) for c in range(N_TILES)]
-        for g in group_order[0]:
-            for c in range(2):
+        for g in GROUP_ORDER:
+            for c in range(N_TILES // 2):
                 profile(y_first[c], attr_operand, 0, c, [g])
-        for c in range(2, N_TILES):
+        for c in range(N_TILES // 2, N_TILES):
             profile(y_first[c], attr_operand, 0, c)
         for c in range(N_TILES):
             profile(gate_first[c], wg_operand, 0, c)
@@ -351,10 +341,10 @@ def tile_list_slate_candidate_profiles_kernel(
         y_second = [bank(y_banks[c], "y1_%d" % c) for c in range(N_TILES)]
         gate_second = [bank(gate_banks[c], "gate1_%d" % c) for c in range(N_TILES)]
         for c in range(N_TILES):
-            profile(gate_second[c], wg_operand, 1, c, [1])
+            profile(gate_second[c], wg_operand, 1, c, GROUP_ORDER[:1])
         for cols in halves(HALF):
             for c in range(N_TILES):
-                profile(gate_second[c], wg_operand, 1, c, [0], cols)
+                profile(gate_second[c], wg_operand, 1, c, GROUP_ORDER[1:], cols)
         for c in range(N_TILES):
             profile(y_second[c], attr_operand, 1, c)
             gate_and_store(1, c, y_second[c], gate_second[c])

@@ -34,11 +34,9 @@ RUN = 4
 FIRST_ROW = P - QUAD
 PLANE_ROW = (12, 0)
 
-SCALAR_GROUP = 0
-SCALAR_PIECES = (2, 4)
-FIRST_PIECES = (0, 1, 4, 5, 2, 3, 6, 7)
-SECOND_PIECES = (4, 0, 5, 1, 2, 3, 6, 7)
-GROUP_ORDER = (1, 0)
+SCALAR_GROUP, VECTOR_GROUP = 0, 1
+GROUP_ORDER = (VECTOR_GROUP, SCALAR_GROUP)
+KIB = 1024
 
 
 def tile_list_slate_candidate_profiles_kernel(
@@ -65,8 +63,8 @@ def tile_list_slate_candidate_profiles_kernel(
 
         idx = keep.tile([P, S // 16], U16, name="idx")
         idx2 = keep.tile([P, S2 // 16], U16, name="idx2")
-        tab_w = [held([P, T], I32, "tab_w%d" % a) for a in range(K_PASSES)]
-        tab2_w = [held([P, T2], I32, "tab2_w0")]
+        tab_w = [held([P, T], I32, "tab_w0"), placed([P, T], I32, "tab_w1", 8 * KIB)]
+        tab2_w = [placed([P, T2], I32, "tab2_w0", 0)]
         tab_s = held([P, T // 4], I32, "tab_s")
         tab2_s = held([P, T2 // 4], I32, "tab2_s")
 
@@ -132,27 +130,26 @@ def tile_list_slate_candidate_profiles_kernel(
                 v2_w[a][:, j0 : j0 + width], tab2_w[a][:].bitcast(U32).indirect(idx2[:, list_cols(j0, width)])
             )
 
+        def load_wg(tile, g, cols):
+            nc.sync.dma_start(tile[:], wg[PASS * g : PASS * (g + 1), cols].rearrange("(p t) n -> p t n", t=PACK))
+
+        low, high = halves(N)
         gather_v2(0, 0, S2)
-        wg_rows = held([P, GROUPS, PACK, N], F32, "wg_rows", after="tab2_w0")
+        wg_low = [placed([P, PACK, N // 2], F32, "wg_low%d" % g, 4 * KIB * g) for g in range(GROUPS)]
         for g in range(GROUPS):
-            nc.sync.dma_start(
-                wg_rows[:, g, :, :], wg[PASS * g : PASS * (g + 1), :].rearrange("(p t) n -> p t n", t=PACK)
-            )
+            load_wg(wg_low[g], g, low)
 
         for g in range(GROUPS):
             gather_v(0, g)
         attr_w = held([P, GROUPS, 2 * N // 4], I32, "attr_w", after="tab_w0")
         nc.sync.dma_start(attr_w[:], attr_words.bitcast(I32).rearrange("g p n -> p g n"))
 
-        rec_sign = held([P, GROUPS, 2, 2], BF16, "rec_sign")
-        rec_size = held([P, GROUPS, PACK], F32, "rec_size")
+        rec_sign = held([P, 2, 2], BF16, "rec_sign")
+        rec_size = held([P, PACK], F32, "rec_size")
         warm = held([P, 1], F32, "warm")
         nc.scalar.activation(warm[:], rec_t[:, 0, 0:1], ACT.Sigmoid)
-        nc.scalar.activation(rec_sign[:].rearrange("p g u e -> p g (u e)"), rec_t[:], ACT.Sign)
-        nc.scalar.activation(rec_size[:], rec_t[:], ACT.Abs)
-
-        def for_scalar(h, b):
-            return b < SCALAR_PIECES[h]
+        nc.scalar.activation(rec_sign[:].rearrange("p u e -> p (u e)"), rec_t[:, SCALAR_GROUP, :], ACT.Sign)
+        nc.scalar.activation(rec_size[:], rec_t[:, SCALAR_GROUP, :], ACT.Abs)
 
         def score(acc, g, t, a, j0, width, start, stop):
             m0 = PASS * g + P * t
@@ -166,57 +163,67 @@ def tile_list_slate_candidate_profiles_kernel(
                 stop=stop,
             )
 
-        def fill(acc, h, b, a, opens=0):
-            g, c = divmod(b, PACK)
+        def fill(acc, h, piece, a, opens=0):
+            g, c = piece
             first_pass, last_pass = a == opens, a != opens
-            if not for_scalar(h, b):
+            if g == VECTOR_GROUP:
                 for t in range(PACK):
                     start, stop = first_pass and t == 0, last_pass and t == PACK - 1
                     score(acc[:, P * t : P * (t + 1)], g, t, a, HALF * h + P * c, P, start, stop)
             elif h == 0:
+                part, u = divmod(c, 2)
                 for e, cols in enumerate(halves(HALF)):
-                    score(acc[:, cols], g, 2 * c + e, a, 0, QUARTER, first_pass and e == 0, last_pass and e == 1)
+                    start, stop = first_pass and e == 0, last_pass and e == 1
+                    score(acc[:, cols], g, 2 * u + e, a, QUARTER * part, QUARTER, start, stop)
             else:
                 score(acc[:], g, c, a, HALF * h, HALF, first_pass, last_pass)
 
-        first = {b: bank(n, "first%d" % b) for n, b in enumerate(FIRST_PIECES)}
-        last_piece = FIRST_PIECES[-1]
-        for b in FIRST_PIECES[:-1]:
-            fill(first[b], 0, b, 0)
+        s_piece = [(SCALAR_GROUP, c) for c in range(PACK)]
+        v_piece = [(VECTOR_GROUP, c) for c in range(PACK)]
+        first_pieces = s_piece[:2] + v_piece[:2] + s_piece[2:] + v_piece[2:]
+        first = {piece: bank(n, "first%d" % n) for n, piece in enumerate(first_pieces)}
+        late_pieces = v_piece[2:]
+        for piece in first_pieces[:-2]:
+            fill(first[piece], 0, piece, 0)
         for g in range(GROUPS):
             gather_v(1, g)
         for part, pieces in enumerate(halves(BANKS)):
             gather_v2(1, QUARTER * part, QUARTER)
-            for b in FIRST_PIECES[pieces]:
-                fill(first[b], 0, b, 1, opens=int(b == last_piece))
-        fill(first[last_piece], 0, last_piece, 0, opens=1)
+            for piece in first_pieces[pieces]:
+                fill(first[piece], 0, piece, 1, opens=int(piece in late_pieces))
+                if piece in late_pieces:
+                    fill(first[piece], 0, piece, 0, opens=1)
         gather_v2(1, HALF, HALF)
-        attr_s = held([P, GROUPS, N // 4], I32, "attr_s", after="tab_w1")
+        attr_s = placed([P, GROUPS, N // 4], I32, "attr_s", 8 * KIB)
         nc.gpsimd.memset(attr_s[:], 0)
         for q in range(QUADRANTS):
             nc.sync.dma_start(
                 attr_s[QUAD * q : QUAD * q + ROWS, :, :],
                 attr_scales[:, ROWS * q : ROWS * (q + 1), :].bitcast(I32).rearrange("g s n -> s g n"),
             )
+        wg_high = [placed([P, PACK, N // 2], F32, "wg_high%d" % g, 12 * KIB + 4 * KIB * g) for g in range(GROUPS)]
+        for g in range(GROUPS):
+            load_wg(wg_high[g], g, high)
+        bg_t = held([P, N_TILES], F32, "bg_t", after="v_w0_0")
 
-        z_pairs = [held([P, 2, QUARTER, 2], BF16, "z_pairs0")]
-        z_first = [held([P, HALF, PACK], BF16, "z_first%d" % g) for g in range(GROUPS)]
-        z_w = [[held([P, HALF], U32, "z_w0_%d" % g) for g in range(GROUPS)], [held([P, HALF], U32, "z_w1_0")]]
+        z_pairs = [held([P, 2, HALF, 2], BF16, "z_pairs%d" % h) for h in range(2)]
+        z_plain = held([P, HALF, PACK], BF16, "z_plain")
         z_second = [held([P, QUARTER, PACK], BF16, "z_second0")]
         z_s = [[held([P, HALF], U8, "z_s%d_%d" % (h, g)) for g in range(GROUPS)] for h in range(2)]
-        wg_bf = [held([P, N, PACK], BF16, "wg_bf0"), placed([P, N, PACK], BF16, "wg_bf1", 0)]
-        wg_w = [held([P, N], U32, "wg_w%d" % g) for g in range(GROUPS)]
-        wg_s = [held([P, N], U8, "wg_s%d" % g) for g in range(GROUPS)]
+        wg_bf = [held([P, GROUPS, N // 2, PACK], BF16, "wg_bf0"), placed([P, GROUPS, N // 2, PACK], BF16, "wg_bf1", 24 * KIB)]
+        wg_w = [held([P, N], U32, "wg_w%d" % part) for part in range(2)]
+        wg_s = [held([P, N], U8, "wg_s%d" % part) for part in range(2)]
 
         def quantize(words, scales, side_by_side):
-            nc.vector.quantize_mx(
-                out=words[:].bitcast(FP8X4), scales=scales[:], in_=side_by_side[:].rearrange("p w t -> p (w t)")
-            )
+            nc.vector.quantize_mx(out=words.bitcast(FP8X4), scales=scales, in_=side_by_side)
 
-        def empty(acc, h, b):
-            g, c = divmod(b, PACK)
-            if not for_scalar(h, b):
-                target, block = (z_first[g], c) if h == 0 else (z_second[c // 2], c % 2)
+        def flat(tile):
+            return tile[:].rearrange("p w t -> p (w t)")
+
+        def empty(acc, h, piece):
+            g, c = piece
+            if g == VECTOR_GROUP:
+                target, block = (z_plain, c) if h == 0 else (z_second[c // 2], c % 2)
                 nc.vector.scalar_tensor_tensor(
                     target[:, P * block : P * (block + 1), :],
                     acc[:].rearrange("p (t j) -> p j t", t=PACK),
@@ -226,125 +233,154 @@ def tile_list_slate_candidate_profiles_kernel(
                     ALU.mult,
                 )
             elif h == 0:
+                part, u = divmod(c, 2)
                 for e, cols in enumerate(halves(HALF)):
-                    size = rec_size[:, g, 2 * c + e : 2 * c + e + 1]
-                    nc.scalar.activation(z_pairs[h][:, c, :, e], acc[:, cols], ACT.Relu, scale=size)
+                    nc.scalar.activation(
+                        z_pairs[h][:, u, QUARTER * part : QUARTER * (part + 1), e],
+                        acc[:, cols],
+                        ACT.Relu,
+                        scale=rec_size[:, 2 * u + e : 2 * u + e + 1],
+                    )
             else:
-                nc.scalar.activation(z_pairs[h][:, c // 2, :, c % 2], acc[:], ACT.Relu, scale=rec_size[:, g, c : c + 1])
+                nc.scalar.activation(z_pairs[h][:, c // 2, :, c % 2], acc[:], ACT.Relu, scale=rec_size[:, c : c + 1])
 
-        def weave(fours, pairs):
+        def weave(fours, pairs, width):
             nc.vector.tensor_tensor(
                 fours.rearrange("p j (u e) -> p j u e", e=2),
                 pairs.rearrange("p u j e -> p j u e"),
-                rec_sign[:, SCALAR_GROUP : SCALAR_GROUP + 1, :, :].to_broadcast([P, QUARTER, 2, 2]),
+                rec_sign[:].unsqueeze(1).to_broadcast([P, width, 2, 2]),
                 ALU.mult,
             )
 
-        second = {}
-        for n, (b_first, b_second) in enumerate(zip(FIRST_PIECES, SECOND_PIECES)):
-            empty(first[b_first], 0, b_first)
-            second[b_second] = bank(n, "second%d" % b_second)
+        for g in range(GROUPS):
+            nc.gpsimd.tensor_scalar(
+                wg_bf[0][:, g, :, :], wg_low[g][:].rearrange("p t n -> p n t"), 1.0, 0.0, ALU.mult, ALU.add
+            )
+
+        freed = (0, 1, 2, 3, 4, 6, 5, 7)
+        second_pieces = [v_piece[0], s_piece[0], v_piece[1], s_piece[1], s_piece[2], s_piece[3], v_piece[2], v_piece[3]]
+        second, second_bank = {}, {}
+        for n, piece in zip(freed, second_pieces):
+            empty(first[first_pieces[n]], 0, first_pieces[n])
+            second[piece] = bank(n, "second%d" % n)
+            second_bank[piece] = n
             for a in range(K_PASSES):
-                fill(second[b_second], 1, b_second, a)
-        weave(z_first[SCALAR_GROUP][:, 0:QUARTER, :], z_pairs[0][:])
-        vector_pieces = range(SCALAR_PIECES[1], BANKS)
-        for g, b in zip(GROUP_ORDER, vector_pieces[:2]):
-            quantize(z_w[0][g], z_s[0][g], z_first[g])
-            empty(second[b], 1, b)
+                fill(second[piece], 1, piece, a)
+        for piece in v_piece[:2] + s_piece:
+            empty(second[piece], 1, piece)
+
+        z_w = [
+            [held([P, HALF], U32, "z_w0_0"), placed([P, HALF], U32, "z_w0_1", 6 * KIB)],
+            [held([P, HALF], U32, "z_w1_%d" % g) for g in range(GROUPS)],
+        ]
+        woven_first = placed([P, HALF, PACK], BF16, "woven_first", 2 * KIB)
+        quantize(z_w[0][VECTOR_GROUP][:], z_s[0][VECTOR_GROUP][:], flat(z_plain))
+        z_second.append(held([P, QUARTER, PACK], BF16, "z_second1", after="z_plain"))
+        weave(woven_first[:], z_pairs[0][:], HALF)
+        empty(second[v_piece[2]], 1, v_piece[2])
+        quantize(z_w[0][SCALAR_GROUP][:], z_s[0][SCALAR_GROUP][:], flat(woven_first))
+        empty(second[v_piece[3]], 1, v_piece[3])
+        quantize(wg_w[0][:], wg_s[0][:], wg_bf[0][:].rearrange("p g n t -> p (g n t)"))
+
+        woven = [held([P, QUARTER, PACK], BF16, "woven0"), placed([P, QUARTER, PACK], BF16, "woven1", 28 * KIB)]
+        parts = halves(HALF)
+        weave(woven[0][:], z_pairs[1][:, :, parts[0], :], QUARTER)
+        for part, cols in enumerate(parts):
+            quantize(z_w[1][VECTOR_GROUP][:, cols], z_s[1][VECTOR_GROUP][:, cols], flat(z_second[part]))
+        weave(woven[1][:], z_pairs[1][:, :, parts[1], :], QUARTER)
+        for part, cols in enumerate(parts):
+            quantize(z_w[1][SCALAR_GROUP][:, cols], z_s[1][SCALAR_GROUP][:, cols], flat(woven[part]))
 
         for g in range(GROUPS):
-            for part, cols in enumerate(halves(N)):
-                if (g, part) == (0, 0):
-                    nc.gpsimd.tensor_scalar(
-                        wg_bf[g][:, cols, :],
-                        wg_rows[:, g, :, cols].rearrange("p t n -> p n t"),
-                        1.0,
-                        0.0,
-                        ALU.mult,
-                        ALU.add,
-                    )
-                else:
-                    nc.scalar.copy(
-                        wg_bf[g][:, cols, :].rearrange("p (c r) t -> p c t r", r=RUN),
-                        wg_rows[:, g, :, cols].rearrange("p t (c r) -> p c t r", r=RUN),
-                    )
-        for g in range(GROUPS):
-            quantize(wg_w[g], wg_s[g], wg_bf[g])
-        z_pairs.append(held([P, 2, HALF, 2], BF16, "z_pairs1", after="tab2_w0"))
-        bg_t = held([P, N_TILES], F32, "bg_t", after="v_w0_0")
+            nc.scalar.copy(
+                wg_bf[1][:, g, :, :].rearrange("p (c r) t -> p c t r", r=RUN),
+                wg_high[g][:].rearrange("p t (c r) -> p c t r", r=RUN),
+            )
+        quantize(wg_w[1][:], wg_s[1][:], wg_bf[1][:].rearrange("p g n t -> p (g n t)"))
         with nc.allow_non_contiguous_dma(reason="one bias value to a partition"):
             nc.sync.dma_start(bg_t[:], bg.rearrange("(c p) -> p c", p=P))
 
-        middle = 2 * HALF
-        z_second.append(placed([P, QUARTER, PACK], BF16, "z_second1", middle))
-        z_w[1].append(held([P, HALF], U32, "z_w1_1", after="wg_bf0"))
-        for b in [*range(SCALAR_PIECES[1]), *vector_pieces[2:]]:
-            empty(second[b], 1, b)
-        for part, cols in enumerate(halves(HALF)):
-            quantize(z_w[1][1][:, cols], z_s[1][1][:, cols], z_second[part])
-        woven = [
-            held([P, QUARTER, PACK], BF16, "woven0", after="z_second0"),
-            placed([P, QUARTER, PACK], BF16, "woven1", middle),
-        ]
-        for part, cols in enumerate(halves(HALF)):
-            weave(woven[part][:], z_pairs[1][:, :, cols, :])
-        for part, cols in enumerate(halves(HALF)):
-            quantize(z_w[1][0][:, cols], z_s[1][0][:, cols], woven[part])
+        def attr_operand(g, c):
+            cols = slice(P * c, P * (c + 1))
+            return attr_w[:, g, :].bitcast(U8).bitcast(FP4X4)[:, cols], attr_s[:, g, :].bitcast(U8)[:, cols]
 
-        attr_operand = [
-            (attr_w[:, g, :].bitcast(U8).bitcast(FP4X4), attr_s[:, g, :].bitcast(U8)) for g in range(GROUPS)
-        ]
-        wg_operand = [(wg_w[g][:].bitcast(FP8X4), wg_s[g][:]) for g in range(GROUPS)]
+        def wg_operand(g, c):
+            part, m = divmod(c, 2)
+            cols = slice(N // 2 * g + P * m, N // 2 * g + P * (m + 1))
+            return wg_w[part][:, cols].bitcast(FP8X4), wg_s[part][:, cols]
 
         def profile(acc, operand, h, c, groups=GROUP_ORDER, cols=slice(0, HALF)):
             for g in groups:
-                words, scales = operand[g]
+                words, scales = operand(g, c)
                 nc.tensor.matmul_mx(
                     out=acc[:, cols],
-                    lhsT=words[:, P * c : P * (c + 1)],
-                    lhsT_scale=scales[:, P * c : P * (c + 1)],
+                    lhsT=words,
+                    lhsT_scale=scales,
                     rhs=z_w[h][g][:, cols].bitcast(FP8X4),
                     rhs_scale=z_s[h][g][:, cols],
                     start=(g == GROUP_ORDER[0]),
-                    stop=(g == GROUP_ORDER[-1] and cols.stop == HALF),
+                    stop=(g == GROUP_ORDER[-1]),
                 )
 
-        def gate_and_store(h, c, y_sum, gate_sum):
-            gate = ring.tile([P, HALF], F32, name="gate")
-            nc.scalar.activation(gate[:], gate_sum[:], ACT.Sigmoid, bias=bg_t[:, c : c + 1])
+        gates = {}
+
+        def sigmoid(h, c, gate_sum, cols=slice(0, HALF)):
+            if cols.start == 0:
+                gates[h, c] = ring.tile([P, HALF], F32, name="gate")
+            nc.scalar.activation(gates[h, c][:, cols], gate_sum[:, cols], ACT.Sigmoid, bias=bg_t[:, c : c + 1])
+
+        def store(h, c, y_sum, cols=slice(0, HALF)):
             if (h, c) == (0, 0):
-                result = placed([P, HALF], F32, "result_low", 0)
-            elif (h, c) == (0, N_TILES - 1):
-                result = placed([P, HALF], F32, "result_high", 2 * middle)
+                result = placed([P, HALF], F32, "result_first", 27 * KIB)
             else:
                 result = ring.tile([P, HALF], F32, name="result")
-            is_last = h == 1 and c == N_TILES - 1
-            for cols in halves(HALF) if is_last else [slice(0, HALF)]:
-                nc.vector.tensor_tensor(result[:, cols], y_sum[:, cols], gate[:, cols], ALU.mult)
-                nc.sync.dma_start(
-                    out[P * c : P * (c + 1), HALF * h + cols.start : HALF * h + cols.stop], result[:, cols]
-                )
+            nc.vector.tensor_tensor(result[:, cols], y_sum[:, cols], gates[h, c][:, cols], ALU.mult)
+            nc.sync.dma_start(out[P * c : P * (c + 1), HALF * h + cols.start : HALF * h + cols.stop], result[:, cols])
 
-        y_banks, gate_banks = range(N_TILES), range(N_TILES, BANKS)
-        y_first = [bank(y_banks[c], "y0_%d" % c) for c in range(N_TILES)]
-        gate_first = [bank(gate_banks[c], "gate0_%d" % c) for c in range(N_TILES)]
+        b = second_bank
+        y_sum, gate_sum = {}, {}
+        for c, piece in enumerate([s_piece[0], v_piece[0], v_piece[1], s_piece[1]]):
+            y_sum[0, c] = bank(b[piece], "y0_%d" % c)
         for g in GROUP_ORDER:
-            for c in range(N_TILES // 2):
-                profile(y_first[c], attr_operand, 0, c, [g])
-        for c in range(N_TILES // 2, N_TILES):
-            profile(y_first[c], attr_operand, 0, c)
-        for c in range(N_TILES):
-            profile(gate_first[c], wg_operand, 0, c)
-        for c in range(N_TILES):
-            gate_and_store(0, c, y_first[c], gate_first[c])
-
-        y_second = [bank(y_banks[c], "y1_%d" % c) for c in range(N_TILES)]
-        gate_second = [bank(gate_banks[c], "gate1_%d" % c) for c in range(N_TILES)]
-        for c in range(N_TILES):
-            profile(gate_second[c], wg_operand, 1, c, GROUP_ORDER[:1])
-        for cols in halves(HALF):
             for c in range(N_TILES):
-                profile(gate_second[c], wg_operand, 1, c, GROUP_ORDER[1:], cols)
-        for c in range(N_TILES):
-            profile(y_second[c], attr_operand, 1, c)
-            gate_and_store(1, c, y_second[c], gate_second[c])
+                profile(y_sum[0, c], attr_operand, 0, c, [g])
+        low_banks = [b[s_piece[2]], b[s_piece[3]]]
+        late_banks = [b[v_piece[2]], b[v_piece[3]]]
+        for c in range(2):
+            gate_sum[0, c] = bank(low_banks[c], "gate0_%d" % c)
+            profile(gate_sum[0, c], wg_operand, 0, c)
+            sigmoid(0, c, gate_sum[0, c])
+        for c in range(2):
+            gate_sum[1, c] = bank(late_banks[c], "gate1_%d" % c)
+            profile(gate_sum[1, c], wg_operand, 1, c, GROUP_ORDER[:1])
+        for c in range(2):
+            y_sum[1, c] = bank(low_banks[c], "y1_%d" % c)
+            profile(y_sum[1, c], attr_operand, 1, c, GROUP_ORDER[:1])
+        for c in range(2):
+            profile(gate_sum[1, c], wg_operand, 1, c, GROUP_ORDER[1:])
+            sigmoid(1, c, gate_sum[1, c])
+        for c in range(2):
+            profile(y_sum[1, c], attr_operand, 1, c, GROUP_ORDER[1:])
+        for h in range(2):
+            for c in range(2):
+                store(h, c, y_sum[h, c])
+        for c in range(2, N_TILES):
+            gate_sum[0, c] = bank(late_banks[c - 2], "gate0_%d" % c)
+            profile(gate_sum[0, c], wg_operand, 0, c)
+            sigmoid(0, c, gate_sum[0, c])
+        gate_sum[1, 2] = bank(b[s_piece[0]], "gate1_2")
+        profile(gate_sum[1, 2], wg_operand, 1, 2)
+        sigmoid(1, 2, gate_sum[1, 2])
+        y_sum[1, 2] = bank(b[v_piece[0]], "y1_2")
+        profile(y_sum[1, 2], attr_operand, 1, 2)
+        for n, cols in zip(low_banks, halves(HALF)):
+            last = bank(n, "gate1_3_%d" % n)
+            profile(last, wg_operand, 1, 3, cols=cols)
+            sigmoid(1, 3, last, cols)
+        for c in range(2, N_TILES):
+            store(0, c, y_sum[0, c])
+        store(1, 2, y_sum[1, 2])
+        for n, cols in zip(late_banks, halves(HALF)):
+            last = bank(n, "y1_3_%d" % n)
+            profile(last, attr_operand, 1, 3, cols=cols)
+            store(1, 3, last, cols)

@@ -63,7 +63,7 @@ def tile_list_slate_candidate_profiles_kernel(
 
         idx = keep.tile([P, S // 16], U16, name="idx")
         idx2 = keep.tile([P, S2 // 16], U16, name="idx2")
-        tab_w = [held([P, T], I32, "tab_w0"), placed([P, T], I32, "tab_w1", 8 * KIB)]
+        tab_w = [placed([P, T], I32, "tab_w0", 44 * KIB), placed([P, T], I32, "tab_w1", 8 * KIB)]
         tab2_w = [placed([P, T2], I32, "tab2_w0", 0)]
         tab_s = held([P, T // 4], I32, "tab_s")
         tab2_s = held([P, T2 // 4], I32, "tab2_s")
@@ -83,13 +83,11 @@ def tile_list_slate_candidate_profiles_kernel(
         nc.sync.dma_start(idx[:], offs)
         load_words(tab2_w[0], tab2_words, 0)
         load_words(tab_w[0], tab_words, 0)
-        rec_t = held([P, GROUPS, PACK], F32, "rec_t")
-        nc.sync.dma_start(rec_t[:], rec.rearrange("(g p t) -> p g t", g=GROUPS, t=PACK))
         load_words(tab_w[1], tab_words, 1)
 
-        v_s_listed = held([P, S], U8, "v_s_listed")
+        v_s_listed = placed([P, S], U8, "v_s_listed", 40 * KIB - S // 2)
         planes = [held([P, S + S2], U8, "planes%d" % a) for a in range(K_PASSES)]
-        nc.gpsimd.memset(planes[1][:].bitcast(I32), 0)
+        nc.vector.memset(planes[1][:].bitcast(I32), 0)
 
         def list_cols(entry, count):
             return slice(entry // PER_COLUMN, (entry + count) // PER_COLUMN)
@@ -102,19 +100,22 @@ def tile_list_slate_candidate_profiles_kernel(
             planes[0][:, 0:S].rearrange("p (g t m) -> p g t m", g=GROUPS, t=PACK),
             v_s_listed[:].rearrange("p (g m t) -> p g t m", g=GROUPS, t=PACK),
         )
-        for q in range(QUADRANTS - 1):
-            source = FIRST_ROW + ROWS * q
-            target = QUAD * q + PLANE_ROW[0]
-            nc.sync.dma_start(
-                planes[0][target : target + ROWS, :].bitcast(I32), planes[0][source : source + ROWS, :].bitcast(I32)
-            )
-        tab2_w.append(held([P, T2], I32, "tab2_w1", after="v_s_listed"))
+
+        def move_rows(a, quadrants):
+            for q in quadrants:
+                source = FIRST_ROW + ROWS * (QUADRANTS * a + q)
+                target = QUAD * q + PLANE_ROW[a]
+                nc.sync.dma_start(
+                    planes[a][target : target + ROWS, :].bitcast(I32),
+                    planes[0][source : source + ROWS, :].bitcast(I32),
+                )
+
+        move_rows(0, range(QUADRANTS - 1))
+        tab2_w.append(placed([P, T2], I32, "tab2_w1", 32 * KIB))
         load_words(tab2_w[1], tab2_words, 1)
-        for s in range(ROWS):
-            source = FIRST_ROW + ROWS * QUADRANTS + s
-            nc.sync.dma_start(
-                planes[1][PLANE_ROW[1] + s : P : QUAD, :].bitcast(I32), planes[0][source:P:ROWS, :].bitcast(I32)
-            )
+        move_rows(1, range(QUADRANTS))
+        rec_t = placed([P, GROUPS, PACK], F32, "rec_t", 40 * KIB)
+        nc.sync.dma_start(rec_t[:], rec.rearrange("(g p t) -> p g t", g=GROUPS, t=PACK))
 
         v_w = [[held([P, PASS], U32, "v_w%d_%d" % (a, g)) for g in range(GROUPS)] for a in range(K_PASSES)]
         v2_w = [held([P, S2], U32, "v2_w%d" % a) for a in range(K_PASSES)]
@@ -141,15 +142,24 @@ def tile_list_slate_candidate_profiles_kernel(
 
         for g in range(GROUPS):
             gather_v(0, g)
-        attr_w = held([P, GROUPS, 2 * N // 4], I32, "attr_w", after="tab_w0")
+        attr_w = placed([P, GROUPS, 2 * N // 4], I32, "attr_w", 44 * KIB)
         nc.sync.dma_start(attr_w[:], attr_words.bitcast(I32).rearrange("g p n -> p g n"))
+
+        attr_s = placed([P, GROUPS, N // 4], I32, "attr_s", 48 * KIB)
+        nc.vector.memset(attr_s[:], 0)
+        for q in range(QUADRANTS):
+            nc.sync.dma_start(
+                attr_s[QUAD * q : QUAD * q + ROWS, :, :],
+                attr_scales[:, ROWS * q : ROWS * (q + 1), :].bitcast(I32).rearrange("g s n -> s g n"),
+            )
 
         rec_sign = held([P, 2, 2], BF16, "rec_sign")
         rec_size = held([P, PACK], F32, "rec_size")
         warm = held([P, 1], F32, "warm")
-        nc.scalar.activation(warm[:], rec_t[:, 0, 0:1], ACT.Sigmoid)
-        nc.scalar.activation(rec_sign[:].rearrange("p u e -> p (u e)"), rec_t[:, SCALAR_GROUP, :], ACT.Sign)
+        nc.vector.memset(warm[:], 0.0)
+        nc.scalar.activation(warm[:], warm[:], ACT.Sigmoid)
         nc.scalar.activation(rec_size[:], rec_t[:, SCALAR_GROUP, :], ACT.Abs)
+        nc.scalar.activation(rec_sign[:].rearrange("p u e -> p (u e)"), rec_t[:, SCALAR_GROUP, :], ACT.Sign)
 
         def score(acc, g, t, a, j0, width, start, stop):
             m0 = PASS * g + P * t
@@ -194,13 +204,6 @@ def tile_list_slate_candidate_profiles_kernel(
                 if piece in late_pieces:
                     fill(first[piece], 0, piece, 0, opens=1)
         gather_v2(1, HALF, HALF)
-        attr_s = placed([P, GROUPS, N // 4], I32, "attr_s", 8 * KIB)
-        nc.gpsimd.memset(attr_s[:], 0)
-        for q in range(QUADRANTS):
-            nc.sync.dma_start(
-                attr_s[QUAD * q : QUAD * q + ROWS, :, :],
-                attr_scales[:, ROWS * q : ROWS * (q + 1), :].bitcast(I32).rearrange("g s n -> s g n"),
-            )
         wg_high = [placed([P, PACK, N // 2], F32, "wg_high%d" % g, 12 * KIB + 4 * KIB * g) for g in range(GROUPS)]
         for g in range(GROUPS):
             load_wg(wg_high[g], g, high)

@@ -191,6 +191,17 @@ def tile_list_slate_candidate_profiles_kernel(
         s_piece = [(SCALAR_GROUP, c) for c in range(PACK)]
         v_piece = [(VECTOR_GROUP, c) for c in range(PACK)]
         first_pieces = s_piece[:2] + v_piece[:2] + s_piece[2:] + v_piece[2:]
+        idle = bank(BANKS - 1, "idle")
+        for t in range(PACK):
+            nc.tensor.matmul_mx(
+                out=idle[:],
+                lhsT=v_w[0][0][:, P * t : P * (t + 1)].bitcast(FP8X4),
+                lhsT_scale=v2_s_listed[:, 0:P],
+                rhs=v2_w[0][:, 0:HALF].bitcast(FP8X4),
+                rhs_scale=v2_s_listed[:, 0:HALF],
+                start=True,
+                stop=True,
+            )
         first = {piece: bank(n, "first%d" % n) for n, piece in enumerate(first_pieces)}
         late_pieces = v_piece[2:]
         for piece in first_pieces[:-2]:

@@ -173,9 +173,9 @@ def tile_list_slate_candidate_profiles_kernel(
                 stop=stop,
             )
 
-        def fill(acc, h, piece, a, opens=0):
+        def fill(acc, h, piece, a):
             g, c = piece
-            first_pass, last_pass = a == opens, a != opens
+            first_pass, last_pass = a == 0, a == K_PASSES - 1
             if g == VECTOR_GROUP:
                 for t in range(PACK):
                     start, stop = first_pass and t == 0, last_pass and t == PACK - 1
@@ -203,17 +203,14 @@ def tile_list_slate_candidate_profiles_kernel(
                 stop=True,
             )
         first = {piece: bank(n, "first%d" % n) for n, piece in enumerate(first_pieces)}
-        late_pieces = v_piece[2:]
-        for piece in first_pieces[:-2]:
+        for piece in first_pieces:
             fill(first[piece], 0, piece, 0)
         for g in range(GROUPS):
             gather_v(1, g)
         for part, pieces in enumerate(halves(BANKS)):
             gather_v2(1, QUARTER * part, QUARTER)
             for piece in first_pieces[pieces]:
-                fill(first[piece], 0, piece, 1, opens=int(piece in late_pieces))
-                if piece in late_pieces:
-                    fill(first[piece], 0, piece, 0, opens=1)
+                fill(first[piece], 0, piece, 1)
         gather_v2(1, HALF, HALF)
         wg_high = [placed([P, PACK, N // 2], F32, "wg_high%d" % g, 12 * KIB + 4 * KIB * g) for g in range(GROUPS)]
         for g in range(GROUPS):

@@ -101,19 +101,19 @@ def tile_list_slate_candidate_profiles_kernel(
             v_s_listed[:].rearrange("p (g m t) -> p g t m", g=GROUPS, t=PACK),
         )
 
-        def move_rows(a, quadrants):
+        def move_rows(a, quadrants, cols):
             for q in quadrants:
                 source = FIRST_ROW + ROWS * (QUADRANTS * a + q)
                 target = QUAD * q + PLANE_ROW[a]
                 nc.sync.dma_start(
-                    planes[a][target : target + ROWS, :].bitcast(I32),
-                    planes[0][source : source + ROWS, :].bitcast(I32),
+                    planes[a][target : target + ROWS, cols].bitcast(I32),
+                    planes[0][source : source + ROWS, cols].bitcast(I32),
                 )
 
-        move_rows(0, range(QUADRANTS - 1))
+        move_rows(0, range(QUADRANTS - 1), slice(0, S + HALF))
         tab2_w.append(placed([P, T2], I32, "tab2_w1", 32 * KIB))
         load_words(tab2_w[1], tab2_words, 1)
-        move_rows(1, range(QUADRANTS))
+        move_rows(1, (2, 3, 0, 1), slice(0, S + S2))
         rec_t = placed([P, GROUPS, PACK], F32, "rec_t", 40 * KIB)
         nc.sync.dma_start(rec_t[:], rec.rearrange("(g p t) -> p g t", g=GROUPS, t=PACK))
 
@@ -132,16 +132,19 @@ def tile_list_slate_candidate_profiles_kernel(
             )
 
         def load_wg(tile, g, cols):
-            nc.sync.dma_start(tile[:], wg[PASS * g : PASS * (g + 1), cols].rearrange("(p t) n -> p t n", t=PACK))
+            nc.sync.dma_start(tile, wg[PASS * g : PASS * (g + 1), cols].rearrange("(p t) n -> p t n", t=PACK))
 
         low, high = halves(N)
         gather_v2(0, 0, S2)
         wg_low = [placed([P, PACK, N // 2], F32, "wg_low%d" % g, 4 * KIB * g) for g in range(GROUPS)]
-        for g in range(GROUPS):
-            load_wg(wg_low[g], g, low)
+        load_wg(wg_low[0][:], 0, low)
+        move_rows(0, range(QUADRANTS - 1), slice(S + HALF, S + S2))
+        load_wg(wg_low[1][:], 1, low)
 
         for g in range(GROUPS):
             gather_v(0, g)
+        wg_high = [placed([P, PACK, N // 2], F32, "wg_high0", 52 * KIB)]
+        load_wg(wg_high[0][:], 0, high)
         attr_w = placed([P, GROUPS, 2 * N // 4], I32, "attr_w", 44 * KIB)
         nc.sync.dma_start(attr_w[:], attr_words.bitcast(I32).rearrange("g p n -> p g n"))
 
@@ -154,11 +157,11 @@ def tile_list_slate_candidate_profiles_kernel(
             )
 
         rec_sign = held([P, 2, 2], BF16, "rec_sign")
-        rec_size = held([P, PACK], F32, "rec_size")
+        rec_size = shared.tile([P, 4 * PACK], F32, name="rec_size", offset=62 * KIB - 32, align_bytes=32)
         warm = held([P, 1], F32, "warm")
         nc.vector.memset(warm[:], 0.0)
         nc.scalar.activation(warm[:], warm[:], ACT.Sigmoid)
-        nc.scalar.activation(rec_size[:], rec_t[:, SCALAR_GROUP, :], ACT.Abs)
+        nc.scalar.activation(rec_size[:, 0:PACK], rec_t[:, SCALAR_GROUP, :], ACT.Abs)
         nc.scalar.activation(rec_sign[:].rearrange("p u e -> p (u e)"), rec_t[:, SCALAR_GROUP, :], ACT.Sign)
 
         def score(acc, g, t, a, j0, width, start, stop):
@@ -212,18 +215,19 @@ def tile_list_slate_candidate_profiles_kernel(
             for piece in first_pieces[pieces]:
                 fill(first[piece], 0, piece, 1)
         gather_v2(1, HALF, HALF)
-        wg_high = [placed([P, PACK, N // 2], F32, "wg_high%d" % g, 12 * KIB + 4 * KIB * g) for g in range(GROUPS)]
-        for g in range(GROUPS):
-            load_wg(wg_high[g], g, high)
+        wg_high.append(placed([P, PACK, N // 2], F32, "wg_high1", 12 * KIB))
+        load_wg(wg_high[1][:], 1, high)
         bg_t = held([P, N_TILES], F32, "bg_t", after="v_w0_0")
 
         z_pairs = [held([P, 2, HALF, 2], BF16, "z_pairs%d" % h) for h in range(2)]
         z_plain = held([P, HALF, PACK], BF16, "z_plain")
         z_second = [held([P, QUARTER, PACK], BF16, "z_second0")]
         z_s = [[held([P, HALF], U8, "z_s%d_%d" % (h, g)) for g in range(GROUPS)] for h in range(2)]
-        wg_bf = [held([P, GROUPS, N // 2, PACK], BF16, "wg_bf0"), placed([P, GROUPS, N // 2, PACK], BF16, "wg_bf1", 24 * KIB)]
-        wg_w = [held([P, N], U32, "wg_w%d" % part) for part in range(2)]
-        wg_s = [held([P, N], U8, "wg_s%d" % part) for part in range(2)]
+        wg_bf = held([P, GROUPS, N // 2, PACK], BF16, "wg_bf")
+        early_bf = held([P, P, PACK], BF16, "early_bf")
+        wg_s = held([P, N], U8, "wg_s")
+        late_w = []
+        late_s = [held([P, GROUPS * P], U8, "late_s%d" % m) for m in range(2)]
 
         def quantize(words, scales, side_by_side):
             nc.vector.quantize_mx(out=words.bitcast(FP8X4), scales=scales, in_=side_by_side)
@@ -265,8 +269,12 @@ def tile_list_slate_candidate_profiles_kernel(
 
         for g in range(GROUPS):
             nc.gpsimd.tensor_scalar(
-                wg_bf[0][:, g, :, :], wg_low[g][:].rearrange("p t n -> p n t"), 1.0, 0.0, ALU.mult, ALU.add
+                wg_bf[:, g, :, :], wg_low[g][:].rearrange("p t n -> p n t"), 1.0, 0.0, ALU.mult, ALU.add
             )
+
+        nc.gpsimd.tensor_scalar(
+            early_bf[:], wg_high[0][:, :, 0:P].rearrange("p t n -> p n t"), 1.0, 0.0, ALU.mult, ALU.add
+        )
 
         freed = (0, 1, 2, 3, 4, 6, 5, 7)
         second_pieces = [v_piece[0], s_piece[0], v_piece[1], s_piece[1], s_piece[2], s_piece[3], v_piece[2], v_piece[3]]
@@ -291,7 +299,8 @@ def tile_list_slate_candidate_profiles_kernel(
         empty(second[v_piece[2]], 1, v_piece[2])
         quantize(z_w[0][SCALAR_GROUP][:], z_s[0][SCALAR_GROUP][:], flat(woven_first))
         empty(second[v_piece[3]], 1, v_piece[3])
-        quantize(wg_w[0][:], wg_s[0][:], wg_bf[0][:].rearrange("p g n t -> p (g n t)"))
+        wg_w = placed([P, N], U32, "wg_w", 2 * KIB)
+        quantize(wg_w[:], wg_s[:], wg_bf[:].rearrange("p g n t -> p (g n t)"))
 
         woven = [held([P, QUARTER, PACK], BF16, "woven0"), placed([P, QUARTER, PACK], BF16, "woven1", 28 * KIB)]
         parts = halves(HALF)
@@ -302,12 +311,13 @@ def tile_list_slate_candidate_profiles_kernel(
         for part, cols in enumerate(parts):
             quantize(z_w[1][SCALAR_GROUP][:, cols], z_s[1][SCALAR_GROUP][:, cols], flat(woven[part]))
 
-        for g in range(GROUPS):
+        third_bf = placed([P, P, PACK], BF16, "third_bf", 61 * KIB)
+        last_bf = placed([P, GROUPS, P, PACK], BF16, "last_bf", 62 * KIB)
+        for target, m, g in [(third_bf[:], 0, 1), (last_bf[:, 0, :, :], 1, 0), (last_bf[:, 1, :, :], 1, 1)]:
             nc.scalar.copy(
-                wg_bf[1][:, g, :, :].rearrange("p (c r) t -> p c t r", r=RUN),
-                wg_high[g][:].rearrange("p t (c r) -> p c t r", r=RUN),
+                target.rearrange("p (c r) t -> p c t r", r=RUN),
+                wg_high[g][:, :, P * m : P * (m + 1)].rearrange("p t (c r) -> p c t r", r=RUN),
             )
-        quantize(wg_w[1][:], wg_s[1][:], wg_bf[1][:].rearrange("p g n t -> p (g n t)"))
         with nc.allow_non_contiguous_dma(reason="one bias value to a partition"):
             nc.sync.dma_start(bg_t[:], bg.rearrange("(c p) -> p c", p=P))
 
@@ -316,9 +326,11 @@ def tile_list_slate_candidate_profiles_kernel(
             return attr_w[:, g, :].bitcast(U8).bitcast(FP4X4)[:, cols], attr_s[:, g, :].bitcast(U8)[:, cols]
 
         def wg_operand(g, c):
-            part, m = divmod(c, 2)
-            cols = slice(N // 2 * g + P * m, N // 2 * g + P * (m + 1))
-            return wg_w[part][:, cols].bitcast(FP8X4), wg_s[part][:, cols]
+            if c >= 2:
+                cols = slice(P * g, P * (g + 1))
+                return late_w[c - 2][:, cols].bitcast(FP8X4), late_s[c - 2][:, cols]
+            cols = slice(N // 2 * g + P * c, N // 2 * g + P * (c + 1))
+            return wg_w[:, cols].bitcast(FP8X4), wg_s[:, cols]
 
         def profile(acc, operand, h, c, groups=GROUP_ORDER, cols=slice(0, HALF)):
             for g in groups:
@@ -342,7 +354,7 @@ def tile_list_slate_candidate_profiles_kernel(
 
         def store(h, c, y_sum, cols=slice(0, HALF)):
             if (h, c) == (0, 0):
-                result = placed([P, HALF], F32, "result_first", 27 * KIB)
+                result = placed([P, HALF], F32, "result_first", 28 * KIB)
             else:
                 result = ring.tile([P, HALF], F32, name="result")
             nc.vector.tensor_tensor(result[:, cols], y_sum[:, cols], gates[h, c][:, cols], ALU.mult)
@@ -372,9 +384,15 @@ def tile_list_slate_candidate_profiles_kernel(
             sigmoid(1, c, gate_sum[1, c])
         for c in range(2):
             profile(y_sum[1, c], attr_operand, 1, c, GROUP_ORDER[1:])
-        for h in range(2):
-            for c in range(2):
-                store(h, c, y_sum[h, c])
+        late_w.append(held([P, GROUPS * P], U32, "late_w0", after="z_pairs1"))
+        for cols, rounded in zip(halves(GROUPS * P), [early_bf, third_bf]):
+            quantize(late_w[0][:, cols], late_s[0][:, cols], flat(rounded))
+        store(0, 0, y_sum[0, 0])
+        late_w.append(held([P, GROUPS * P], U32, "late_w1", after="early_bf"))
+        quantize(late_w[1][:], late_s[1][:], last_bf[:].rearrange("p g n t -> p (g n t)"))
+        store(0, 1, y_sum[0, 1])
+        for c in range(2):
+            store(1, c, y_sum[1, c])
         for c in range(2, N_TILES):
             gate_sum[0, c] = bank(late_banks[c - 2], "gate0_%d" % c)
             profile(gate_sum[0, c], wg_operand, 0, c)

@@ -224,7 +224,6 @@ def tile_list_slate_candidate_profiles_kernel(
         z_second = [held([P, QUARTER, PACK], BF16, "z_second0")]
         z_s = [[held([P, HALF], U8, "z_s%d_%d" % (h, g)) for g in range(GROUPS)] for h in range(2)]
         wg_bf = held([P, GROUPS, N // 2, PACK], BF16, "wg_bf")
-        early_bf = held([P, P, PACK], BF16, "early_bf")
         wg_s = held([P, N], U8, "wg_s")
         late_w = []
         late_s = [held([P, GROUPS * P], U8, "late_s%d" % m) for m in range(2)]
@@ -272,10 +271,6 @@ def tile_list_slate_candidate_profiles_kernel(
                 wg_bf[:, g, :, :], wg_low[g][:].rearrange("p t n -> p n t"), 1.0, 0.0, ALU.mult, ALU.add
             )
 
-        nc.gpsimd.tensor_scalar(
-            early_bf[:], wg_high[0][:, :, 0:P].rearrange("p t n -> p n t"), 1.0, 0.0, ALU.mult, ALU.add
-        )
-
         freed = (0, 1, 2, 3, 4, 6, 5, 7)
         second_pieces = [v_piece[0], s_piece[0], v_piece[1], s_piece[1], s_piece[2], s_piece[3], v_piece[2], v_piece[3]]
         second, second_bank = {}, {}
@@ -311,13 +306,17 @@ def tile_list_slate_candidate_profiles_kernel(
         for part, cols in enumerate(parts):
             quantize(z_w[1][SCALAR_GROUP][:, cols], z_s[1][SCALAR_GROUP][:, cols], flat(woven[part]))
 
-        third_bf = placed([P, P, PACK], BF16, "third_bf", 61 * KIB)
-        last_bf = placed([P, GROUPS, P, PACK], BF16, "last_bf", 62 * KIB)
-        for target, m, g in [(third_bf[:], 0, 1), (last_bf[:, 0, :, :], 1, 0), (last_bf[:, 1, :, :], 1, 1)]:
-            nc.scalar.copy(
+        def runs(copy, target, m, g):
+            copy(
                 target.rearrange("p (c r) t -> p c t r", r=RUN),
                 wg_high[g][:, :, P * m : P * (m + 1)].rearrange("p t (c r) -> p c t r", r=RUN),
             )
+
+        third_bf = placed([P, GROUPS, P, PACK], BF16, "third_bf", 60 * KIB)
+        last_bf = [held([P, P, PACK], BF16, "last_bf0", after="woven0"), placed([P, P, PACK], BF16, "last_bf1", 62 * KIB)]
+        for g in range(GROUPS):
+            runs(nc.scalar.copy, third_bf[:, g, :, :], 0, g)
+        runs(nc.scalar.copy, last_bf[1][:], 1, 1)
         with nc.allow_non_contiguous_dma(reason="one bias value to a partition"):
             nc.sync.dma_start(bg_t[:], bg.rearrange("(c p) -> p c", p=P))
 
@@ -385,11 +384,12 @@ def tile_list_slate_candidate_profiles_kernel(
         for c in range(2):
             profile(y_sum[1, c], attr_operand, 1, c, GROUP_ORDER[1:])
         late_w.append(held([P, GROUPS * P], U32, "late_w0", after="z_pairs1"))
-        for cols, rounded in zip(halves(GROUPS * P), [early_bf, third_bf]):
-            quantize(late_w[0][:, cols], late_s[0][:, cols], flat(rounded))
+        quantize(late_w[0][:], late_s[0][:], third_bf[:].rearrange("p g n t -> p (g n t)"))
+        runs(nc.vector.tensor_copy, last_bf[0][:], 1, 0)
         store(0, 0, y_sum[0, 0])
-        late_w.append(held([P, GROUPS * P], U32, "late_w1", after="early_bf"))
-        quantize(late_w[1][:], late_s[1][:], last_bf[:].rearrange("p g n t -> p (g n t)"))
+        late_w.append(held([P, GROUPS * P], U32, "late_w1", after="z_second0"))
+        for cols, rounded in zip(halves(GROUPS * P), last_bf):
+            quantize(late_w[1][:, cols], late_s[1][:, cols], flat(rounded))
         store(0, 1, y_sum[0, 1])
         for c in range(2):
             store(1, c, y_sum[1, c])

@@ -143,8 +143,6 @@ def tile_list_slate_candidate_profiles_kernel(
 
         for g in range(GROUPS):
             gather_v(0, g)
-        wg_high = [placed([P, PACK, N // 2], F32, "wg_high0", 52 * KIB)]
-        load_wg(wg_high[0][:], 0, high)
         attr_w = placed([P, GROUPS, 2 * N // 4], I32, "attr_w", 44 * KIB)
         nc.sync.dma_start(attr_w[:], attr_words.bitcast(I32).rearrange("g p n -> p g n"))
 
@@ -183,17 +181,16 @@ def tile_list_slate_candidate_profiles_kernel(
                 for t in range(PACK):
                     start, stop = first_pass and t == 0, last_pass and t == PACK - 1
                     score(acc[:, P * t : P * (t + 1)], g, t, a, HALF * h + P * c, P, start, stop)
-            elif h == 0:
-                part, u = divmod(c, 2)
+            elif h == 0 and c < 2:
                 for e, cols in enumerate(halves(HALF)):
                     start, stop = first_pass and e == 0, last_pass and e == 1
-                    score(acc[:, cols], g, 2 * u + e, a, QUARTER * part, QUARTER, start, stop)
+                    score(acc[:, cols], g, e, a, QUARTER * c, QUARTER, start, stop)
             else:
                 score(acc[:], g, c, a, HALF * h, HALF, first_pass, last_pass)
 
         s_piece = [(SCALAR_GROUP, c) for c in range(PACK)]
         v_piece = [(VECTOR_GROUP, c) for c in range(PACK)]
-        first_pieces = s_piece[:2] + v_piece[:2] + s_piece[2:] + v_piece[2:]
+        first_pieces = [s_piece[0], v_piece[0], v_piece[1], s_piece[2], s_piece[3], v_piece[2], s_piece[1], v_piece[3]]
         idle = bank(BANKS - 1, "idle")
         for t in range(PACK):
             nc.tensor.matmul_mx(
@@ -210,13 +207,14 @@ def tile_list_slate_candidate_profiles_kernel(
             fill(first[piece], 0, piece, 0)
         for g in range(GROUPS):
             gather_v(1, g)
-        for part, pieces in enumerate(halves(BANKS)):
+        for part, pieces in enumerate((slice(0, 3), slice(3, BANKS))):
             gather_v2(1, QUARTER * part, QUARTER)
             for piece in first_pieces[pieces]:
                 fill(first[piece], 0, piece, 1)
         gather_v2(1, HALF, HALF)
-        wg_high.append(placed([P, PACK, N // 2], F32, "wg_high1", 12 * KIB))
-        load_wg(wg_high[1][:], 1, high)
+        wg_high = [placed([P, PACK, N // 2], F32, "wg_high%d" % g, (12 + 4 * g) * KIB) for g in range(GROUPS)]
+        for g in range(GROUPS):
+            load_wg(wg_high[g][:], g, high)
         bg_t = held([P, N_TILES], F32, "bg_t", after="v_w0_0")
 
         z_pairs = [held([P, 2, HALF, 2], BF16, "z_pairs%d" % h) for h in range(2)]
@@ -246,14 +244,13 @@ def tile_list_slate_candidate_profiles_kernel(
                     ALU.max,
                     ALU.mult,
                 )
-            elif h == 0:
-                part, u = divmod(c, 2)
+            elif h == 0 and c < 2:
                 for e, cols in enumerate(halves(HALF)):
                     nc.scalar.activation(
-                        z_pairs[h][:, u, QUARTER * part : QUARTER * (part + 1), e],
+                        z_pairs[h][:, 0, QUARTER * c : QUARTER * (c + 1), e],
                         acc[:, cols],
                         ACT.Relu,
-                        scale=rec_size[:, 2 * u + e : 2 * u + e + 1],
+                        scale=rec_size[:, e : e + 1],
                     )
             else:
                 nc.scalar.activation(z_pairs[h][:, c // 2, :, c % 2], acc[:], ACT.Relu, scale=rec_size[:, c : c + 1])
@@ -271,7 +268,7 @@ def tile_list_slate_candidate_profiles_kernel(
                 wg_bf[:, g, :, :], wg_low[g][:].rearrange("p t n -> p n t"), 1.0, 0.0, ALU.mult, ALU.add
             )
 
-        freed = (0, 1, 2, 3, 4, 6, 5, 7)
+        freed = (0, 1, 3, 2, 4, 5, 7, 6)
         second_pieces = [v_piece[0], s_piece[0], v_piece[1], s_piece[1], s_piece[2], s_piece[3], v_piece[2], v_piece[3]]
         second, second_bank = {}, {}
         for n, piece in zip(freed, second_pieces):

@@ -50,10 +50,10 @@ def tile_list_slate_candidate_profiles_kernel(
         shared = ctx.enter_context(tc.tile_pool(name="shared", bufs=1))
 
         def placed(shape, dtype, name, offset):
-            return shared.tile(shape, dtype, name=name, offset=offset, align_bytes=64)
+            return shared.tile(shape, dtype, name=name, offset=offset, align_bytes=256)
 
         def held(shape, dtype, name, after=""):
-            return keep.tile(shape, dtype, name=name, tag=after or name, align_bytes=64)
+            return keep.tile(shape, dtype, name=name, tag=after or name, align_bytes=256)
 
         def bank(b, name):
             return psum.tile([P, HALF], F32, name=name, tag="bank%d" % b)
@@ -345,14 +345,14 @@ def tile_list_slate_candidate_profiles_kernel(
 
         def sigmoid(h, c, gate_sum, cols=slice(0, HALF)):
             if cols.start == 0:
-                gates[h, c] = ring.tile([P, HALF], F32, name="gate")
+                gates[h, c] = ring.tile([P, HALF], F32, name="gate", align_bytes=256)
             nc.scalar.activation(gates[h, c][:, cols], gate_sum[:, cols], ACT.Sigmoid, bias=bg_t[:, c : c + 1])
 
         def store(h, c, y_sum, cols=slice(0, HALF)):
             if (h, c) == (0, 0):
                 result = placed([P, HALF], F32, "result_first", 28 * KIB)
             else:
-                result = ring.tile([P, HALF], F32, name="result")
+                result = ring.tile([P, HALF], F32, name="result", align_bytes=256)
             nc.vector.tensor_tensor(result[:, cols], y_sum[:, cols], gates[h, c][:, cols], ALU.mult)
             nc.sync.dma_start(out[P * c : P * (c + 1), HALF * h + cols.start : HALF * h + cols.stop], result[:, cols])
 

from contextlib import ExitStack

import concourse.mybir as mybir

K, T, S, T2, S2, N = 1024, 4096, 1024, 2048, 1024, 512
FLOPS = 2 * K * S * S2 + 2 * 2 * S * N * S2

F32 = mybir.dt.float32
BF16 = mybir.dt.bfloat16
I32 = mybir.dt.int32
U32 = mybir.dt.uint32
U16 = mybir.dt.uint16
U8 = mybir.dt.uint8
FP8X4 = mybir.dt.float8_e4m3fn_x4
FP4X4 = mybir.dt.float4_e2m1fn_x4
ALU = mybir.AluOpType
ACT = mybir.ActivationFunctionType

P = 128
PACK = 4
PASS = P * PACK
K_PASSES = K // PASS
GROUPS = S // PASS
QUADRANTS = 4
QUAD = P // QUADRANTS
ROWS = 4
BANKS = 8
HALF = S2 // 2
QUARTER = HALF // 2
PER_COLUMN = 16
N_TILES = N // P
RUN = 4

FIRST_ROW = P - QUAD
PLANE_ROW = (12, 0)

SCALAR_GROUP, VECTOR_GROUP = 0, 1
GROUP_ORDER = (VECTOR_GROUP, SCALAR_GROUP)
KIB = 1024


def tile_list_slate_candidate_profiles_kernel(
    tc, tab_words, tab_scales, tab2_words, tab2_scales, offs, offs2, rec, attr_words, attr_scales, wg, bg, out
):
    nc = tc.nc
    with ExitStack() as ctx:
        keep = ctx.enter_context(tc.tile_pool(name="keep", bufs=1))
        ring = ctx.enter_context(tc.tile_pool(name="ring", bufs=2 * N_TILES))
        psum = ctx.enter_context(tc.psum_pool(name="psum", bufs=1))
        shared = ctx.enter_context(tc.tile_pool(name="shared", bufs=1))

        def placed(shape, dtype, name, offset):
            return shared.tile(shape, dtype, name=name, offset=offset, align_bytes=256)

        def held(shape, dtype, name, after=""):
            return keep.tile(shape, dtype, name=name, tag=after or name, align_bytes=256)

        def bank(b, name):
            return psum.tile([P, HALF], F32, name=name, tag="bank%d" % b)

        def halves(width):
            return [slice(0, width // 2), slice(width // 2, width)]

        idx = keep.tile([P, S // 16], U16, name="idx")
        idx2 = keep.tile([P, S2 // 16], U16, name="idx2")
        tab_w = [placed([P, T], I32, "tab_w0", 44 * KIB), placed([P, T], I32, "tab_w1", 8 * KIB)]
        tab2_w = [placed([P, T2], I32, "tab2_w0", 0)]
        tab_s = held([P, T // 4], I32, "tab_s")
        tab2_s = held([P, T2 // 4], I32, "tab2_s")

        nc.vector.memset(tab2_s[0:FIRST_ROW, :], 0)
        nc.vector.memset(tab_s[0:FIRST_ROW, :], 0)

        def load_words(tile, words, a):
            nc.sync.dma_start(tile[:], words[a].rearrange("p n t -> p (n t)").bitcast(I32))

        def load_scales(tile, scales):
            nc.sync.dma_start(tile[FIRST_ROW:P, :], scales.rearrange("a q n -> (a q) n").bitcast(I32))

        load_scales(tab2_s, tab2_scales)
        nc.sync.dma_start(idx2[:], offs2)
        load_scales(tab_s, tab_scales)
        nc.sync.dma_start(idx[:], offs)
        load_words(tab2_w[0], tab2_words, 0)
        load_words(tab_w[0], tab_words, 0)
        load_words(tab_w[1], tab_words, 1)

        v_s_listed = placed([P, S], U8, "v_s_listed", 40 * KIB - S // 2)
        planes = [held([P, S + S2], U8, "planes%d" % a) for a in range(K_PASSES)]
        nc.vector.memset(planes[1][:].bitcast(I32), 0)

        def list_cols(entry, count):
            return slice(entry // PER_COLUMN, (entry + count) // PER_COLUMN)

        v2_s_listed = held([P, S2], U8, "v2_s_listed")
        nc.vector.tensor_copy(v2_s_listed[:], tab2_s[:].bitcast(U8).indirect(idx2[:]))
        nc.vector.tensor_copy(v_s_listed[:], tab_s[:].bitcast(U8).indirect(idx[:]))
        nc.vector.tensor_copy(planes[0][:, S : S + S2].bitcast(I32), v2_s_listed[:].bitcast(I32))
        nc.vector.tensor_copy(
            planes[0][:, 0:S].rearrange("p (g t m) -> p g t m", g=GROUPS, t=PACK),
            v_s_listed[:].rearrange("p (g m t) -> p g t m", g=GROUPS, t=PACK),
        )

        def move_rows(a, quadrants, cols):
            for q in quadrants:
                source = FIRST_ROW + ROWS * (QUADRANTS * a + q)
                target = QUAD * q + PLANE_ROW[a]
                nc.sync.dma_start(
                    planes[a][target : target + ROWS, cols].bitcast(I32),
                    planes[0][source : source + ROWS, cols].bitcast(I32),
                )

        move_rows(0, range(QUADRANTS - 1), slice(0, S + HALF))
        tab2_w.append(placed([P, T2], I32, "tab2_w1", 32 * KIB))
        load_words(tab2_w[1], tab2_words, 1)
        move_rows(1, (2, 3, 0, 1), slice(0, S + S2))
        rec_t = placed([P, GROUPS, PACK], F32, "rec_t", 40 * KIB)
        nc.sync.dma_start(rec_t[:], rec.rearrange("(g p t) -> p g t", g=GROUPS, t=PACK))

        v_w = [[held([P, PASS], U32, "v_w%d_%d" % (a, g)) for g in range(GROUPS)] for a in range(K_PASSES)]
        v2_w = [held([P, S2], U32, "v2_w%d" % a) for a in range(K_PASSES)]

        def gather_v(a, g):
            nc.vector.tensor_copy(
                v_w[a][g][:].rearrange("p (t m) -> p m t", t=PACK),
                tab_w[a][:].bitcast(U32).indirect(idx[:, list_cols(PASS * g, PASS)]),
            )

        def gather_v2(a, j0, width):
            nc.vector.tensor_copy(
                v2_w[a][:, j0 : j0 + width], tab2_w[a][:].bitcast(U32).indirect(idx2[:, list_cols(j0, width)])
            )

        def load_wg(tile, g, cols):
            nc.sync.dma_start(tile, wg[PASS * g : PASS * (g + 1), cols].rearrange("(p t) n -> p t n", t=PACK))

        low, high = halves(N)
        gather_v2(0, 0, S2)
        wg_low = [placed([P, PACK, N // 2], F32, "wg_low%d" % g, 4 * KIB * g) for g in range(GROUPS)]
        load_wg(wg_low[0][:], 0, low)
        move_rows(0, range(QUADRANTS - 1), slice(S + HALF, S + S2))
        load_wg(wg_low[1][:], 1, low)

        for g in range(GROUPS):
            gather_v(0, g)
        attr_w = placed([P, GROUPS, 2 * N // 4], I32, "attr_w", 44 * KIB)
        nc.sync.dma_start(attr_w[:], attr_words.bitcast(I32).rearrange("g p n -> p g n"))

        attr_s = placed([P, GROUPS, N // 4], I32, "attr_s", 48 * KIB)
        nc.vector.memset(attr_s[:], 0)
        for q in range(QUADRANTS):
            nc.sync.dma_start(
                attr_s[QUAD * q : QUAD * q + ROWS, :, :],
                attr_scales[:, ROWS * q : ROWS * (q + 1), :].bitcast(I32).rearrange("g s n -> s g n"),
            )

        rec_sign = held([P, 2, 2], BF16, "rec_sign")
        rec_size = shared.tile([P, 4 * PACK], F32, name="rec_size", offset=62 * KIB - 32, align_bytes=32)
        warm = held([P, 1], F32, "warm")
        nc.vector.memset(warm[:], 0.0)
        nc.scalar.activation(warm[:], warm[:], ACT.Sigmoid)
        nc.scalar.activation(rec_size[:, 0:PACK], rec_t[:, SCALAR_GROUP, :], ACT.Abs)
        nc.scalar.activation(rec_sign[:].rearrange("p u e -> p (u e)"), rec_t[:, SCALAR_GROUP, :], ACT.Sign)

        def score(acc, g, t, a, j0, width, start, stop):
            m0 = PASS * g + P * t
            nc.tensor.matmul_mx(
                out=acc,
                lhsT=v_w[a][g][:, P * t : P * (t + 1)].bitcast(FP8X4),
                lhsT_scale=planes[a][PLANE_ROW[a] : P, m0 : m0 + P],
                rhs=v2_w[a][:, j0 : j0 + width].bitcast(FP8X4),
                rhs_scale=planes[a][PLANE_ROW[a] : P, S + j0 : S + j0 + width],
                start=start,
                stop=stop,
            )

        def fill(acc, h, piece, a):
            g, c = piece
            first_pass, last_pass = a == 0, a == K_PASSES - 1
            if g == VECTOR_GROUP:
                for t in range(PACK):
                    start, stop = first_pass and t == 0, last_pass and t == PACK - 1
                    score(acc[:, P * t : P * (t + 1)], g, t, a, HALF * h + P * c, P, start, stop)
            elif h == 0 and c < 2:
                for e, cols in enumerate(halves(HALF)):
                    start, stop = first_pass and e == 0, last_pass and e == 1
                    score(acc[:, cols], g, e, a, QUARTER * c, QUARTER, start, stop)
            else:
                score(acc[:], g, c, a, HALF * h, HALF, first_pass, last_pass)

        s_piece = [(SCALAR_GROUP, c) for c in range(PACK)]
        v_piece = [(VECTOR_GROUP, c) for c in range(PACK)]
        first_pieces = [s_piece[0], v_piece[0], v_piece[1], s_piece[2], s_piece[3], v_piece[2], s_piece[1], v_piece[3]]
        idle = bank(BANKS - 1, "idle")
        for t in range(PACK):
            nc.tensor.matmul_mx(
                out=idle[:],
                lhsT=v_w[0][0][:, P * t : P * (t + 1)].bitcast(FP8X4),
                lhsT_scale=v2_s_listed[:, 0:P],
                rhs=v2_w[0][:, 0:HALF].bitcast(FP8X4),
                rhs_scale=v2_s_listed[:, 0:HALF],
                start=True,
                stop=True,
            )
        first = {piece: bank(n, "first%d" % n) for n, piece in enumerate(first_pieces)}
        for piece in first_pieces:
            fill(first[piece], 0, piece, 0)
        for g in range(GROUPS):
            gather_v(1, g)
        for part, pieces in enumerate((slice(0, 3), slice(3, BANKS))):
            gather_v2(1, QUARTER * part, QUARTER)
            for piece in first_pieces[pieces]:
                fill(first[piece], 0, piece, 1)
        gather_v2(1, HALF, HALF)
        wg_high = [placed([P, PACK, N // 2], F32, "wg_high%d" % g, (12 + 4 * g) * KIB) for g in range(GROUPS)]
        for g in range(GROUPS):
            load_wg(wg_high[g][:], g, high)
        bg_t = held([P, N_TILES], F32, "bg_t", after="v_w0_0")

        z_pairs = [held([P, 2, HALF, 2], BF16, "z_pairs%d" % h) for h in range(2)]
        z_plain = held([P, HALF, PACK], BF16, "z_plain")
        z_second = [held([P, QUARTER, PACK], BF16, "z_second0")]
        z_s = [[held([P, HALF], U8, "z_s%d_%d" % (h, g)) for g in range(GROUPS)] for h in range(2)]
        wg_bf = held([P, GROUPS, N // 2, PACK], BF16, "wg_bf")
        wg_s = held([P, N], U8, "wg_s")
        late_w = []
        late_s = [held([P, GROUPS * P], U8, "late_s%d" % m) for m in range(2)]

        def quantize(words, scales, side_by_side):
            nc.vector.quantize_mx(out=words.bitcast(FP8X4), scales=scales, in_=side_by_side)

        def flat(tile):
            return tile[:].rearrange("p w t -> p (w t)")

        def empty(acc, h, piece):
            g, c = piece
            if g == VECTOR_GROUP:
                target, block = (z_plain, c) if h == 0 else (z_second[c // 2], c % 2)
                nc.vector.scalar_tensor_tensor(
                    target[:, P * block : P * (block + 1), :],
                    acc[:].rearrange("p (t j) -> p j t", t=PACK),
                    0.0,
                    rec_t[:, g : g + 1, :].to_broadcast([P, P, PACK]),
                    ALU.max,
                    ALU.mult,
                )
            elif h == 0 and c < 2:
                for e, cols in enumerate(halves(HALF)):
                    nc.scalar.activation(
                        z_pairs[h][:, 0, QUARTER * c : QUARTER * (c + 1), e],
                        acc[:, cols],
                        ACT.Relu,
                        scale=rec_size[:, e : e + 1],
                    )
            else:
                nc.scalar.activation(z_pairs[h][:, c // 2, :, c % 2], acc[:], ACT.Relu, scale=rec_size[:, c : c + 1])

        def weave(fours, pairs, width):
            nc.vector.tensor_tensor(
                fours.rearrange("p j (u e) -> p j u e", e=2),
                pairs.rearrange("p u j e -> p j u e"),
                rec_sign[:].unsqueeze(1).to_broadcast([P, width, 2, 2]),
                ALU.mult,
            )

        for g in range(GROUPS):
            nc.gpsimd.tensor_scalar(
                wg_bf[:, g, :, :], wg_low[g][:].rearrange("p t n -> p n t"), 1.0, 0.0, ALU.mult, ALU.add
            )

        freed = (0, 1, 3, 2, 4, 5, 7, 6)
        second_pieces = [v_piece[0], s_piece[0], v_piece[1], s_piece[1], s_piece[2], s_piece[3], v_piece[2], v_piece[3]]
        second, second_bank = {}, {}
        for n, piece in zip(freed, second_pieces):
            empty(first[first_pieces[n]], 0, first_pieces[n])
            second[piece] = bank(n, "second%d" % n)
            second_bank[piece] = n
            for a in range(K_PASSES):
                fill(second[piece], 1, piece, a)
        for piece in v_piece[:2] + s_piece:
            empty(second[piece], 1, piece)

        z_w = [
            [held([P, HALF], U32, "z_w0_0"), placed([P, HALF], U32, "z_w0_1", 6 * KIB)],
            [held([P, HALF], U32, "z_w1_%d" % g) for g in range(GROUPS)],
        ]
        woven_first = placed([P, HALF, PACK], BF16, "woven_first", 2 * KIB)
        quantize(z_w[0][VECTOR_GROUP][:], z_s[0][VECTOR_GROUP][:], flat(z_plain))
        z_second.append(held([P, QUARTER, PACK], BF16, "z_second1", after="z_plain"))
        weave(woven_first[:], z_pairs[0][:], HALF)
        empty(second[v_piece[2]], 1, v_piece[2])
        quantize(z_w[0][SCALAR_GROUP][:], z_s[0][SCALAR_GROUP][:], flat(woven_first))
        empty(second[v_piece[3]], 1, v_piece[3])
        wg_w = placed([P, N], U32, "wg_w", 2 * KIB)
        quantize(wg_w[:], wg_s[:], wg_bf[:].rearrange("p g n t -> p (g n t)"))

        woven = [held([P, QUARTER, PACK], BF16, "woven0"), placed([P, QUARTER, PACK], BF16, "woven1", 28 * KIB)]
        parts = halves(HALF)
        weave(woven[0][:], z_pairs[1][:, :, parts[0], :], QUARTER)
        for part, cols in enumerate(parts):
            quantize(z_w[1][VECTOR_GROUP][:, cols], z_s[1][VECTOR_GROUP][:, cols], flat(z_second[part]))
        weave(woven[1][:], z_pairs[1][:, :, parts[1], :], QUARTER)
        for part, cols in enumerate(parts):
            quantize(z_w[1][SCALAR_GROUP][:, cols], z_s[1][SCALAR_GROUP][:, cols], flat(woven[part]))

        def runs(copy, target, m, g):
            copy(
                target.rearrange("p (c r) t -> p c t r", r=RUN),
                wg_high[g][:, :, P * m : P * (m + 1)].rearrange("p t (c r) -> p c t r", r=RUN),
            )

        third_bf = placed([P, GROUPS, P, PACK], BF16, "third_bf", 60 * KIB)
        last_bf = [held([P, P, PACK], BF16, "last_bf0", after="woven0"), placed([P, P, PACK], BF16, "last_bf1", 62 * KIB)]
        for g in range(GROUPS):
            runs(nc.scalar.copy, third_bf[:, g, :, :], 0, g)
        runs(nc.scalar.copy, last_bf[1][:], 1, 1)
        with nc.allow_non_contiguous_dma(reason="one bias value to a partition"):
            nc.sync.dma_start(bg_t[:], bg.rearrange("(c p) -> p c", p=P))

        def attr_operand(g, c):
            cols = slice(P * c, P * (c + 1))
            return attr_w[:, g, :].bitcast(U8).bitcast(FP4X4)[:, cols], attr_s[:, g, :].bitcast(U8)[:, cols]

        def wg_operand(g, c):
            if c >= 2:
                cols = slice(P * g, P * (g + 1))
                return late_w[c - 2][:, cols].bitcast(FP8X4), late_s[c - 2][:, cols]
            cols = slice(N // 2 * g + P * c, N // 2 * g + P * (c + 1))
            return wg_w[:, cols].bitcast(FP8X4), wg_s[:, cols]

        def profile(acc, operand, h, c, groups=GROUP_ORDER, cols=slice(0, HALF)):
            for g in groups:
                words, scales = operand(g, c)
                nc.tensor.matmul_mx(
                    out=acc[:, cols],
                    lhsT=words,
                    lhsT_scale=scales,
                    rhs=z_w[h][g][:, cols].bitcast(FP8X4),
                    rhs_scale=z_s[h][g][:, cols],
                    start=(g == GROUP_ORDER[0]),
                    stop=(g == GROUP_ORDER[-1]),
                )

        gates = {}

        def sigmoid(h, c, gate_sum, cols=slice(0, HALF)):
            if cols.start == 0:
                gates[h, c] = ring.tile([P, HALF], F32, name="gate", align_bytes=256)
            nc.scalar.activation(gates[h, c][:, cols], gate_sum[:, cols], ACT.Sigmoid, bias=bg_t[:, c : c + 1])

        def store(h, c, y_sum, cols=slice(0, HALF)):
            if (h, c) == (0, 0):
                result = placed([P, HALF], F32, "result_first", 28 * KIB)
            else:
                result = ring.tile([P, HALF], F32, name="result", align_bytes=256)
            nc.vector.tensor_tensor(result[:, cols], y_sum[:, cols], gates[h, c][:, cols], ALU.mult)
            nc.sync.dma_start(out[P * c : P * (c + 1), HALF * h + cols.start : HALF * h + cols.stop], result[:, cols])

        b = second_bank
        y_sum, gate_sum = {}, {}
        for c, piece in enumerate([s_piece[0], v_piece[0], v_piece[1], s_piece[1]]):
            y_sum[0, c] = bank(b[piece], "y0_%d" % c)
        for g in GROUP_ORDER:
            for c in range(N_TILES):
                profile(y_sum[0, c], attr_operand, 0, c, [g])
        low_banks = [b[s_piece[2]], b[s_piece[3]]]
        late_banks = [b[v_piece[2]], b[v_piece[3]]]
        for c in range(2):
            gate_sum[0, c] = bank(low_banks[c], "gate0_%d" % c)
            profile(gate_sum[0, c], wg_operand, 0, c)
            sigmoid(0, c, gate_sum[0, c])
        for c in range(2):
            gate_sum[1, c] = bank(late_banks[c], "gate1_%d" % c)
            profile(gate_sum[1, c], wg_operand, 1, c, GROUP_ORDER[:1])
        for c in range(2):
            y_sum[1, c] = bank(low_banks[c], "y1_%d" % c)
            profile(y_sum[1, c], attr_operand, 1, c, GROUP_ORDER[:1])
        for c in range(2):
            profile(gate_sum[1, c], wg_operand, 1, c, GROUP_ORDER[1:])
            sigmoid(1, c, gate_sum[1, c])
        for c in range(2):
            profile(y_sum[1, c], attr_operand, 1, c, GROUP_ORDER[1:])
        late_w.append(held([P, GROUPS * P], U32, "late_w0", after="z_pairs1"))
        quantize(late_w[0][:], late_s[0][:], third_bf[:].rearrange("p g n t -> p (g n t)"))
        runs(nc.vector.tensor_copy, last_bf[0][:], 1, 0)
        store(0, 0, y_sum[0, 0])
        late_w.append(held([P, GROUPS * P], U32, "late_w1", after="z_second0"))
        for cols, rounded in zip(halves(GROUPS * P), last_bf):
            quantize(late_w[1][:, cols], late_s[1][:, cols], flat(rounded))
        store(0, 1, y_sum[0, 1])
        for c in range(2):
            store(1, c, y_sum[1, c])
        for c in range(2, N_TILES):
            gate_sum[0, c] = bank(late_banks[c - 2], "gate0_%d" % c)
            profile(gate_sum[0, c], wg_operand, 0, c)
            sigmoid(0, c, gate_sum[0, c])
        gate_sum[1, 2] = bank(b[s_piece[0]], "gate1_2")
        profile(gate_sum[1, 2], wg_operand, 1, 2)
        sigmoid(1, 2, gate_sum[1, 2])
        y_sum[1, 2] = bank(b[v_piece[0]], "y1_2")
        profile(y_sum[1, 2], attr_operand, 1, 2)
        for n, cols in zip(low_banks, halves(HALF)):
            last = bank(n, "gate1_3_%d" % n)
            profile(last, wg_operand, 1, 3, cols=cols)
            sigmoid(1, 3, last, cols)
        for c in range(2, N_TILES):
            store(0, c, y_sum[0, c])
        store(1, 2, y_sum[1, 2])
        for n, cols in zip(late_banks, halves(HALF)):
            last = bank(n, "y1_3_%d" % n)
            profile(last, attr_operand, 1, 3, cols=cols)
            store(1, 3, last, cols)
